import numpy as np
import ml_dtypes


def mxq(x, axis, fmt="e4m3"):
    dtype, down = {"e4m3": (ml_dtypes.float8_e4m3fn, 7), "e5m2": (ml_dtypes.float8_e5m2, 14)}[fmt]
    v = np.moveaxis(np.asarray(x, np.float32).astype(ml_dtypes.bfloat16).astype(np.float64), axis, -1)
    blocks = v.reshape(v.shape[:-1] + (-1, 32))
    amax = np.abs(blocks).max(-1, keepdims=True)
    byte = np.maximum(np.where(amax > 0, np.frexp(amax)[1] - 1 + 127, 0) - down, 1)
    scale = np.exp2(byte - 127.0)
    codes = (blocks / scale).astype(np.float32).astype(dtype).astype(np.float64)
    return np.moveaxis((codes * scale).reshape(v.shape), -1, axis)


WIDE = False


def mx_kscale(k):
    if not WIDE:
        return np.ones(k)
    levels = np.array([10, -10, 5, -5, 0])
    if k % 512:
        return np.exp2(np.random.permutation(np.resize(levels, k // 32))).repeat(32)
    a = np.empty((k // 512, 16))
    for p in range(k // 512):
        a[p, :8] = np.random.permutation(np.resize(levels, 8))
        for g in range(8):
            far = levels[np.abs(levels - a[p, g]) >= 10]
            a[p, g + 8] = far[np.random.randint(len(far))]
    return np.exp2(a.ravel()).repeat(32)


def f64(x):
    return np.asarray(x).astype(np.float64)


def striped(idx):
    return np.tile(idx.reshape(-1, 16).T, (8, 1)).astype(np.uint16)


def unstriped(offs):
    return offs[:16].T.reshape(-1).astype(np.int64)


E2M1 = np.array([0.0, 0.5, 1.0, 1.5, 2.0, 3.0, 4.0, 6.0, -0.0, -0.5, -1.0, -1.5, -2.0, -3.0, -4.0, -6.0])


def pack_weight(w, fmt):
    k, n = w.shape
    w = f64(np.asarray(w, np.float32).astype(ml_dtypes.bfloat16)).reshape(k // 32, 32, n)
    amax = np.abs(w).max(1)
    if fmt == "e4m3":
        byte = np.frexp(amax)[1] - 1 + 127 - 7
    else:
        mant, ex = np.frexp(amax / 6.0)
        byte = np.where(mant > 0.5, ex, ex - 1) + 127
    byte = np.clip(np.where(amax > 0, byte, 1), 1, 254)
    scaled = (w * np.exp2(127.0 - byte)[:, None, :]).reshape(k, n).astype(np.float32)
    by_word = np.ascontiguousarray(scaled.reshape(k // 512, 128, 4, n).transpose(0, 1, 3, 2))
    if fmt == "e4m3":
        words = by_word.astype(ml_dtypes.float8_e4m3fn).view(np.uint8)
    else:
        c = by_word.astype(ml_dtypes.float4_e2m1fn).view(np.uint8) & 0xF
        words = (c[..., 0::2] | (c[..., 1::2] << 4)).reshape(k // 512, 128, 2 * n)
    return np.ascontiguousarray(words), np.ascontiguousarray(byte.astype(np.uint8).reshape(k // 512, 16, n))


def unpack_weight(words, scales, fmt):
    g, _, n = scales.shape
    words = np.ascontiguousarray(words).reshape(g, 128, n, -1)
    if fmt == "e4m3":
        vals = words.view(ml_dtypes.float8_e4m3fn).astype(np.float64)
    else:
        nib = np.empty((g, 128, n, 4), np.uint8)
        nib[..., 0::2] = words & 0xF
        nib[..., 1::2] = words >> 4
        vals = E2M1[nib]
    vals = vals * np.repeat(np.exp2(scales.astype(np.float64) - 127.0), 8, axis=1)[..., None]
    return vals.transpose(0, 1, 3, 2).reshape(g * 512, n)


def gelu(v):
    return 0.5 * v * (1.0 + np.tanh(np.sqrt(2.0 / np.pi) * (v + 0.044715 * v**3)))


def striped8(idx):
    return np.concatenate([v.reshape(-1, 16).T for v in idx]).astype(np.uint16)


def unstriped8(offs):
    return np.stack([offs[16 * g:16 * g + 16].T.reshape(-1) for g in range(8)]).astype(np.int64)


def runs(v, idx8):
    k = np.arange(v.shape[0])
    return v[k[:, None], idx8[k % 512 // 64]]


K, K2, H, T, S = 1024, 512, 1024, 2048, 1024

def setup_inputs():
    n = np.random.standard_normal
    s = mx_kscale(K)[:, None]
    s2 = mx_kscale(K2)[:, None]
    u = mx_kscale(H)[:, None]
    tab_words, tab_scales = pack_weight(n((K, T)) * s, "e4m3")
    tab2_words, tab2_scales = pack_weight(n((K2, T)) * s2, "e4m3")
    w1_words, w1_scales = pack_weight(n((K, H)) / np.sqrt(K) / s, "e2m1")
    w3_words, w3_scales = pack_weight(2.0 * n((H, H)) / np.sqrt(H) / u, "e4m3")
    return {
        "tab_words": tab_words, "tab_scales": tab_scales,
        "offs": striped8(np.stack([np.random.permutation(T)[:S] for _ in range(8)])),
        "tab2_words": tab2_words, "tab2_scales": tab2_scales,
        "offs2": striped(np.random.permutation(T)[:S]),
        "w1_words": w1_words, "w1_scales": w1_scales,
        "w2": (n((K2, H)) / np.sqrt(K2) / s2).astype(np.float32),
        "bias": (0.5 * n(H)).astype(np.float32),
        "gain": (np.exp(0.3 * n(H)) * u[:, 0]).astype(np.float32),
        "w3_words": w3_words, "w3_scales": w3_scales,
    }

def reference(tab_words, tab_scales, offs, tab2_words, tab2_scales, offs2,
              w1_words, w1_scales, w2, bias, gain, w3_words, w3_scales):
    v = runs(unpack_weight(tab_words, tab_scales, "e4m3"), unstriped8(offs))
    v2 = unpack_weight(tab2_words, tab2_scales, "e4m3")[:, unstriped(offs2)]
    w1 = unpack_weight(w1_words, w1_scales, "e2m1")
    w3 = unpack_weight(w3_words, w3_scales, "e4m3")
    load = w1.T @ v
    weather = mxq(f64(w2), 0, "e4m3").T @ v2
    x = load + weather + f64(bias)[:, None]
    stress = 1.0 / (1.0 + np.exp(-x))
    h = f64(gain)[:, None] * stress
    y = w3.T @ mxq(h, 0, "e4m3")
    return y + load

@@ -1,0 +1,239 @@
+from contextlib import ExitStack
+
+import concourse.mybir as mybir
+
+K, K2, H, T, S = 1024, 512, 1024, 2048, 1024
+FLOPS = 2 * S * H * (K + K2 + H)
+
+F32 = mybir.dt.float32
+BF16 = mybir.dt.bfloat16
+I32 = mybir.dt.int32
+U32 = mybir.dt.uint32
+U16 = mybir.dt.uint16
+U8 = mybir.dt.uint8
+FP8X4 = mybir.dt.float8_e4m3fn_x4
+FP4X4 = mybir.dt.float4_e2m1fn_x4
+MULT = mybir.AluOpType.mult
+ADD = mybir.AluOpType.add
+SIGMOID = mybir.ActivationFunctionType.Sigmoid
+COPY = mybir.ActivationFunctionType.Copy
+
+P = 128
+N = 512
+CHUNK = 128
+GROUPS = ((0, 0), (0, 1), (1, 0), (1, 1))
+MODES = (("pool", 0), ("pool", 0), ("pool", 0), ("fused", 0))
+SYNC_MOVES = 5
+TWICE = 3
+
+
+def tile_list_fleet_ageing_kernel(tc, tab_words, tab_scales, offs, tab2_words, tab2_scales, offs2,
+                                           w1_words, w1_scales, w2, bias, gain, w3_words, w3_scales, out):
+    nc = tc.nc
+    with ExitStack() as ctx:
+        lists = ctx.enter_context(tc.tile_pool(name="lists", bufs=1))
+        keep = ctx.enter_context(tc.tile_pool(name="keep", bufs=1))
+        work = ctx.enter_context(tc.tile_pool(name="work", bufs=2))
+        psum = ctx.enter_context(tc.psum_pool(name="psum", bufs=1))
+
+        def held(shape, dtype, name, tag=""):
+            return keep.tile(shape, dtype, name=name, tag=tag or name, align_bytes=64)
+
+        def words_of(dram_pass):
+            return dram_pass.rearrange("p c i -> p (c i)").bitcast(I32)
+
+        list8 = lists.tile([P, S // 16], U16, name="list8")
+        nc.sync.dma_start(list8[:], offs)
+
+        tab_sc = held([P, T], U8, "tab_sc", "late_w2_0")
+        for a in range(2):
+            nc.sync.dma_start(tab_sc[a:P:2, :].bitcast(I32), tab_scales[a].bitcast(I32).unsqueeze(1).to_broadcast([16, 4, T // 4]))
+        w1_raw = held([P, 2, H // 2], I32, "w1_raw", "late_tab2")
+        nc.sync.dma_start(w1_raw[:], w1_words.bitcast(I32).rearrange("a p c -> p a c"))
+        tab_w = [held([P, T], I32, "tab_w0", "late_w3"), held([P, T], I32, "tab_w1")]
+        for a in range(2):
+            nc.sync.dma_start(tab_w[a][:], words_of(tab_words[a]))
+        list1 = lists.tile([P, S // 16], U16, name="list1")
+        nc.sync.dma_start(list1[:], offs2)
+
+        w1_sc_raw = held([P, 2 * H], U8, "w1_sc_raw", "late_w2_1")
+        v_planes = held([P, 2 * S], U8, "v_planes")
+        w3_sc_raw = held([P, H], U8, "w3_sc_raw")
+        tab2_sc = held([P, T], U8, "tab2_sc")
+        for tile in (w1_sc_raw, tab2_sc, v_planes, w3_sc_raw):
+            nc.vector.memset(tile[:].bitcast(I32), 0)
+        warm = held([P, 8], F32, "warm")
+        nc.vector.memset(warm[:], 0.0)
+        warm2 = held([P, 8], F32, "warm2")
+        nc.scalar.activation(warm2[:], warm[:], SIGMOID)
+        for d in range(4):
+            nc.gpsimd.dma_start(w1_sc_raw[32 * d:32 * d + 4, :].bitcast(I32).rearrange("r (a c) -> r a c", a=2),
+                                w1_scales[:, 4 * d:4 * d + 4, :].bitcast(I32).rearrange("a r c -> r a c"))
+
+        picked_sc = held([P, S], U8, "picked_sc")
+        nc.vector.tensor_copy(picked_sc[:], tab_sc[:].indirect(list8[:]))
+        w2_view = w2.rearrange("(p j) c -> p j c", j=4)
+        w2_raw = [held([P, 4, N], F32, "w2_raw0", "late_w2_0")]
+        for a in range(2):
+            for r in range(4):
+                if 4 * a + r == SYNC_MOVES:
+                    nc.sync.dma_start(w2_raw[0][:], w2_view[:, :, 0:N])
+                nc.sync.dma_start(v_planes[r:P:32, a * S:(a + 1) * S].bitcast(I32),
+                                  picked_sc[8 * r + a:P:32, :].bitcast(I32))
+
+        w1_codes = held([P, 4 * H], U8, "w1_codes")
+        nc.vector.tensor_copy(w1_codes[:].bitcast(U16).rearrange("p (g t m i) -> p g m t i", g=4, t=4, i=8),
+                              w1_raw[:].bitcast(U16).rearrange("p a (b m i t) -> p (a b) m t i", b=2, t=4, i=8))
+        w1_planes = held([P, 2 * H], U8, "w1_planes")
+        nc.vector.tensor_copy(w1_planes[:].rearrange("p (g t m) -> p g t m", t=4, m=P),
+                              w1_sc_raw[:].rearrange("p (g m t) -> p g t m", t=4, m=P))
+
+        tab2_w = held([P, T], I32, "tab2_w", "late_tab2")
+        nc.sync.dma_start(tab2_w[:], words_of(tab2_words[0]))
+        w2_raw.append(held([P, 4, N], F32, "w2_raw1", "late_w2_1"))
+        nc.sync.dma_start(w2_raw[1][:], w2_view[:, :, N:2 * N])
+
+        for d in range(4):
+            nc.gpsimd.dma_start(tab2_sc[32 * d:32 * d + 4, :].bitcast(I32), tab2_scales[0, 4 * d:4 * d + 4, :].bitcast(I32))
+
+        bias_sb = held([P, 2, 4], F32, "bias_sb")
+        gain_sb = held([P, 2, 4], F32, "gain_sb")
+        nc.gpsimd.dma_start(bias_sb[:], bias.rearrange("(b p t) -> p b t", b=2, t=4))
+        nc.gpsimd.dma_start(gain_sb[:], gain.rearrange("(b p t) -> p b t", b=2, t=4))
+        for d in range(4):
+            nc.gpsimd.dma_start(w3_sc_raw[32 * d:32 * d + 8, :].bitcast(I32), w3_scales[:, 4 * d:4 * d + 4, :].bitcast(I32))
+        w2_codes, w2_plane = {}, {}
+
+        def prepare_w2(b):
+            grouped = work.tile([P, 4 * N], BF16, name="w2_grouped", align_bytes=64)
+            nc.scalar.copy(grouped[:].rearrange("p (t m j) -> p m t j", t=4, j=4),
+                           w2_raw[b][:].rearrange("p j (m t) -> p m t j", t=4))
+            w2_codes[b] = held([P, N], U32, "w2_codes%d" % b)
+            w2_plane[b] = held([P, N], U8, "w2_plane%d" % b)
+            nc.vector.quantize_mx(w2_codes[b][:].bitcast(FP8X4), w2_plane[b][:], grouped[:])
+
+        v_codes, v2_codes, v2_plane = {}, {}, {}
+
+        def gather(h):
+            cols = slice(h * N // 16, (h + 1) * N // 16)
+            for a in range(2):
+                v_codes[h, a] = held([P, N], U32, "v_codes%d%d" % (h, a))
+                nc.vector.tensor_copy(v_codes[h, a][:], tab_w[a][:].bitcast(U32).indirect(list8[:, cols]))
+            v2_plane[h] = held([P, N], U8, "v2_plane%d" % h)
+            nc.vector.tensor_copy(v2_plane[h][:], tab2_sc[:].indirect(list1[:, cols]))
+            v2_codes[h] = held([P, N], U32, "v2_codes%d" % h)
+            nc.vector.tensor_copy(v2_codes[h][:], tab2_w[:].bitcast(U32).indirect(list1[:, cols]))
+
+        def load_passes(bank, h, b, t, stop):
+            for a in range(2):
+                nc.tensor.matmul_mx(
+                    bank[:],
+                    lhsT=w1_codes[:, 2 * (a * H + b * N + t * P):2 * (a * H + b * N + (t + 1) * P)].bitcast(FP4X4),
+                    lhsT_scale=w1_planes[:, a * H + b * N + t * P:a * H + b * N + (t + 1) * P],
+                    rhs=v_codes[h, a][:].bitcast(FP8X4),
+                    rhs_scale=v_planes[:, a * S + h * N:a * S + (h + 1) * N],
+                    start=(a == 0), stop=(stop and a == 1))
+
+        def weather_pass(bank, h, b, t, start):
+            nc.tensor.matmul_mx(
+                bank[:],
+                lhsT=w2_codes[b][:, t * P:(t + 1) * P].bitcast(FP8X4), lhsT_scale=w2_plane[b][:, t * P:(t + 1) * P],
+                rhs=v2_codes[h][:].bitcast(FP8X4), rhs_scale=v2_plane[h][:], start=start, stop=True)
+
+        load_sb, h_codes, h_plane = {}, {}, {}
+
+        def first_stage(g):
+            h, b = GROUPS[g]
+            mode, pool_chunks = MODES[g]
+            stress = work.tile([P, 4 * N], F32, name="stress")
+            woven = stress[:].rearrange("p (c t i) -> p c t i", t=4, i=4)
+            flat = work.tile([P, 4, N], BF16, name="h_flat")
+            for t in range(4):
+                column = bias_sb[:, b, t:t + 1]
+                if g == TWICE:
+                    bank = psum.tile([P, N], F32, name="sum_bank", bufs=3)
+                    load_passes(bank, h, b, t, False)
+                    weather_pass(bank, h, b, t, False)
+                    source = bank
+                else:
+                    bank = psum.tile([P, N], F32, name="load_bank", bufs=2)
+                    load_passes(bank, h, b, t, True)
+                    load_sb[h, b, t] = held([P, N], F32, "load_sb%d%d%d" % (h, b, t))
+                    nc.scalar.copy(load_sb[h, b, t][:], bank[:])
+                    bank = psum.tile([P, N], F32, name="sum_bank", bufs=3)
+                    weather_pass(bank, h, b, t, True)
+                    source = work.tile([P, N], F32, name="summed", bufs=4)
+                    nc.vector.tensor_tensor(source[:], bank[:], load_sb[h, b, t][:], ADD)
+                if mode == "fused":
+                    nc.scalar.activation(woven[:, :, t, :], source[:].rearrange("p (c i) -> p c i", i=4), SIGMOID, bias=column)
+                else:
+                    nc.scalar.activation(stress[:, t * N:(t + 1) * N], source[:], SIGMOID, bias=column)
+                    if mode == "pool":
+                        nc.gpsimd.tensor_scalar(flat[:, t, :], stress[:, t * N:(t + 1) * N], gain_sb[:, b, t:t + 1], 0.0, MULT, ADD)
+                    else:
+                        nc.scalar.activation(flat[:, t, :], stress[:, t * N:(t + 1) * N], COPY, scale=gain_sb[:, b, t:t + 1])
+            grouped = work.tile([P, N // 4, 4, 4], BF16, name="h_grouped", align_bytes=64)
+            if mode == "fused":
+                gains = gain_sb[:, b, :].unsqueeze(1).unsqueeze(3)
+                pieces = [(k * CHUNK, (k + 1) * CHUNK, nc.gpsimd) for k in range(pool_chunks)]
+                if pool_chunks * CHUNK < N:
+                    pieces.append((pool_chunks * CHUNK, N, nc.vector))
+                for lo, hi, engine in pieces:
+                    cs = slice(lo // 4, hi // 4)
+                    engine.tensor_tensor(grouped[:, cs, :, :].rearrange("p c i t -> p c t i"), woven[:, cs, :, :],
+                                         gains.to_broadcast([P, (hi - lo) // 4, 4, 4]), MULT)
+            else:
+                nc.vector.tensor_copy(grouped[:].rearrange("p c i t -> p c t i"),
+                                      flat[:].rearrange("p t (c i) -> p c t i", i=4))
+            h_codes[h, b] = held([P, N], U32, "h_codes%d%d" % (h, b))
+            h_plane[h, b] = held([P, N], U8, "h_plane%d%d" % (h, b))
+            nc.vector.quantize_mx(h_codes[h, b][:].bitcast(FP8X4), h_plane[h, b][:],
+                                  grouped[:].rearrange("p c i t -> p (c i t)"))
+
+        w3_codes = held([P, 2 * H], U32, "w3_codes")
+
+        w3_planes = held([P, H], U8, "w3_planes")
+
+        def prepare_w3():
+            nc.vector.tensor_copy(w3_planes[:].rearrange("p (g t m) -> p g t m", t=4, m=P),
+                                  w3_sc_raw[:].rearrange("p (g m t) -> p g t m", t=4, m=P))
+            w3_raw = held([P, 2, H], I32, "w3_raw", "late_w3")
+            nc.sync.dma_start(w3_raw[:], w3_words.rearrange("a p c i -> p a (c i)").bitcast(I32))
+            nc.vector.tensor_copy(w3_codes[:].rearrange("p (g t m i) -> p g m t i", t=4, m=P // 4, i=4),
+                                  w3_raw[:].bitcast(U32).rearrange("p a (b m i t) -> p (a b) m t i", b=2, i=4, t=4))
+
+        out_view = out.rearrange("(b p t) j -> b t p j", b=2, t=4)
+
+        def second_stage(h):
+            for b in range(2):
+                for t in range(4):
+                    twice = GROUPS[TWICE] == (h, b)
+                    bank = psum.tile([P, N], F32, name="second_bank", bufs=3)
+                    if twice:
+                        load_passes(bank, h, b, t, False)
+                    cols = slice(b * N + t * P, b * N + (t + 1) * P)
+                    for a in range(2):
+                        nc.tensor.matmul_mx(
+                            bank[:],
+                            lhsT=w3_codes[:, a * H + cols.start:a * H + cols.stop].bitcast(FP8X4),
+                            lhsT_scale=w3_planes[4 * a:P, cols],
+                            rhs=h_codes[h, a][:].bitcast(FP8X4), rhs_scale=h_plane[h, a][:],
+                            start=(a == 0 and not twice), stop=(a == 1))
+                    result = work.tile([P, N], F32, name="result", bufs=8)
+                    if twice:
+                        nc.scalar.copy(result[:], bank[:])
+                    else:
+                        nc.vector.tensor_tensor(result[:], bank[:], load_sb[h, b, t][:], ADD)
+                    nc.sync.dma_start(out_view[b, t, :, h * N:(h + 1) * N], result[:])
+
+        gather(0)
+        prepare_w2(0)
+        first_stage(0)
+        prepare_w2(1)
+        first_stage(1)
+        gather(1)
+        prepare_w3()
+        first_stage(2)
+        second_stage(0)
+        first_stage(3)
+        second_stage(1)

@@ -22,7 +22,7 @@ P = 128
 N = 512
 CHUNK = 128
 GROUPS = ((0, 0), (0, 1), (1, 0), (1, 1))
-MODES = (("pool", 0), ("pool", 0), ("pool", 0), ("fused", 0))
+MODES = (("fused", 0), ("fused", 0), ("fused", 0), ("fused", 0))
 SYNC_MOVES = 5
 TWICE = 3
 
@@ -45,92 +45,113 @@ def tile_list_fleet_ageing_kernel(tc, tab_words, tab_scales, offs, tab2_words, t
         list8 = lists.tile([P, S // 16], U16, name="list8")
         nc.sync.dma_start(list8[:], offs)
 
-        tab_sc = held([P, T], U8, "tab_sc", "late_w2_0")
+        tab_sc = held([P, T], U8, "tab_sc")
         for a in range(2):
             nc.sync.dma_start(tab_sc[a:P:2, :].bitcast(I32), tab_scales[a].bitcast(I32).unsqueeze(1).to_broadcast([16, 4, T // 4]))
-        w1_raw = held([P, 2, H // 2], I32, "w1_raw", "late_tab2")
-        nc.sync.dma_start(w1_raw[:], w1_words.bitcast(I32).rearrange("a p c -> p a c"))
-        tab_w = [held([P, T], I32, "tab_w0", "late_w3"), held([P, T], I32, "tab_w1")]
-        for a in range(2):
-            nc.sync.dma_start(tab_w[a][:], words_of(tab_words[a]))
-        list1 = lists.tile([P, S // 16], U16, name="list1")
-        nc.sync.dma_start(list1[:], offs2)
-
-        w1_sc_raw = held([P, 2 * H], U8, "w1_sc_raw", "late_w2_1")
+        w2_view = w2.rearrange("(p j) c -> p j c", j=4)
+        w2_raw, tab_w, big = {}, {}, {}
+        w1_sc_raw = held([P, 2 * H], U8, "w1_sc_raw")
         v_planes = held([P, 2 * S], U8, "v_planes")
-        w3_sc_raw = held([P, H], U8, "w3_sc_raw")
         tab2_sc = held([P, T], U8, "tab2_sc")
-        for tile in (w1_sc_raw, tab2_sc, v_planes, w3_sc_raw):
+        warm = held([P, 8], F32, "warm", "c")
+        nc.gpsimd.memset(warm[:], 0.0)
+        for tile in (w1_sc_raw, tab2_sc, v_planes):
             nc.vector.memset(tile[:].bitcast(I32), 0)
-        warm = held([P, 8], F32, "warm")
-        nc.vector.memset(warm[:], 0.0)
         warm2 = held([P, 8], F32, "warm2")
-        nc.scalar.activation(warm2[:], warm[:], SIGMOID)
-        for d in range(4):
-            nc.gpsimd.dma_start(w1_sc_raw[32 * d:32 * d + 4, :].bitcast(I32).rearrange("r (a c) -> r a c", a=2),
+        list1 = lists.tile([P, S // 16], U16, name="list1")
+
+        def load_w2(b, queue, tag=""):
+            w2_raw[b] = held([P, 4, N], F32, "w2_raw%d" % b, tag)
+            queue.dma_start(w2_raw[b][:], w2_view[:, :, b * N:(b + 1) * N])
+
+        def load_tab(a, queue, tag=""):
+            tab_w[a] = held([P, T], I32, "tab_w%d" % a, tag)
+            queue.dma_start(tab_w[a][:], words_of(tab_words[a] if a < 2 else tab2_words[0]))
+
+        def load_w1(queue, tag=""):
+            big["w1"] = held([P, 2, H // 2], I32, "w1_raw", tag)
+            queue.dma_start(big["w1"][:], w1_words.bitcast(I32).rearrange("a p c -> p a c"))
+
+        def load_w3(queue, tag=""):
+            big["w3"] = held([P, 2, H], I32, "w3_raw", tag)
+            queue.dma_start(big["w3"][:], w3_words.rearrange("a p c i -> p a (c i)").bitcast(I32))
+
+        def load_w1_scales(queue):
+            for d in range(4):
+                queue.dma_start(w1_sc_raw[32 * d:32 * d + 4, :].bitcast(I32).rearrange("r (a c) -> r a c", a=2),
                                 w1_scales[:, 4 * d:4 * d + 4, :].bitcast(I32).rearrange("a r c -> r a c"))
 
-        picked_sc = held([P, S], U8, "picked_sc")
-        nc.vector.tensor_copy(picked_sc[:], tab_sc[:].indirect(list8[:]))
-        w2_view = w2.rearrange("(p j) c -> p j c", j=4)
-        w2_raw = [held([P, 4, N], F32, "w2_raw0", "late_w2_0")]
-        for a in range(2):
-            for r in range(4):
-                if 4 * a + r == SYNC_MOVES:
-                    nc.sync.dma_start(w2_raw[0][:], w2_view[:, :, 0:N])
-                nc.sync.dma_start(v_planes[r:P:32, a * S:(a + 1) * S].bitcast(I32),
-                                  picked_sc[8 * r + a:P:32, :].bitcast(I32))
+        def load_w3_scales(queue, tag=""):
+            big["w3_sc"] = held([P, H], U8, "w3_sc_raw", tag)
+            nc.vector.memset(big["w3_sc"][:].bitcast(I32), 0)
+            for d in range(4):
+                queue.dma_start(big["w3_sc"][32 * d:32 * d + 8, :].bitcast(I32), w3_scales[:, 4 * d:4 * d + 4, :].bitcast(I32))
 
-        w1_codes = held([P, 4 * H], U8, "w1_codes")
-        nc.vector.tensor_copy(w1_codes[:].bitcast(U16).rearrange("p (g t m i) -> p g m t i", g=4, t=4, i=8),
-                              w1_raw[:].bitcast(U16).rearrange("p a (b m i t) -> p (a b) m t i", b=2, t=4, i=8))
-        w1_planes = held([P, 2 * H], U8, "w1_planes")
-        nc.vector.tensor_copy(w1_planes[:].rearrange("p (g t m) -> p g t m", t=4, m=P),
-                              w1_sc_raw[:].rearrange("p (g m t) -> p g t m", t=4, m=P))
+        def load_tab2_scales(queue):
+            for d in range(4):
+                queue.dma_start(tab2_sc[32 * d:32 * d + 4, :].bitcast(I32), tab2_scales[0, 4 * d:4 * d + 4, :].bitcast(I32))
 
-        tab2_w = held([P, T], I32, "tab2_w", "late_tab2")
-        nc.sync.dma_start(tab2_w[:], words_of(tab2_words[0]))
-        w2_raw.append(held([P, 4, N], F32, "w2_raw1", "late_w2_1"))
-        nc.sync.dma_start(w2_raw[1][:], w2_view[:, :, N:2 * N])
+        def load_columns(queue, tag=""):
+            big["columns"] = held([P, 2, 2, 4], F32, "columns", tag)
+            queue.dma_start(big["columns"][:, 0, :, :], bias.rearrange("(b p t) -> p b t", b=2, t=4))
+            queue.dma_start(big["columns"][:, 1, :, :], gain.rearrange("(b p t) -> p b t", b=2, t=4))
 
-        for d in range(4):
-            nc.gpsimd.dma_start(tab2_sc[32 * d:32 * d + 4, :].bitcast(I32), tab2_scales[0, 4 * d:4 * d + 4, :].bitcast(I32))
+        def pick_scales(tag=""):
+            big["picked"] = held([P, S], U8, "picked_sc", tag)
+            nc.vector.tensor_copy(big["picked"][:], tab_sc[:].indirect(list8[:]))
 
-        bias_sb = held([P, 2, 4], F32, "bias_sb")
-        gain_sb = held([P, 2, 4], F32, "gain_sb")
-        nc.gpsimd.dma_start(bias_sb[:], bias.rearrange("(b p t) -> p b t", b=2, t=4))
-        nc.gpsimd.dma_start(gain_sb[:], gain.rearrange("(b p t) -> p b t", b=2, t=4))
-        for d in range(4):
-            nc.gpsimd.dma_start(w3_sc_raw[32 * d:32 * d + 8, :].bitcast(I32), w3_scales[:, 4 * d:4 * d + 4, :].bitcast(I32))
+        def move_rows(queue, a, rows):
+            for r in rows:
+                queue.dma_start(v_planes[r:P:32, a * S:(a + 1) * S].bitcast(I32),
+                                big["picked"][8 * r + a:P:32, :].bitcast(I32))
+
+        def order_w1_planes(tag=""):
+            big["w1_planes"] = held([P, 2 * H], U8, "w1_planes", tag)
+            nc.vector.tensor_copy(big["w1_planes"][:].rearrange("p (g t m) -> p g t m", t=4, m=P),
+                                  w1_sc_raw[:].rearrange("p (g m t) -> p g t m", t=4, m=P))
+
+        def order_w1(tag=""):
+            big["w1_codes"] = held([P, 4 * H], U8, "w1_codes", tag)
+            nc.vector.tensor_copy(big["w1_codes"][:].bitcast(U16).rearrange("p (g t m i) -> p g m t i", g=4, t=4, i=8),
+                                  big["w1"][:].bitcast(U16).rearrange("p a (b m i t) -> p (a b) m t i", b=2, t=4, i=8))
+
         w2_codes, w2_plane = {}, {}
 
-        def prepare_w2(b):
-            grouped = work.tile([P, 4 * N], BF16, name="w2_grouped", align_bytes=64)
+        def prepare_w2(b, tag=""):
+            grouped = held([P, 4 * N], BF16, "w2_grouped%d" % b, tag)
             nc.scalar.copy(grouped[:].rearrange("p (t m j) -> p m t j", t=4, j=4),
                            w2_raw[b][:].rearrange("p j (m t) -> p m t j", t=4))
             w2_codes[b] = held([P, N], U32, "w2_codes%d" % b)
             w2_plane[b] = held([P, N], U8, "w2_plane%d" % b)
             nc.vector.quantize_mx(w2_codes[b][:].bitcast(FP8X4), w2_plane[b][:], grouped[:])
 
-        v_codes, v2_codes, v2_plane = {}, {}, {}
+        picked = {}
 
-        def gather(h):
-            cols = slice(h * N // 16, (h + 1) * N // 16)
-            for a in range(2):
-                v_codes[h, a] = held([P, N], U32, "v_codes%d%d" % (h, a))
-                nc.vector.tensor_copy(v_codes[h, a][:], tab_w[a][:].bitcast(U32).indirect(list8[:, cols]))
-            v2_plane[h] = held([P, N], U8, "v2_plane%d" % h)
-            nc.vector.tensor_copy(v2_plane[h][:], tab2_sc[:].indirect(list1[:, cols]))
-            v2_codes[h] = held([P, N], U32, "v2_codes%d" % h)
-            nc.vector.tensor_copy(v2_codes[h][:], tab2_w[:].bitcast(U32).indirect(list1[:, cols]))
+        def pick(a, h, tag=""):
+            picked[a, h] = held([P, N], U32, "picked%d%d" % (a, h), tag)
+            picks = list8 if a < 2 else list1
+            nc.vector.tensor_copy(picked[a, h][:], tab_w[a][:].bitcast(U32).indirect(picks[:, h * N // 16:(h + 1) * N // 16]))
+
+        def pick_tab2_scales(h, tag=""):
+            picked[3, h] = held([P, N], U8, "v2_plane%d" % h, tag)
+            nc.vector.tensor_copy(picked[3, h][:], tab2_sc[:].indirect(list1[:, h * N // 16:(h + 1) * N // 16]))
+
+        def order_w3(tag="", tag2=""):
+            big["w3_planes"] = held([P, H], U8, "w3_planes", tag2)
+            nc.vector.tensor_copy(big["w3_planes"][:].rearrange("p (g t m) -> p g t m", t=4, m=P),
+                                  big["w3_sc"][:].rearrange("p (g m t) -> p g t m", t=4, m=P))
+            big["w3_codes"] = held([P, 2 * H], U32, "w3_codes", tag)
+            for g in range(0, 4, 4):
+                nc.vector.tensor_copy(big["w3_codes"][:].rearrange("p (g t m i) -> p g m t i", t=4, m=P // 4, i=4)[:, g:g + 4, :, :, :],
+                                  big["w3"][:].bitcast(U32).rearrange("p a (b m i t) -> p (a b) m t i", b=2, i=4, t=4)[:, g:g + 4, :, :, :])
 
         def load_passes(bank, h, b, t, stop):
             for a in range(2):
                 nc.tensor.matmul_mx(
                     bank[:],
-                    lhsT=w1_codes[:, 2 * (a * H + b * N + t * P):2 * (a * H + b * N + (t + 1) * P)].bitcast(FP4X4),
-                    lhsT_scale=w1_planes[:, a * H + b * N + t * P:a * H + b * N + (t + 1) * P],
-                    rhs=v_codes[h, a][:].bitcast(FP8X4),
+                    lhsT=big["w1_codes"][:, 2 * (a * H + b * N + t * P):2 * (a * H + b * N + (t + 1) * P)].bitcast(FP4X4),
+                    lhsT_scale=big["w1_planes"][:, a * H + b * N + t * P:a * H + b * N + (t + 1) * P],
+                    rhs=picked[a, h][:].bitcast(FP8X4),
                     rhs_scale=v_planes[:, a * S + h * N:a * S + (h + 1) * N],
                     start=(a == 0), stop=(stop and a == 1))
 
@@ -138,18 +159,18 @@ def tile_list_fleet_ageing_kernel(tc, tab_words, tab_scales, offs, tab2_words, t
             nc.tensor.matmul_mx(
                 bank[:],
                 lhsT=w2_codes[b][:, t * P:(t + 1) * P].bitcast(FP8X4), lhsT_scale=w2_plane[b][:, t * P:(t + 1) * P],
-                rhs=v2_codes[h][:].bitcast(FP8X4), rhs_scale=v2_plane[h][:], start=start, stop=True)
+                rhs=picked[2, h][:].bitcast(FP8X4), rhs_scale=picked[3, h][:], start=start, stop=True)
 
         load_sb, h_codes, h_plane = {}, {}, {}
 
         def first_stage(g):
             h, b = GROUPS[g]
             mode, pool_chunks = MODES[g]
-            stress = work.tile([P, 4 * N], F32, name="stress")
+            stress = work.tile([P, 4 * N], F32, name="stress", bufs=3)
             woven = stress[:].rearrange("p (c t i) -> p c t i", t=4, i=4)
-            flat = work.tile([P, 4, N], BF16, name="h_flat")
+            flat = work.tile([P, 4, N], BF16, name="h_flat", bufs=3)
             for t in range(4):
-                column = bias_sb[:, b, t:t + 1]
+                column = big["columns"][:, 0, b, t:t + 1]
                 if g == TWICE:
                     bank = psum.tile([P, N], F32, name="sum_bank", bufs=3)
                     load_passes(bank, h, b, t, False)
@@ -162,78 +183,117 @@ def tile_list_fleet_ageing_kernel(tc, tab_words, tab_scales, offs, tab2_words, t
                     nc.scalar.copy(load_sb[h, b, t][:], bank[:])
                     bank = psum.tile([P, N], F32, name="sum_bank", bufs=3)
                     weather_pass(bank, h, b, t, True)
-                    source = work.tile([P, N], F32, name="summed", bufs=4)
+                    source = held([P, N], F32, "summed%d%d" % (g, t))
                     nc.vector.tensor_tensor(source[:], bank[:], load_sb[h, b, t][:], ADD)
                 if mode == "fused":
                     nc.scalar.activation(woven[:, :, t, :], source[:].rearrange("p (c i) -> p c i", i=4), SIGMOID, bias=column)
                 else:
                     nc.scalar.activation(stress[:, t * N:(t + 1) * N], source[:], SIGMOID, bias=column)
                     if mode == "pool":
-                        nc.gpsimd.tensor_scalar(flat[:, t, :], stress[:, t * N:(t + 1) * N], gain_sb[:, b, t:t + 1], 0.0, MULT, ADD)
+                        nc.gpsimd.tensor_scalar(flat[:, t, :], stress[:, t * N:(t + 1) * N], big["columns"][:, 1, b, t:t + 1], 0.0, MULT, ADD)
                     else:
-                        nc.scalar.activation(flat[:, t, :], stress[:, t * N:(t + 1) * N], COPY, scale=gain_sb[:, b, t:t + 1])
+                        nc.scalar.activation(flat[:, t, :], stress[:, t * N:(t + 1) * N], COPY, scale=big["columns"][:, 1, b, t:t + 1])
+            return woven, flat
+
+        def quantise_h(g, woven, flat):
+            h, b = GROUPS[g]
+            mode, pool_chunks = MODES[g]
             grouped = work.tile([P, N // 4, 4, 4], BF16, name="h_grouped", align_bytes=64)
             if mode == "fused":
-                gains = gain_sb[:, b, :].unsqueeze(1).unsqueeze(3)
+                gains = big["columns"][:, 1, b, :].unsqueeze(1).unsqueeze(3)
                 pieces = [(k * CHUNK, (k + 1) * CHUNK, nc.gpsimd) for k in range(pool_chunks)]
                 if pool_chunks * CHUNK < N:
                     pieces.append((pool_chunks * CHUNK, N, nc.vector))
                 for lo, hi, engine in pieces:
                     cs = slice(lo // 4, hi // 4)
-                    engine.tensor_tensor(grouped[:, cs, :, :].rearrange("p c i t -> p c t i"), woven[:, cs, :, :],
-                                         gains.to_broadcast([P, (hi - lo) // 4, 4, 4]), MULT)
+                    if engine is nc.vector:
+                        engine.tensor_tensor(grouped[:, cs, :, :].rearrange("p c i t -> p c t i"), woven[:, cs, :, :],
+                                             gains.to_broadcast([P, (hi - lo) // 4, 4, 4]), MULT)
+                    else:
+                        engine.tensor_tensor(grouped[:, cs, :, :], woven[:, cs, :, :].rearrange("p c t i -> p c i t"),
+                                             gains.to_broadcast([P, (hi - lo) // 4, 4, 4]).rearrange("p c t i -> p c i t"), MULT)
             else:
-                nc.vector.tensor_copy(grouped[:].rearrange("p c i t -> p c t i"),
-                                      flat[:].rearrange("p t (c i) -> p c t i", i=4))
+                weave = nc.scalar.copy if pool_chunks else nc.vector.tensor_copy
+                weave(grouped[:].rearrange("p c i t -> p c t i"), flat[:].rearrange("p t (c i) -> p c t i", i=4))
             h_codes[h, b] = held([P, N], U32, "h_codes%d%d" % (h, b))
             h_plane[h, b] = held([P, N], U8, "h_plane%d%d" % (h, b))
             nc.vector.quantize_mx(h_codes[h, b][:].bitcast(FP8X4), h_plane[h, b][:],
                                   grouped[:].rearrange("p c i t -> p (c i t)"))
 
-        w3_codes = held([P, 2 * H], U32, "w3_codes")
-
-        w3_planes = held([P, H], U8, "w3_planes")
-
-        def prepare_w3():
-            nc.vector.tensor_copy(w3_planes[:].rearrange("p (g t m) -> p g t m", t=4, m=P),
-                                  w3_sc_raw[:].rearrange("p (g m t) -> p g t m", t=4, m=P))
-            w3_raw = held([P, 2, H], I32, "w3_raw", "late_w3")
-            nc.sync.dma_start(w3_raw[:], w3_words.rearrange("a p c i -> p a (c i)").bitcast(I32))
-            nc.vector.tensor_copy(w3_codes[:].rearrange("p (g t m i) -> p g m t i", t=4, m=P // 4, i=4),
-                                  w3_raw[:].bitcast(U32).rearrange("p a (b m i t) -> p (a b) m t i", b=2, i=4, t=4))
 
         out_view = out.rearrange("(b p t) j -> b t p j", b=2, t=4)
+
+        def mix_pass(bank, h, b, t, a):
+            cols = slice(b * N + t * P, b * N + (t + 1) * P)
+            nc.tensor.matmul_mx(
+                bank[:],
+                lhsT=big["w3_codes"][:, a * H + cols.start:a * H + cols.stop].bitcast(FP8X4),
+                lhsT_scale=big["w3_planes"][4 * a:P, cols],
+                rhs=h_codes[h, a][:].bitcast(FP8X4), rhs_scale=h_plane[h, a][:],
+                start=(a == 0 and GROUPS[TWICE] != (h, b)), stop=(a == 1))
+
+        def open_tile(h, b, t, tag, bufs):
+            bank = psum.tile([P, N], F32, name=tag, bufs=bufs)
+            if GROUPS[TWICE] == (h, b):
+                load_passes(bank, h, b, t, False)
+            mix_pass(bank, h, b, t, 0)
+            return bank
+
+        def close_tile(bank, h, b, t):
+            mix_pass(bank, h, b, t, 1)
+            result = work.tile([P, N], F32, name="result", bufs=8)
+            if GROUPS[TWICE] == (h, b):
+                nc.scalar.copy(result[:], bank[:])
+            else:
+                nc.vector.tensor_tensor(result[:], bank[:], load_sb[h, b, t][:], ADD)
+            nc.sync.dma_start(out_view[b, t, :, h * N:(h + 1) * N], result[:])
 
         def second_stage(h):
             for b in range(2):
                 for t in range(4):
-                    twice = GROUPS[TWICE] == (h, b)
-                    bank = psum.tile([P, N], F32, name="second_bank", bufs=3)
-                    if twice:
-                        load_passes(bank, h, b, t, False)
-                    cols = slice(b * N + t * P, b * N + (t + 1) * P)
-                    for a in range(2):
-                        nc.tensor.matmul_mx(
-                            bank[:],
-                            lhsT=w3_codes[:, a * H + cols.start:a * H + cols.stop].bitcast(FP8X4),
-                            lhsT_scale=w3_planes[4 * a:P, cols],
-                            rhs=h_codes[h, a][:].bitcast(FP8X4), rhs_scale=h_plane[h, a][:],
-                            start=(a == 0 and not twice), stop=(a == 1))
-                    result = work.tile([P, N], F32, name="result", bufs=8)
-                    if twice:
-                        nc.scalar.copy(result[:], bank[:])
-                    else:
-                        nc.vector.tensor_tensor(result[:], bank[:], load_sb[h, b, t][:], ADD)
-                    nc.sync.dma_start(out_view[b, t, :, h * N:(h + 1) * N], result[:])
+                    close_tile(open_tile(h, b, t, "second_bank", 3), h, b, t)
 
-        gather(0)
+        last_tiles = [(b, t) for t in range(4) for b in range(2)]
+        last_tags = [("load_bank", 2)] * 2 + [("second_bank", 3)] * 3 + [("sum_bank", 3)] * 3
+
+        nc.scalar.activation(warm2[:], warm[:], SIGMOID)
+        load_w1_scales(nc.sync)
+        load_w1(nc.sync)
+        load_tab(0, nc.sync)
+        load_tab(1, nc.sync)
+        nc.sync.dma_start(list1[:], offs2)
+        load_tab2_scales(nc.gpsimd)
+        load_columns(nc.gpsimd, "c")
+        pick_scales()
+        move_rows(nc.sync, 0, range(4))
+        move_rows(nc.sync, 1, range(1))
+        load_w2(0, nc.sync)
+        move_rows(nc.sync, 1, range(1, 4))
+        load_tab(2, nc.sync)
+        load_w2(1, nc.sync)
+        load_w3(nc.sync)
+        load_w3_scales(nc.sync)
+        order_w1()
+        order_w1_planes()
+        pick(0, 0)
+        pick(1, 0)
         prepare_w2(0)
-        first_stage(0)
-        prepare_w2(1)
-        first_stage(1)
-        gather(1)
-        prepare_w3()
-        first_stage(2)
+        pick_tab2_scales(0)
+        pick(2, 0)
+        pick(0, 1)
+        pick(1, 1)
+        pick_tab2_scales(1)
+        pick(2, 1)
+        first = first_stage(0)
+        prepare_w2(1, "summed03")
+        quantise_h(0, *first)
+        order_w3()
+        quantise_h(1, *first_stage(1))
+        third = first_stage(2)
         second_stage(0)
-        first_stage(3)
-        second_stage(1)
+        fourth = first_stage(3)
+        quantise_h(2, *third)
+        quantise_h(3, *fourth)
+        banks = [open_tile(1, b, t, tag, bufs) for (b, t), (tag, bufs) in zip(last_tiles, last_tags)]
+        for bank, (b, t) in zip(banks, last_tiles):
+            close_tile(bank, 1, b, t)

@@ -22,7 +22,7 @@ P = 128
 N = 512
 CHUNK = 128
 GROUPS = ((0, 0), (0, 1), (1, 0), (1, 1))
-MODES = (("fused", 0), ("fused", 0), ("fused", 0), ("fused", 0))
+MODES = (("fused", 0), ("fused", 0), ("act", 0), ("act", 4))
 SYNC_MOVES = 5
 TWICE = 3
 
@@ -53,7 +53,7 @@ def tile_list_fleet_ageing_kernel(tc, tab_words, tab_scales, offs, tab2_words, t
         w1_sc_raw = held([P, 2 * H], U8, "w1_sc_raw")
         v_planes = held([P, 2 * S], U8, "v_planes")
         tab2_sc = held([P, T], U8, "tab2_sc")
-        warm = held([P, 8], F32, "warm", "c")
+        warm = held([P, 8], F32, "warm")
         nc.gpsimd.memset(warm[:], 0.0)
         for tile in (w1_sc_raw, tab2_sc, v_planes):
             nc.vector.memset(tile[:].bitcast(I32), 0)
@@ -91,10 +91,10 @@ def tile_list_fleet_ageing_kernel(tc, tab_words, tab_scales, offs, tab2_words, t
             for d in range(4):
                 queue.dma_start(tab2_sc[32 * d:32 * d + 4, :].bitcast(I32), tab2_scales[0, 4 * d:4 * d + 4, :].bitcast(I32))
 
-        def load_columns(queue, tag=""):
-            big["columns"] = held([P, 2, 2, 4], F32, "columns", tag)
-            queue.dma_start(big["columns"][:, 0, :, :], bias.rearrange("(b p t) -> p b t", b=2, t=4))
-            queue.dma_start(big["columns"][:, 1, :, :], gain.rearrange("(b p t) -> p b t", b=2, t=4))
+        def load_columns(queue):
+            for name, vector in (("bias", bias), ("gain", gain)):
+                big[name] = held([P, 2, 4], F32, name + "_sb")
+                queue.dma_start(big[name][:], vector.rearrange("(b p t) -> p b t", b=2, t=4))
 
         def pick_scales(tag=""):
             big["picked"] = held([P, S], U8, "picked_sc", tag)
@@ -117,9 +117,9 @@ def tile_list_fleet_ageing_kernel(tc, tab_words, tab_scales, offs, tab2_words, t
 
         w2_codes, w2_plane = {}, {}
 
-        def prepare_w2(b, tag=""):
+        def prepare_w2(b, tag="", cast=nc.scalar.copy):
             grouped = held([P, 4 * N], BF16, "w2_grouped%d" % b, tag)
-            nc.scalar.copy(grouped[:].rearrange("p (t m j) -> p m t j", t=4, j=4),
+            cast(grouped[:].rearrange("p (t m j) -> p m t j", t=4, j=4),
                            w2_raw[b][:].rearrange("p j (m t) -> p m t j", t=4))
             w2_codes[b] = held([P, N], U32, "w2_codes%d" % b)
             w2_plane[b] = held([P, N], U8, "w2_plane%d" % b)
@@ -163,62 +163,59 @@ def tile_list_fleet_ageing_kernel(tc, tab_words, tab_scales, offs, tab2_words, t
 
         load_sb, h_codes, h_plane = {}, {}, {}
 
+        def keep_load(g):
+            h, b = GROUPS[g]
+            for t in range(4):
+                bank = psum.tile([P, N], F32, name="sum_bank", bufs=5)
+                load_passes(bank, h, b, t, True)
+                load_sb[h, b, t] = held([P, N], F32, "load_sb%d%d%d" % (h, b, t))
+                nc.scalar.copy(load_sb[h, b, t][:], bank[:])
+
         def first_stage(g):
             h, b = GROUPS[g]
             mode, pool_chunks = MODES[g]
-            stress = work.tile([P, 4 * N], F32, name="stress", bufs=3)
-            woven = stress[:].rearrange("p (c t i) -> p c t i", t=4, i=4)
-            flat = work.tile([P, 4, N], BF16, name="h_flat", bufs=3)
+            stress = work.tile([P, 4, N], F32, name="stress", bufs=4)
+            flat = work.tile([P, 4, N], BF16, name="h_flat", bufs=4) if mode != "fused" else None
             for t in range(4):
-                column = big["columns"][:, 0, b, t:t + 1]
+                column = big["bias"][:, b, t:t + 1]
                 if g == TWICE:
-                    bank = psum.tile([P, N], F32, name="sum_bank", bufs=3)
+                    bank = psum.tile([P, N], F32, name="sum_bank", bufs=5)
                     load_passes(bank, h, b, t, False)
                     weather_pass(bank, h, b, t, False)
                     source = bank
                 else:
-                    bank = psum.tile([P, N], F32, name="load_bank", bufs=2)
-                    load_passes(bank, h, b, t, True)
-                    load_sb[h, b, t] = held([P, N], F32, "load_sb%d%d%d" % (h, b, t))
-                    nc.scalar.copy(load_sb[h, b, t][:], bank[:])
-                    bank = psum.tile([P, N], F32, name="sum_bank", bufs=3)
+                    bank = psum.tile([P, N], F32, name="sum_bank", bufs=5)
                     weather_pass(bank, h, b, t, True)
                     source = held([P, N], F32, "summed%d%d" % (g, t))
                     nc.vector.tensor_tensor(source[:], bank[:], load_sb[h, b, t][:], ADD)
-                if mode == "fused":
-                    nc.scalar.activation(woven[:, :, t, :], source[:].rearrange("p (c i) -> p c i", i=4), SIGMOID, bias=column)
-                else:
-                    nc.scalar.activation(stress[:, t * N:(t + 1) * N], source[:], SIGMOID, bias=column)
-                    if mode == "pool":
-                        nc.gpsimd.tensor_scalar(flat[:, t, :], stress[:, t * N:(t + 1) * N], big["columns"][:, 1, b, t:t + 1], 0.0, MULT, ADD)
-                    else:
-                        nc.scalar.activation(flat[:, t, :], stress[:, t * N:(t + 1) * N], COPY, scale=big["columns"][:, 1, b, t:t + 1])
-            return woven, flat
+                nc.scalar.activation(stress[:, t, :], source[:], SIGMOID, bias=column)
+                if mode == "pool":
+                    nc.gpsimd.tensor_scalar(flat[:, t, :], stress[:, t, :], big["gain"][:, b, t:t + 1], 0.0, MULT, ADD)
+                if mode == "act":
+                    nc.scalar.activation(flat[:, t, :], stress[:, t, :], COPY, scale=big["gain"][:, b, t:t + 1])
+            return stress, flat
 
-        def quantise_h(g, woven, flat):
+        def quantise_h(g, stress, flat):
             h, b = GROUPS[g]
-            mode, pool_chunks = MODES[g]
-            grouped = work.tile([P, N // 4, 4, 4], BF16, name="h_grouped", align_bytes=64)
+            mode, on_scalar = MODES[g]
+            grouped = work.tile([P, 4 * N], BF16, name="h_grouped", align_bytes=64, bufs=3)
             if mode == "fused":
-                gains = big["columns"][:, 1, b, :].unsqueeze(1).unsqueeze(3)
-                pieces = [(k * CHUNK, (k + 1) * CHUNK, nc.gpsimd) for k in range(pool_chunks)]
-                if pool_chunks * CHUNK < N:
-                    pieces.append((pool_chunks * CHUNK, N, nc.vector))
-                for lo, hi, engine in pieces:
-                    cs = slice(lo // 4, hi // 4)
-                    if engine is nc.vector:
-                        engine.tensor_tensor(grouped[:, cs, :, :].rearrange("p c i t -> p c t i"), woven[:, cs, :, :],
-                                             gains.to_broadcast([P, (hi - lo) // 4, 4, 4]), MULT)
-                    else:
-                        engine.tensor_tensor(grouped[:, cs, :, :], woven[:, cs, :, :].rearrange("p c t i -> p c i t"),
-                                             gains.to_broadcast([P, (hi - lo) // 4, 4, 4]).rearrange("p c t i -> p c i t"), MULT)
+                gains = big["gain"][:, b, :].unsqueeze(1).unsqueeze(3).to_broadcast([P, N // 2, 4, 2])
+                nc.vector.tensor_tensor(grouped[:].rearrange("p (c i t) -> p c t i", i=2, t=4),
+                                        stress[:].rearrange("p t (c i) -> p c t i", i=2), gains, MULT)
             else:
-                weave = nc.scalar.copy if pool_chunks else nc.vector.tensor_copy
-                weave(grouped[:].rearrange("p c i t -> p c t i"), flat[:].rearrange("p t (c i) -> p c t i", i=4))
+                for k in range(on_scalar):
+                    cs = slice(k * 32, (k + 1) * 32)
+                    nc.scalar.copy(grouped[:].rearrange("p (c i t) -> p c t i", i=4, t=4)[:, cs, :, :],
+                                   flat[:].rearrange("p t (c i) -> p c t i", i=4)[:, cs, :, :])
+                if on_scalar < 4:
+                    cs = slice(on_scalar * 32, 128)
+                    nc.vector.tensor_copy(grouped[:].rearrange("p (c i t) -> p c t i", i=4, t=4)[:, cs, :, :],
+                                          flat[:].rearrange("p t (c i) -> p c t i", i=4)[:, cs, :, :])
             h_codes[h, b] = held([P, N], U32, "h_codes%d%d" % (h, b))
             h_plane[h, b] = held([P, N], U8, "h_plane%d%d" % (h, b))
             nc.vector.quantize_mx(h_codes[h, b][:].bitcast(FP8X4), h_plane[h, b][:],
-                                  grouped[:].rearrange("p c i t -> p (c i t)"))
+                                  grouped[:])
 
 
         out_view = out.rearrange("(b p t) j -> b t p j", b=2, t=4)
@@ -254,7 +251,7 @@ def tile_list_fleet_ageing_kernel(tc, tab_words, tab_scales, offs, tab2_words, t
                     close_tile(open_tile(h, b, t, "second_bank", 3), h, b, t)
 
         last_tiles = [(b, t) for t in range(4) for b in range(2)]
-        last_tags = [("load_bank", 2)] * 2 + [("second_bank", 3)] * 3 + [("sum_bank", 3)] * 3
+        last_tags = [("sum_bank", 5)] * 5 + [("second_bank", 3)] * 3
 
         nc.scalar.activation(warm2[:], warm[:], SIGMOID)
         load_w1_scales(nc.sync)
@@ -263,7 +260,7 @@ def tile_list_fleet_ageing_kernel(tc, tab_words, tab_scales, offs, tab2_words, t
         load_tab(1, nc.sync)
         nc.sync.dma_start(list1[:], offs2)
         load_tab2_scales(nc.gpsimd)
-        load_columns(nc.gpsimd, "c")
+        load_columns(nc.gpsimd)
         pick_scales()
         move_rows(nc.sync, 0, range(4))
         move_rows(nc.sync, 1, range(1))
@@ -277,23 +274,26 @@ def tile_list_fleet_ageing_kernel(tc, tab_words, tab_scales, offs, tab2_words, t
         order_w1_planes()
         pick(0, 0)
         pick(1, 0)
-        prepare_w2(0)
         pick_tab2_scales(0)
+        prepare_w2(0, "", nc.vector.tensor_copy)
         pick(2, 0)
         pick(0, 1)
         pick(1, 1)
         pick_tab2_scales(1)
         pick(2, 1)
+        keep_load(0)
+        keep_load(1)
+        keep_load(2)
+        prepare_w2(1, "", nc.scalar.copy)
         first = first_stage(0)
-        prepare_w2(1, "summed03")
-        quantise_h(0, *first)
         order_w3()
-        quantise_h(1, *first_stage(1))
+        second = first_stage(1)
+        quantise_h(0, *first)
         third = first_stage(2)
-        second_stage(0)
-        fourth = first_stage(3)
+        quantise_h(1, *second)
         quantise_h(2, *third)
-        quantise_h(3, *fourth)
+        quantise_h(3, *first_stage(3))
+        second_stage(0)
         banks = [open_tile(1, b, t, tag, bufs) for (b, t), (tag, bufs) in zip(last_tiles, last_tags)]
         for bank, (b, t) in zip(banks, last_tiles):
             close_tile(bank, 1, b, t)

@@ -20,11 +20,10 @@ COPY = mybir.ActivationFunctionType.Copy
 
 P = 128
 N = 512
-CHUNK = 128
 GROUPS = ((0, 0), (0, 1), (1, 0), (1, 1))
-MODES = (("fused", 0), ("fused", 0), ("act", 0), ("act", 4))
-SYNC_MOVES = 5
-TWICE = 3
+LAST = GROUPS[3]
+RING = 4
+WEAVE_PIECES = 4
 
 
 def tile_list_fleet_ageing_kernel(tc, tab_words, tab_scales, offs, tab2_words, tab2_scales, offs2,
@@ -33,205 +32,205 @@ def tile_list_fleet_ageing_kernel(tc, tab_words, tab_scales, offs, tab2_words, t
     with ExitStack() as ctx:
         lists = ctx.enter_context(tc.tile_pool(name="lists", bufs=1))
         keep = ctx.enter_context(tc.tile_pool(name="keep", bufs=1))
-        work = ctx.enter_context(tc.tile_pool(name="work", bufs=2))
-        psum = ctx.enter_context(tc.psum_pool(name="psum", bufs=1))
+        work = ctx.enter_context(tc.tile_pool(name="work", bufs=1))
+        psum = ctx.enter_context(tc.psum_pool(name="psum", bufs=RING))
 
-        def held(shape, dtype, name, tag=""):
-            return keep.tile(shape, dtype, name=name, tag=tag or name, align_bytes=64)
-
-        def words_of(dram_pass):
-            return dram_pass.rearrange("p c i -> p (c i)").bitcast(I32)
+        def held(shape, dtype, name):
+            return keep.tile(shape, dtype, name=name, align_bytes=64)
 
         list8 = lists.tile([P, S // 16], U16, name="list8")
         nc.sync.dma_start(list8[:], offs)
 
         tab_sc = held([P, T], U8, "tab_sc")
         for a in range(2):
-            nc.sync.dma_start(tab_sc[a:P:2, :].bitcast(I32), tab_scales[a].bitcast(I32).unsqueeze(1).to_broadcast([16, 4, T // 4]))
-        w2_view = w2.rearrange("(p j) c -> p j c", j=4)
-        w2_raw, tab_w, big = {}, {}, {}
+            nc.sync.dma_start(tab_sc[a:P:2, :].bitcast(I32),
+                              tab_scales[a].bitcast(I32).unsqueeze(1).to_broadcast([16, 4, T // 4]))
+
         w1_sc_raw = held([P, 2 * H], U8, "w1_sc_raw")
-        v_planes = held([P, 2 * S], U8, "v_planes")
         tab2_sc = held([P, T], U8, "tab2_sc")
-        warm = held([P, 8], F32, "warm")
-        nc.gpsimd.memset(warm[:], 0.0)
-        for tile in (w1_sc_raw, tab2_sc, v_planes):
-            nc.vector.memset(tile[:].bitcast(I32), 0)
-        warm2 = held([P, 8], F32, "warm2")
+        v_planes = [held([P, S], U8, "v_plane%d" % a) for a in range(2)]
+        for plane in (w1_sc_raw, tab2_sc, *v_planes):
+            nc.vector.memset(plane[:].bitcast(I32), 0)
+
+        w1_raw = held([P, 2, H // 2], I32, "w1_raw")
+        nc.sync.dma_start(w1_raw[:], w1_words.bitcast(I32).rearrange("a p c -> p a c"))
+        for d in range(4):
+            nc.sync.dma_start(w1_sc_raw[32 * d:32 * d + 4, :].bitcast(I32).rearrange("r (a c) -> r a c", a=2),
+                              w1_scales[:, 4 * d:4 * d + 4, :].bitcast(I32).rearrange("a r c -> r a c"))
         list1 = lists.tile([P, S // 16], U16, name="list1")
+        nc.sync.dma_start(list1[:], offs2)
 
-        def load_w2(b, queue, tag=""):
-            w2_raw[b] = held([P, 4, N], F32, "w2_raw%d" % b, tag)
-            queue.dma_start(w2_raw[b][:], w2_view[:, :, b * N:(b + 1) * N])
+        def load_table(dram_pass, name):
+            window = held([P, T], I32, name)
+            nc.sync.dma_start(window[:], dram_pass.rearrange("p c i -> p (c i)").bitcast(I32))
+            return window
 
-        def load_tab(a, queue, tag=""):
-            tab_w[a] = held([P, T], I32, "tab_w%d" % a, tag)
-            queue.dma_start(tab_w[a][:], words_of(tab_words[a] if a < 2 else tab2_words[0]))
+        def load_tab2_scales(quadrants):
+            for d in quadrants:
+                nc.sync.dma_start(tab2_sc[32 * d:32 * d + 4, :].bitcast(I32),
+                                  tab2_scales[0, 4 * d:4 * d + 4, :].bitcast(I32))
 
-        def load_w1(queue, tag=""):
-            big["w1"] = held([P, 2, H // 2], I32, "w1_raw", tag)
-            queue.dma_start(big["w1"][:], w1_words.bitcast(I32).rearrange("a p c -> p a c"))
+        def load_w2(b):
+            rows = held([P, 4, N], F32, "w2_raw%d" % b)
+            nc.sync.dma_start(rows[:], w2.rearrange("(p j) c -> p j c", j=4)[:, :, b * N:(b + 1) * N])
+            return rows
 
-        def load_w3(queue, tag=""):
-            big["w3"] = held([P, 2, H], I32, "w3_raw", tag)
-            queue.dma_start(big["w3"][:], w3_words.rearrange("a p c i -> p a (c i)").bitcast(I32))
+        def load_per_channel(vector, name):
+            columns = held([P, 2, 4], F32, name)
+            nc.sync.dma_start(columns[:], vector.rearrange("(b p t) -> p b t", b=2, t=4))
+            return columns
 
-        def load_w1_scales(queue):
-            for d in range(4):
-                queue.dma_start(w1_sc_raw[32 * d:32 * d + 4, :].bitcast(I32).rearrange("r (a c) -> r a c", a=2),
-                                w1_scales[:, 4 * d:4 * d + 4, :].bitcast(I32).rearrange("a r c -> r a c"))
+        def move_scale_rows(a):
+            for r in range(4):
+                nc.sync.dma_start(v_planes[a][r:P:32, :].bitcast(I32), picked_sc[8 * r + a:P:32, :].bitcast(I32))
 
-        def load_w3_scales(queue, tag=""):
-            big["w3_sc"] = held([P, H], U8, "w3_sc_raw", tag)
-            nc.vector.memset(big["w3_sc"][:].bitcast(I32), 0)
-            for d in range(4):
-                queue.dma_start(big["w3_sc"][32 * d:32 * d + 8, :].bitcast(I32), w3_scales[:, 4 * d:4 * d + 4, :].bitcast(I32))
+        tab_w = [load_table(tab_words[a], "tab_w%d" % a) for a in range(2)]
+        load_tab2_scales(range(0, 2))
+        picked_sc = held([P, S], U8, "picked_sc")
+        nc.vector.tensor_copy(picked_sc[:], tab_sc[:].indirect(list8[:]))
+        move_scale_rows(0)
+        w2_raw = [load_w2(0)]
+        load_tab2_scales(range(2, 4))
+        move_scale_rows(1)
+        tab2_w = load_table(tab2_words[0], "tab2_w")
+        bias_sb = load_per_channel(bias, "bias_sb")
+        gain_sb = load_per_channel(gain, "gain_sb")
+        w2_raw.append(load_w2(1))
+        w3_raw = held([P, 2, H], I32, "w3_raw")
+        nc.sync.dma_start(w3_raw[:], w3_words.rearrange("a p c i -> p a (c i)").bitcast(I32))
+        w3_sc_raw = held([P, H], U8, "w3_sc_raw")
+        nc.vector.memset(w3_sc_raw[:].bitcast(I32), 0)
+        for d in range(4):
+            nc.sync.dma_start(w3_sc_raw[32 * d:32 * d + 8, :].bitcast(I32), w3_scales[:, 4 * d:4 * d + 4, :].bitcast(I32))
 
-        def load_tab2_scales(queue):
-            for d in range(4):
-                queue.dma_start(tab2_sc[32 * d:32 * d + 4, :].bitcast(I32), tab2_scales[0, 4 * d:4 * d + 4, :].bitcast(I32))
+        def order_words(target, source, per_line):
+            nc.vector.tensor_copy(target.rearrange("p (g t m i) -> p g m t i", g=4, t=4, i=per_line),
+                                  source.rearrange("p a (b m i t) -> p (a b) m t i", b=2, t=4, i=per_line))
 
-        def load_columns(queue):
-            for name, vector in (("bias", bias), ("gain", gain)):
-                big[name] = held([P, 2, 4], F32, name + "_sb")
-                queue.dma_start(big[name][:], vector.rearrange("(b p t) -> p b t", b=2, t=4))
+        def order_plane(target, source):
+            nc.vector.tensor_copy(target.rearrange("p (g t m) -> p g t m", t=4, m=P),
+                                  source.rearrange("p (g m t) -> p g t m", t=4, m=P))
 
-        def pick_scales(tag=""):
-            big["picked"] = held([P, S], U8, "picked_sc", tag)
-            nc.vector.tensor_copy(big["picked"][:], tab_sc[:].indirect(list8[:]))
-
-        def move_rows(queue, a, rows):
-            for r in rows:
-                queue.dma_start(v_planes[r:P:32, a * S:(a + 1) * S].bitcast(I32),
-                                big["picked"][8 * r + a:P:32, :].bitcast(I32))
-
-        def order_w1_planes(tag=""):
-            big["w1_planes"] = held([P, 2 * H], U8, "w1_planes", tag)
-            nc.vector.tensor_copy(big["w1_planes"][:].rearrange("p (g t m) -> p g t m", t=4, m=P),
-                                  w1_sc_raw[:].rearrange("p (g m t) -> p g t m", t=4, m=P))
-
-        def order_w1(tag=""):
-            big["w1_codes"] = held([P, 4 * H], U8, "w1_codes", tag)
-            nc.vector.tensor_copy(big["w1_codes"][:].bitcast(U16).rearrange("p (g t m i) -> p g m t i", g=4, t=4, i=8),
-                                  big["w1"][:].bitcast(U16).rearrange("p a (b m i t) -> p (a b) m t i", b=2, t=4, i=8))
+        w1_codes = held([P, 4 * H], U8, "w1_codes")
+        order_words(w1_codes[:].bitcast(U16), w1_raw[:].bitcast(U16), 8)
+        w1_planes = held([P, 2 * H], U8, "w1_planes")
+        order_plane(w1_planes[:], w1_sc_raw[:])
 
         w2_codes, w2_plane = {}, {}
 
-        def prepare_w2(b, tag="", cast=nc.scalar.copy):
-            grouped = held([P, 4 * N], BF16, "w2_grouped%d" % b, tag)
+        def quantise_w2(b, cast):
+            grouped = held([P, 4 * N], BF16, "w2_grouped%d" % b)
             cast(grouped[:].rearrange("p (t m j) -> p m t j", t=4, j=4),
-                           w2_raw[b][:].rearrange("p j (m t) -> p m t j", t=4))
+                 w2_raw[b][:].rearrange("p j (m t) -> p m t j", t=4))
             w2_codes[b] = held([P, N], U32, "w2_codes%d" % b)
             w2_plane[b] = held([P, N], U8, "w2_plane%d" % b)
             nc.vector.quantize_mx(w2_codes[b][:].bitcast(FP8X4), w2_plane[b][:], grouped[:])
 
-        picked = {}
+        def gather(window, offsets, h, dtype, name):
+            picked = held([P, N], dtype, name + str(h))
+            nc.vector.tensor_copy(picked[:], window.indirect(offsets[:, h * N // 16:(h + 1) * N // 16]))
+            return picked
 
-        def pick(a, h, tag=""):
-            picked[a, h] = held([P, N], U32, "picked%d%d" % (a, h), tag)
-            picks = list8 if a < 2 else list1
-            nc.vector.tensor_copy(picked[a, h][:], tab_w[a][:].bitcast(U32).indirect(picks[:, h * N // 16:(h + 1) * N // 16]))
-
-        def pick_tab2_scales(h, tag=""):
-            picked[3, h] = held([P, N], U8, "v2_plane%d" % h, tag)
-            nc.vector.tensor_copy(picked[3, h][:], tab2_sc[:].indirect(list1[:, h * N // 16:(h + 1) * N // 16]))
-
-        def order_w3(tag="", tag2=""):
-            big["w3_planes"] = held([P, H], U8, "w3_planes", tag2)
-            nc.vector.tensor_copy(big["w3_planes"][:].rearrange("p (g t m) -> p g t m", t=4, m=P),
-                                  big["w3_sc"][:].rearrange("p (g m t) -> p g t m", t=4, m=P))
-            big["w3_codes"] = held([P, 2 * H], U32, "w3_codes", tag)
-            for g in range(0, 4, 4):
-                nc.vector.tensor_copy(big["w3_codes"][:].rearrange("p (g t m i) -> p g m t i", t=4, m=P // 4, i=4)[:, g:g + 4, :, :, :],
-                                  big["w3"][:].bitcast(U32).rearrange("p a (b m i t) -> p (a b) m t i", b=2, i=4, t=4)[:, g:g + 4, :, :, :])
+        v_codes, v2_codes, v2_plane = {}, {}, {}
+        for h in range(2):
+            for a in range(2):
+                v_codes[h, a] = gather(tab_w[a][:].bitcast(U32), list8, h, U32, "v_codes%d" % a)
+            v2_plane[h] = gather(tab2_sc[:], list1, h, U8, "v2_plane")
+            if h == 0:
+                quantise_w2(0, nc.scalar.copy)
+            v2_codes[h] = gather(tab2_w[:].bitcast(U32), list1, h, U32, "v2_codes")
+        quantise_w2(1, nc.vector.tensor_copy)
 
         def load_passes(bank, h, b, t, stop):
             for a in range(2):
+                first = a * H + b * N + t * P
                 nc.tensor.matmul_mx(
                     bank[:],
-                    lhsT=big["w1_codes"][:, 2 * (a * H + b * N + t * P):2 * (a * H + b * N + (t + 1) * P)].bitcast(FP4X4),
-                    lhsT_scale=big["w1_planes"][:, a * H + b * N + t * P:a * H + b * N + (t + 1) * P],
-                    rhs=picked[a, h][:].bitcast(FP8X4),
-                    rhs_scale=v_planes[:, a * S + h * N:a * S + (h + 1) * N],
+                    lhsT=w1_codes[:, 2 * first:2 * (first + P)].bitcast(FP4X4), lhsT_scale=w1_planes[:, first:first + P],
+                    rhs=v_codes[h, a][:].bitcast(FP8X4), rhs_scale=v_planes[a][:, h * N:(h + 1) * N],
                     start=(a == 0), stop=(stop and a == 1))
 
         def weather_pass(bank, h, b, t, start):
             nc.tensor.matmul_mx(
                 bank[:],
                 lhsT=w2_codes[b][:, t * P:(t + 1) * P].bitcast(FP8X4), lhsT_scale=w2_plane[b][:, t * P:(t + 1) * P],
-                rhs=picked[2, h][:].bitcast(FP8X4), rhs_scale=picked[3, h][:], start=start, stop=True)
+                rhs=v2_codes[h][:].bitcast(FP8X4), rhs_scale=v2_plane[h][:], start=start, stop=True)
 
-        load_sb, h_codes, h_plane = {}, {}, {}
-
-        def keep_load(g):
-            h, b = GROUPS[g]
+        load_sb = {}
+        for h, b in GROUPS[:3]:
             for t in range(4):
-                bank = psum.tile([P, N], F32, name="sum_bank", bufs=5)
+                bank = psum.tile([P, N], F32, name="first_bank")
                 load_passes(bank, h, b, t, True)
                 load_sb[h, b, t] = held([P, N], F32, "load_sb%d%d%d" % (h, b, t))
                 nc.scalar.copy(load_sb[h, b, t][:], bank[:])
 
-        def first_stage(g):
-            h, b = GROUPS[g]
-            mode, pool_chunks = MODES[g]
-            stress = work.tile([P, 4, N], F32, name="stress", bufs=4)
-            flat = work.tile([P, 4, N], BF16, name="h_flat", bufs=4) if mode != "fused" else None
+        def stress_of(group, gain_on_scalar):
+            h, b = group
+            stress = held([P, 4, N], F32, "stress%d%d" % group)
+            scaled = held([P, 4, N], BF16, "scaled%d%d" % group) if gain_on_scalar else None
             for t in range(4):
-                column = big["bias"][:, b, t:t + 1]
-                if g == TWICE:
-                    bank = psum.tile([P, N], F32, name="sum_bank", bufs=5)
+                bank = psum.tile([P, N], F32, name="first_bank")
+                if group == LAST:
                     load_passes(bank, h, b, t, False)
                     weather_pass(bank, h, b, t, False)
-                    source = bank
+                    summed = bank
                 else:
-                    bank = psum.tile([P, N], F32, name="sum_bank", bufs=5)
                     weather_pass(bank, h, b, t, True)
-                    source = held([P, N], F32, "summed%d%d" % (g, t))
-                    nc.vector.tensor_tensor(source[:], bank[:], load_sb[h, b, t][:], ADD)
-                nc.scalar.activation(stress[:, t, :], source[:], SIGMOID, bias=column)
-                if mode == "pool":
-                    nc.gpsimd.tensor_scalar(flat[:, t, :], stress[:, t, :], big["gain"][:, b, t:t + 1], 0.0, MULT, ADD)
-                if mode == "act":
-                    nc.scalar.activation(flat[:, t, :], stress[:, t, :], COPY, scale=big["gain"][:, b, t:t + 1])
-            return stress, flat
+                    summed = held([P, N], F32, "summed%d%d%d" % (h, b, t))
+                    nc.vector.tensor_tensor(summed[:], bank[:], load_sb[h, b, t][:], ADD)
+                nc.scalar.activation(stress[:, t, :], summed[:], SIGMOID, bias=bias_sb[:, b, t:t + 1])
+                if gain_on_scalar:
+                    nc.scalar.activation(scaled[:, t, :], stress[:, t, :], COPY, scale=gain_sb[:, b, t:t + 1])
+            return scaled if gain_on_scalar else stress
 
-        def quantise_h(g, stress, flat):
-            h, b = GROUPS[g]
-            mode, on_scalar = MODES[g]
-            grouped = work.tile([P, 4 * N], BF16, name="h_grouped", align_bytes=64, bufs=3)
-            if mode == "fused":
-                gains = big["gain"][:, b, :].unsqueeze(1).unsqueeze(3).to_broadcast([P, N // 2, 4, 2])
-                nc.vector.tensor_tensor(grouped[:].rearrange("p (c i t) -> p c t i", i=2, t=4),
-                                        stress[:].rearrange("p t (c i) -> p c t i", i=2), gains, MULT)
-            else:
-                for k in range(on_scalar):
-                    cs = slice(k * 32, (k + 1) * 32)
-                    nc.scalar.copy(grouped[:].rearrange("p (c i t) -> p c t i", i=4, t=4)[:, cs, :, :],
-                                   flat[:].rearrange("p t (c i) -> p c t i", i=4)[:, cs, :, :])
-                if on_scalar < 4:
-                    cs = slice(on_scalar * 32, 128)
-                    nc.vector.tensor_copy(grouped[:].rearrange("p (c i t) -> p c t i", i=4, t=4)[:, cs, :, :],
-                                          flat[:].rearrange("p t (c i) -> p c t i", i=4)[:, cs, :, :])
-            h_codes[h, b] = held([P, N], U32, "h_codes%d%d" % (h, b))
-            h_plane[h, b] = held([P, N], U8, "h_plane%d%d" % (h, b))
-            nc.vector.quantize_mx(h_codes[h, b][:].bitcast(FP8X4), h_plane[h, b][:],
-                                  grouped[:])
+        def gain_and_weave(woven, stress, b):
+            gains = gain_sb[:, b, :].unsqueeze(1).unsqueeze(3).to_broadcast([P, N // 2, 4, 2])
+            nc.vector.tensor_tensor(woven.rearrange("p (c i t) -> p c t i", i=2, t=4),
+                                    stress.rearrange("p t (c i) -> p c t i", i=2), gains, MULT)
 
+        def weave(woven, scaled, copy, pieces):
+            target = woven.rearrange("p (c i t) -> p c t i", i=4, t=4)
+            source = scaled.rearrange("p t (c i) -> p c t i", i=4)
+            step = N // 4 // pieces
+            for c in range(0, N // 4, step):
+                copy(target[:, c:c + step, :, :], source[:, c:c + step, :, :])
 
-        out_view = out.rearrange("(b p t) j -> b t p j", b=2, t=4)
+        h_codes, h_plane = {}, {}
+
+        def quantise_h(group, fill):
+            woven = work.tile([P, 4 * N], BF16, name="woven", align_bytes=64, bufs=3)
+            fill(woven[:])
+            h_codes[group] = held([P, N], U32, "h_codes%d%d" % group)
+            h_plane[group] = held([P, N], U8, "h_plane%d%d" % group)
+            nc.vector.quantize_mx(h_codes[group][:].bitcast(FP8X4), h_plane[group][:], woven[:])
+
+        scaled_first = stress_of(GROUPS[0], True)
+        w3_planes = held([P, H], U8, "w3_planes")
+        order_plane(w3_planes[:], w3_sc_raw[:])
+        w3_codes = held([P, 2 * H], U32, "w3_codes")
+        order_words(w3_codes[:], w3_raw[:].bitcast(U32), 4)
+        stress_second = stress_of(GROUPS[1], False)
+        quantise_h(GROUPS[0], lambda woven: weave(woven, scaled_first[:], nc.scalar.copy, WEAVE_PIECES))
+        stress_third = stress_of(GROUPS[2], False)
+        quantise_h(GROUPS[1], lambda woven: gain_and_weave(woven, stress_second[:], GROUPS[1][1]))
+        quantise_h(GROUPS[2], lambda woven: gain_and_weave(woven, stress_third[:], GROUPS[2][1]))
+        scaled_last = stress_of(LAST, True)
+        quantise_h(LAST, lambda woven: weave(woven, scaled_last[:], nc.vector.tensor_copy, 1))
+
+        out_tiles = out.rearrange("(b p t) j -> b t p j", b=2, t=4)
 
         def mix_pass(bank, h, b, t, a):
-            cols = slice(b * N + t * P, b * N + (t + 1) * P)
+            first = b * N + t * P
             nc.tensor.matmul_mx(
                 bank[:],
-                lhsT=big["w3_codes"][:, a * H + cols.start:a * H + cols.stop].bitcast(FP8X4),
-                lhsT_scale=big["w3_planes"][4 * a:P, cols],
+                lhsT=w3_codes[:, a * H + first:a * H + first + P].bitcast(FP8X4),
+                lhsT_scale=w3_planes[4 * a:P, first:first + P],
                 rhs=h_codes[h, a][:].bitcast(FP8X4), rhs_scale=h_plane[h, a][:],
-                start=(a == 0 and GROUPS[TWICE] != (h, b)), stop=(a == 1))
+                start=(a == 0 and (h, b) != LAST), stop=(a == 1))
 
-        def open_tile(h, b, t, tag, bufs):
-            bank = psum.tile([P, N], F32, name=tag, bufs=bufs)
-            if GROUPS[TWICE] == (h, b):
+        def open_tile(h, b, t, ring):
+            bank = psum.tile([P, N], F32, name=ring)
+            if (h, b) == LAST:
                 load_passes(bank, h, b, t, False)
             mix_pass(bank, h, b, t, 0)
             return bank
@@ -239,61 +238,17 @@ def tile_list_fleet_ageing_kernel(tc, tab_words, tab_scales, offs, tab2_words, t
         def close_tile(bank, h, b, t):
             mix_pass(bank, h, b, t, 1)
             result = work.tile([P, N], F32, name="result", bufs=8)
-            if GROUPS[TWICE] == (h, b):
+            if (h, b) == LAST:
                 nc.scalar.copy(result[:], bank[:])
             else:
                 nc.vector.tensor_tensor(result[:], bank[:], load_sb[h, b, t][:], ADD)
-            nc.sync.dma_start(out_view[b, t, :, h * N:(h + 1) * N], result[:])
+            nc.sync.dma_start(out_tiles[b, t, :, h * N:(h + 1) * N], result[:])
 
-        def second_stage(h):
-            for b in range(2):
-                for t in range(4):
-                    close_tile(open_tile(h, b, t, "second_bank", 3), h, b, t)
-
-        last_tiles = [(b, t) for t in range(4) for b in range(2)]
-        last_tags = [("sum_bank", 5)] * 5 + [("second_bank", 3)] * 3
-
-        nc.scalar.activation(warm2[:], warm[:], SIGMOID)
-        load_w1_scales(nc.sync)
-        load_w1(nc.sync)
-        load_tab(0, nc.sync)
-        load_tab(1, nc.sync)
-        nc.sync.dma_start(list1[:], offs2)
-        load_tab2_scales(nc.gpsimd)
-        load_columns(nc.gpsimd)
-        pick_scales()
-        move_rows(nc.sync, 0, range(4))
-        move_rows(nc.sync, 1, range(1))
-        load_w2(0, nc.sync)
-        move_rows(nc.sync, 1, range(1, 4))
-        load_tab(2, nc.sync)
-        load_w2(1, nc.sync)
-        load_w3(nc.sync)
-        load_w3_scales(nc.sync)
-        order_w1()
-        order_w1_planes()
-        pick(0, 0)
-        pick(1, 0)
-        pick_tab2_scales(0)
-        prepare_w2(0, "", nc.vector.tensor_copy)
-        pick(2, 0)
-        pick(0, 1)
-        pick(1, 1)
-        pick_tab2_scales(1)
-        pick(2, 1)
-        keep_load(0)
-        keep_load(1)
-        keep_load(2)
-        prepare_w2(1, "", nc.scalar.copy)
-        first = first_stage(0)
-        order_w3()
-        second = first_stage(1)
-        quantise_h(0, *first)
-        third = first_stage(2)
-        quantise_h(1, *second)
-        quantise_h(2, *third)
-        quantise_h(3, *first_stage(3))
-        second_stage(0)
-        banks = [open_tile(1, b, t, tag, bufs) for (b, t), (tag, bufs) in zip(last_tiles, last_tags)]
-        for bank, (b, t) in zip(banks, last_tiles):
+        for b in range(2):
+            for t in range(4):
+                close_tile(open_tile(0, b, t, "second_bank"), 0, b, t)
+        tiles = [(b, t) for t in range(4) for b in range(2)]
+        rings = ["first_bank"] * RING + ["second_bank"] * RING
+        banks = [open_tile(1, b, t, ring) for (b, t), ring in zip(tiles, rings)]
+        for bank, (b, t) in zip(banks, tiles):
             close_tile(bank, 1, b, t)

@@ -22,6 +22,8 @@ P = 128
 N = 512
 GROUPS = ((0, 0), (0, 1), (1, 0), (1, 1))
 LAST = GROUPS[3]
+TAB2_SHIFT = 4
+W3_SHIFT = 8
 RING = 4
 WEAVE_PIECES = 4
 
@@ -49,8 +51,12 @@ def tile_list_fleet_ageing_kernel(tc, tab_words, tab_scales, offs, tab2_words, t
         w1_sc_raw = held([P, 2 * H], U8, "w1_sc_raw")
         tab2_sc = held([P, T], U8, "tab2_sc")
         v_planes = [held([P, S], U8, "v_plane%d" % a) for a in range(2)]
+        warm = held([P, 8], F32, "warm")
+        nc.vector.memset(warm[:], 0.0)
         for plane in (w1_sc_raw, tab2_sc, *v_planes):
             nc.vector.memset(plane[:].bitcast(I32), 0)
+        warmed = held([P, 8], F32, "warmed")
+        nc.scalar.activation(warmed[:], warm[:], SIGMOID)
 
         w1_raw = held([P, 2, H // 2], I32, "w1_raw")
         nc.sync.dma_start(w1_raw[:], w1_words.bitcast(I32).rearrange("a p c -> p a c"))
@@ -67,7 +73,7 @@ def tile_list_fleet_ageing_kernel(tc, tab_words, tab_scales, offs, tab2_words, t
 
         def load_tab2_scales(quadrants):
             for d in quadrants:
-                nc.sync.dma_start(tab2_sc[32 * d:32 * d + 4, :].bitcast(I32),
+                nc.sync.dma_start(tab2_sc[32 * d + TAB2_SHIFT:32 * d + TAB2_SHIFT + 4, :].bitcast(I32),
                                   tab2_scales[0, 4 * d:4 * d + 4, :].bitcast(I32))
 
         def load_w2(b):
@@ -101,7 +107,8 @@ def tile_list_fleet_ageing_kernel(tc, tab_words, tab_scales, offs, tab2_words, t
         w3_sc_raw = held([P, H], U8, "w3_sc_raw")
         nc.vector.memset(w3_sc_raw[:].bitcast(I32), 0)
         for d in range(4):
-            nc.sync.dma_start(w3_sc_raw[32 * d:32 * d + 8, :].bitcast(I32), w3_scales[:, 4 * d:4 * d + 4, :].bitcast(I32))
+            nc.sync.dma_start(w3_sc_raw[32 * d + W3_SHIFT:32 * d + W3_SHIFT + 8, :].bitcast(I32),
+                              w3_scales[:, 4 * d:4 * d + 4, :].bitcast(I32))
 
         def order_words(target, source, per_line):
             nc.vector.tensor_copy(target.rearrange("p (g t m i) -> p g m t i", g=4, t=4, i=per_line),
@@ -154,7 +161,7 @@ def tile_list_fleet_ageing_kernel(tc, tab_words, tab_scales, offs, tab2_words, t
             nc.tensor.matmul_mx(
                 bank[:],
                 lhsT=w2_codes[b][:, t * P:(t + 1) * P].bitcast(FP8X4), lhsT_scale=w2_plane[b][:, t * P:(t + 1) * P],
-                rhs=v2_codes[h][:].bitcast(FP8X4), rhs_scale=v2_plane[h][:], start=start, stop=True)
+                rhs=v2_codes[h][:].bitcast(FP8X4), rhs_scale=v2_plane[h][TAB2_SHIFT:P, :], start=start, stop=True)
 
         load_sb = {}
         for h, b in GROUPS[:3]:
@@ -224,7 +231,7 @@ def tile_list_fleet_ageing_kernel(tc, tab_words, tab_scales, offs, tab2_words, t
             nc.tensor.matmul_mx(
                 bank[:],
                 lhsT=w3_codes[:, a * H + first:a * H + first + P].bitcast(FP8X4),
-                lhsT_scale=w3_planes[4 * a:P, first:first + P],
+                lhsT_scale=w3_planes[W3_SHIFT + 4 * a:P, first:first + P],
                 rhs=h_codes[h, a][:].bitcast(FP8X4), rhs_scale=h_plane[h, a][:],
                 start=(a == 0 and (h, b) != LAST), stop=(a == 1))
 

@@ -20,242 +20,349 @@ COPY = mybir.ActivationFunctionType.Copy
 
 P = 128
 N = 512
-GROUPS = ((0, 0), (0, 1), (1, 0), (1, 1))
-LAST = GROUPS[3]
-TAB2_SHIFT = 4
+TAB2_SHIFT = 0
 W3_SHIFT = 8
-RING = 4
 WEAVE_PIECES = 4
+LOADS = "L1s TSs S1a T0s UUs T1s WUa GSs M0a M1s T2s S2s A0s BIs A1s GAs W3s S3s"
+STEPS = "O0 o0 g0 G0 L0 o1 O1 g1 G1 w0 p0 c0 C0 L1 L2 L3 S0 c1 C1 S1 p1 w1 S2 S3 x0 W0 Q0 W1 Q1 M0 W2 Q2 W3 Q3 M1 S4 S5 W4 Q4 W5 Q5 M2 M3 A5 A4 E0"
+RING = 4
+PLANES_ON = "VVP"
+W3_ON = "PPPP"
+CAST_ON = "PP"
+GAIN_WEAVE = ("SV", "SV", "SV", "SV", "SV", "SV")
+LOAD_RING = "1122"
+CAST_PIECES = 1
+STRESS_RING = "121111"
+UNITS = ((0, 512, 0), (0, 512, 1), (512, 256, 0), (512, 256, 1), (768, 256, 0), (768, 256, 1))
+TWICE = (4, 5)
+OUT_ON = "SV"
+MIX_RING = "222212"
+STAGE_BUFS = 1
 
 
 def tile_list_fleet_ageing_kernel(tc, tab_words, tab_scales, offs, tab2_words, tab2_scales, offs2,
-                                           w1_words, w1_scales, w2, bias, gain, w3_words, w3_scales, out):
+                                              w1_words, w1_scales, w2, bias, gain, w3_words, w3_scales, out):
     nc = tc.nc
+    queue = {"s": nc.sync, "a": nc.scalar, "g": nc.gpsimd}
+    copier = {"V": nc.vector.tensor_copy, "S": nc.scalar.copy, "P": nc.gpsimd.tensor_copy}
     with ExitStack() as ctx:
         lists = ctx.enter_context(tc.tile_pool(name="lists", bufs=1))
         keep = ctx.enter_context(tc.tile_pool(name="keep", bufs=1))
         work = ctx.enter_context(tc.tile_pool(name="work", bufs=1))
-        psum = ctx.enter_context(tc.psum_pool(name="psum", bufs=RING))
+        psum = ctx.enter_context(tc.psum_pool(name="psum", bufs=1))
 
         def held(shape, dtype, name):
             return keep.tile(shape, dtype, name=name, align_bytes=64)
 
+        def first_bank():
+            return psum.tile([P, N], F32, name="first_bank", bufs=RING)
+
+        def second_bank():
+            return psum.tile([P, N], F32, name="second_bank", bufs=8 - RING)
+
         list8 = lists.tile([P, S // 16], U16, name="list8")
-        nc.sync.dma_start(list8[:], offs)
-
-        tab_sc = held([P, T], U8, "tab_sc")
-        for a in range(2):
-            nc.sync.dma_start(tab_sc[a:P:2, :].bitcast(I32),
-                              tab_scales[a].bitcast(I32).unsqueeze(1).to_broadcast([16, 4, T // 4]))
-
-        w1_sc_raw = held([P, 2 * H], U8, "w1_sc_raw")
-        tab2_sc = held([P, T], U8, "tab2_sc")
-        v_planes = [held([P, S], U8, "v_plane%d" % a) for a in range(2)]
-        warm = held([P, 8], F32, "warm")
-        nc.vector.memset(warm[:], 0.0)
-        for plane in (w1_sc_raw, tab2_sc, *v_planes):
-            nc.vector.memset(plane[:].bitcast(I32), 0)
-        warmed = held([P, 8], F32, "warmed")
-        nc.scalar.activation(warmed[:], warm[:], SIGMOID)
-
-        w1_raw = held([P, 2, H // 2], I32, "w1_raw")
-        nc.sync.dma_start(w1_raw[:], w1_words.bitcast(I32).rearrange("a p c -> p a c"))
-        for d in range(4):
-            nc.sync.dma_start(w1_sc_raw[32 * d:32 * d + 4, :].bitcast(I32).rearrange("r (a c) -> r a c", a=2),
-                              w1_scales[:, 4 * d:4 * d + 4, :].bitcast(I32).rearrange("a r c -> r a c"))
         list1 = lists.tile([P, S // 16], U16, name="list1")
-        nc.sync.dma_start(list1[:], offs2)
-
-        def load_table(dram_pass, name):
-            window = held([P, T], I32, name)
-            nc.sync.dma_start(window[:], dram_pass.rearrange("p c i -> p (c i)").bitcast(I32))
-            return window
-
-        def load_tab2_scales(quadrants):
-            for d in quadrants:
-                nc.sync.dma_start(tab2_sc[32 * d + TAB2_SHIFT:32 * d + TAB2_SHIFT + 4, :].bitcast(I32),
-                                  tab2_scales[0, 4 * d:4 * d + 4, :].bitcast(I32))
-
-        def load_w2(b):
-            rows = held([P, 4, N], F32, "w2_raw%d" % b)
-            nc.sync.dma_start(rows[:], w2.rearrange("(p j) c -> p j c", j=4)[:, :, b * N:(b + 1) * N])
-            return rows
-
-        def load_per_channel(vector, name):
-            columns = held([P, 2, 4], F32, name)
-            nc.sync.dma_start(columns[:], vector.rearrange("(b p t) -> p b t", b=2, t=4))
-            return columns
-
-        def move_scale_rows(a):
-            for r in range(4):
-                nc.sync.dma_start(v_planes[a][r:P:32, :].bitcast(I32), picked_sc[8 * r + a:P:32, :].bitcast(I32))
-
-        tab_w = [load_table(tab_words[a], "tab_w%d" % a) for a in range(2)]
-        load_tab2_scales(range(0, 2))
-        picked_sc = held([P, S], U8, "picked_sc")
-        nc.vector.tensor_copy(picked_sc[:], tab_sc[:].indirect(list8[:]))
-        move_scale_rows(0)
-        w2_raw = [load_w2(0)]
-        load_tab2_scales(range(2, 4))
-        move_scale_rows(1)
-        tab2_w = load_table(tab2_words[0], "tab2_w")
-        bias_sb = load_per_channel(bias, "bias_sb")
-        gain_sb = load_per_channel(gain, "gain_sb")
-        w2_raw.append(load_w2(1))
-        w3_raw = held([P, 2, H], I32, "w3_raw")
-        nc.sync.dma_start(w3_raw[:], w3_words.rearrange("a p c i -> p a (c i)").bitcast(I32))
+        tab_sc = work.tile([P, T], U8, name="scale_window", align_bytes=64)
+        w1_sc_raw = held([P, 2 * H], U8, "w1_sc_raw")
+        v_planes = [held([P, S], U8, "v_plane%d" % a) for a in range(2)]
         w3_sc_raw = held([P, H], U8, "w3_sc_raw")
+        warm = held([P, 8], F32, "warm")
+        warmed = held([P, 8], F32, "warmed")
+        picked_sc = work.tile([P, S], U8, name="picked_first", align_bytes=64)
+        w1_raw = held([P, 2, N], I32, "w1_raw")
+        tab_w = [held([P, T], I32, "tab_w%d" % a) for a in range(2)]
+        tab2_w = held([P, T], I32, "tab2_w")
+        w2_raw = [held([P, 4, N], F32, "w2_raw%d" % b) for b in range(2)]
+        bias_sb = held([P, 2, 4], F32, "bias_sb")
+        gain_sb = held([P, 2, 4], F32, "gain_sb")
+        w3_raw = held([P, 2, H], I32, "w3_raw")
+
+        nc.sync.dma_start(list8[:], offs)
+        for plane in (tab_sc, w1_sc_raw, v_planes[1]):
+            nc.vector.memset(plane[:].bitcast(I32), 0)
+        nc.vector.memset(warm[:], 0.0)
         nc.vector.memset(w3_sc_raw[:].bitcast(I32), 0)
-        for d in range(4):
-            nc.sync.dma_start(w3_sc_raw[32 * d + W3_SHIFT:32 * d + W3_SHIFT + 8, :].bitcast(I32),
-                              w3_scales[:, 4 * d:4 * d + 4, :].bitcast(I32))
 
-        def order_words(target, source, per_line):
-            nc.vector.tensor_copy(target.rearrange("p (g t m i) -> p g m t i", g=4, t=4, i=per_line),
-                                  source.rearrange("p a (b m i t) -> p (a b) m t i", b=2, t=4, i=per_line))
+        def load_tab_scales(q):
+            for e in range(2):
+                q.dma_start(tab_sc[e:P:8, :].bitcast(I32), tab_scales[:, e:16:2, :].bitcast(I32).rearrange("a g c -> g a c"))
 
-        def order_plane(target, source):
-            nc.vector.tensor_copy(target.rearrange("p (g t m) -> p g t m", t=4, m=P),
-                                  source.rearrange("p (g m t) -> p g t m", t=4, m=P))
+        def load_w1(q):
+            q.dma_start(w1_raw[:], w1_words.bitcast(I32).rearrange("a p c -> p a c"))
 
-        w1_codes = held([P, 4 * H], U8, "w1_codes")
-        order_words(w1_codes[:].bitcast(U16), w1_raw[:].bitcast(U16), 8)
-        w1_planes = held([P, 2 * H], U8, "w1_planes")
-        order_plane(w1_planes[:], w1_sc_raw[:])
+        def load_w1_scales(q):
+            for d in range(4):
+                q.dma_start(w1_sc_raw[32 * d:32 * d + 4, :].bitcast(I32).rearrange("r (a c) -> r a c", a=2),
+                            w1_scales[:, 4 * d:4 * d + 4, :].bitcast(I32).rearrange("a r c -> r a c"))
 
-        w2_codes, w2_plane = {}, {}
+        def load_table(q, window, dram_pass):
+            q.dma_start(window[:], dram_pass.rearrange("p c i -> p (c i)").bitcast(I32))
 
-        def quantise_w2(b, cast):
-            grouped = held([P, 4 * N], BF16, "w2_grouped%d" % b)
-            cast(grouped[:].rearrange("p (t m j) -> p m t j", t=4, j=4),
-                 w2_raw[b][:].rearrange("p j (m t) -> p m t j", t=4))
+        late = {}
+
+        def load_tab2_scales(q):
+            tab2_sc = work.tile([P, T], U8, name="scale_window", align_bytes=64)
+            late["tab2_sc"] = tab2_sc
+            for r in range(4):
+                q.dma_start(tab2_sc[r:P:4, :].bitcast(I32),
+                            tab2_scales[0, r:16:4, :].bitcast(I32).unsqueeze(1).to_broadcast([4, 8, T // 4]))
+
+        def load_w2(q, b):
+            q.dma_start(w2_raw[b][:], w2.rearrange("(p j) c -> p j c", j=4)[:, :, b * N:(b + 1) * N])
+
+        def load_per_channel(q, columns, vector):
+            q.dma_start(columns[:], vector.rearrange("(b p t) -> p b t", b=2, t=4))
+
+        def load_w3_scales(q):
+            for d in range(4):
+                q.dma_start(w3_sc_raw[32 * d + W3_SHIFT:32 * d + W3_SHIFT + 8, :].bitcast(I32),
+                            w3_scales[:, 4 * d:4 * d + 4, :].bitcast(I32))
+
+        def move_scale_rows(q, a):
+            if a == 0:
+                nc.vector.tensor_copy(v_planes[0][:].bitcast(U32), picked_sc[:].bitcast(U32))
+            for r in range(2 if a == 0 else 0, 4):
+                q.dma_start(v_planes[a][r:P:32, :].bitcast(I32),
+                            picked_sc[16 * (r // 2) + 8 * a + r % 2:P:32, :].bitcast(I32))
+
+        loads = {
+            "TS": load_tab_scales, "S1": load_w1_scales, "S2": load_tab2_scales, "S3": load_w3_scales,
+            "T0": lambda q: load_table(q, tab_w[0], tab_words[0]), "T1": lambda q: load_table(q, tab_w[1], tab_words[1]),
+            "T2": lambda q: load_table(q, tab2_w, tab2_words[0]),
+            "UU": load_w1,
+            "A0": lambda q: load_w2(q, 0), "A1": lambda q: load_w2(q, 1),
+            "L1": lambda q: nc.sync.dma_start(list1[:], offs2),
+            "BI": lambda q: load_per_channel(q, bias_sb, bias), "GA": lambda q: load_per_channel(q, gain_sb, gain),
+            "W3": lambda q: q.dma_start(w3_raw[:], w3_words.rearrange("a p c i -> p a (c i)").bitcast(I32)),
+            "WU": lambda q: nc.scalar.activation(warmed[:], warm[:], SIGMOID),
+            "GS": lambda q: nc.vector.tensor_copy(picked_sc[:], tab_sc[:].indirect(list8[:])),
+            "M0": lambda q: move_scale_rows(q, 0), "M1": lambda q: move_scale_rows(q, 1),
+        }
+        for word in LOADS.split():
+            loads[word[:2]](queue[word[2]])
+
+        def order_words(copy, target, source, per_line):
+            copy(target.rearrange("p g (t m i) -> p g m t i", t=4, i=per_line),
+                 source.rearrange("p g (m i t) -> p g m t i", t=4, i=per_line))
+
+        def order_plane(copy, target, source):
+            copy(target.rearrange("p g (t m) -> p g t m", t=4), source.rearrange("p g (m t) -> p g t m", t=4))
+
+        w1_codes, w1_planes = {}, {}
+
+        def order_w1_words(b):
+            w1_codes[b] = held([P, 2, 2 * N], U8, "w1_codes%d" % b)
+            order_words(nc.vector.tensor_copy, w1_codes[b][:].bitcast(U16), w1_raw[:].bitcast(U16)[:, :, b * N:(b + 1) * N], 8)
+
+        def order_w1_plane(b):
+            w1_planes[b] = held([P, 2, N], U8, "w1_planes%d" % b)
+            order_plane(copier[PLANES_ON[b]], w1_planes[b][:],
+                        w1_sc_raw[:].rearrange("p (a c) -> p a c", a=2)[:, :, b * N:(b + 1) * N])
+
+        w3_planes = held([P, H], U8, "w3_planes")
+
+        def order_w3():
+            w3_codes = work.tile([P, 2 * H], U32, name="weight_stage", align_bytes=64, bufs=STAGE_BUFS)
+            late["w3_codes"] = w3_codes
+            for g in range(4):
+                order_words(copier[W3_ON[g]], w3_codes[:, g * N:(g + 1) * N].unsqueeze(1),
+                            w3_raw[:, g // 2, (g % 2) * N:(g % 2 + 1) * N].bitcast(U32).unsqueeze(1), 4)
+            order_plane(copier[PLANES_ON[2]], w3_planes[:].rearrange("p (g c) -> p g c", g=2),
+                        w3_sc_raw[:].rearrange("p (g c) -> p g c", g=2))
+
+        w2_grouped, w2_codes, w2_plane = {}, {}, {}
+
+        def cast_w2(b):
+            w2_grouped[b] = work.tile([P, 4 * N], BF16, name="weight_stage", align_bytes=64, bufs=STAGE_BUFS)
+            target = w2_grouped[b][:].rearrange("p (t m j) -> p m t j", t=4, j=4)
+            source = w2_raw[b][:].rearrange("p j (m t) -> p m t j", t=4)
+            step = P // CAST_PIECES
+            for m in range(0, P, step):
+                copier[CAST_ON[b]](target[:, m:m + step, :, :], source[:, m:m + step, :, :])
+
+        def quantise_w2(b):
             w2_codes[b] = held([P, N], U32, "w2_codes%d" % b)
             w2_plane[b] = held([P, N], U8, "w2_plane%d" % b)
-            nc.vector.quantize_mx(w2_codes[b][:].bitcast(FP8X4), w2_plane[b][:], grouped[:])
+            nc.vector.quantize_mx(w2_codes[b][:].bitcast(FP8X4), w2_plane[b][:], w2_grouped[b][:])
 
         def gather(window, offsets, h, dtype, name):
-            picked = held([P, N], dtype, name + str(h))
+            if name + str(h) == "v_codes01":
+                picked = work.tile([P, N], dtype, name="picked_first", align_bytes=64)
+            else:
+                picked = held([P, N], dtype, name + str(h))
             nc.vector.tensor_copy(picked[:], window.indirect(offsets[:, h * N // 16:(h + 1) * N // 16]))
             return picked
 
         v_codes, v2_codes, v2_plane = {}, {}, {}
-        for h in range(2):
-            for a in range(2):
-                v_codes[h, a] = gather(tab_w[a][:].bitcast(U32), list8, h, U32, "v_codes%d" % a)
-            v2_plane[h] = gather(tab2_sc[:], list1, h, U8, "v2_plane")
-            if h == 0:
-                quantise_w2(0, nc.scalar.copy)
+
+        def gather_load(h, a):
+            v_codes[h, a] = gather(tab_w[a][:].bitcast(U32), list8, h, U32, "v_codes%d" % a)
+
+        def gather_weather_plane(h):
+            v2_plane[h] = gather(late["tab2_sc"][:], list1, h, U8, "v2_plane")
+
+        def gather_weather(h):
             v2_codes[h] = gather(tab2_w[:].bitcast(U32), list1, h, U32, "v2_codes")
-        quantise_w2(1, nc.vector.tensor_copy)
 
-        def load_passes(bank, h, b, t, stop):
-            for a in range(2):
-                first = a * H + b * N + t * P
+        def unit_tiles(g):
+            width = UNITS[g][1]
+            per_bank = N // width
+            return [[(t0 + i, slice(i * width, (i + 1) * width)) for i in range(per_bank)] for t0 in range(0, 4, per_bank)]
+
+        def load_passes(target, g, t, start, stop):
+            first, width, b = UNITS[g]
+            h, step = first // N, (N if width == N else P)
+            pieces = [(a, c) for c in range(0, width, step) for a in range(2)]
+            for a, c in pieces:
                 nc.tensor.matmul_mx(
-                    bank[:],
-                    lhsT=w1_codes[:, 2 * first:2 * (first + P)].bitcast(FP4X4), lhsT_scale=w1_planes[:, first:first + P],
-                    rhs=v_codes[h, a][:].bitcast(FP8X4), rhs_scale=v_planes[a][:, h * N:(h + 1) * N],
-                    start=(a == 0), stop=(stop and a == 1))
+                    target[:, c:c + step],
+                    lhsT=w1_codes[b][:, a, 2 * t * P:2 * (t + 1) * P].bitcast(FP4X4),
+                    lhsT_scale=w1_planes[b][:, a, t * P:(t + 1) * P],
+                    rhs=v_codes[h, a][:, first % N + c:first % N + c + step].bitcast(FP8X4),
+                    rhs_scale=v_planes[a][:, first + c:first + c + step],
+                    start=(start and (a, c) == pieces[0]), stop=(stop and (a, c) == pieces[-1]))
 
-        def weather_pass(bank, h, b, t, start):
+        def weather_pass(target, g, t, start):
+            first, width, b = UNITS[g]
+            h, c = first // N, first % N
             nc.tensor.matmul_mx(
-                bank[:],
+                target,
                 lhsT=w2_codes[b][:, t * P:(t + 1) * P].bitcast(FP8X4), lhsT_scale=w2_plane[b][:, t * P:(t + 1) * P],
-                rhs=v2_codes[h][:].bitcast(FP8X4), rhs_scale=v2_plane[h][TAB2_SHIFT:P, :], start=start, stop=True)
+                rhs=v2_codes[h][:, c:c + width].bitcast(FP8X4), rhs_scale=v2_plane[h][:, c:c + width],
+                start=start, stop=True)
+
+        def ring(which):
+            return first_bank() if which == "1" else second_bank()
 
         load_sb = {}
-        for h, b in GROUPS[:3]:
-            for t in range(4):
-                bank = psum.tile([P, N], F32, name="first_bank")
-                load_passes(bank, h, b, t, True)
-                load_sb[h, b, t] = held([P, N], F32, "load_sb%d%d%d" % (h, b, t))
-                nc.scalar.copy(load_sb[h, b, t][:], bank[:])
 
-        def stress_of(group, gain_on_scalar):
-            h, b = group
-            stress = held([P, 4, N], F32, "stress%d%d" % group)
-            scaled = held([P, 4, N], BF16, "scaled%d%d" % group) if gain_on_scalar else None
-            for t in range(4):
-                bank = psum.tile([P, N], F32, name="first_bank")
-                if group == LAST:
-                    load_passes(bank, h, b, t, False)
-                    weather_pass(bank, h, b, t, False)
-                    summed = bank
-                else:
-                    weather_pass(bank, h, b, t, True)
-                    summed = held([P, N], F32, "summed%d%d%d" % (h, b, t))
-                    nc.vector.tensor_tensor(summed[:], bank[:], load_sb[h, b, t][:], ADD)
-                nc.scalar.activation(stress[:, t, :], summed[:], SIGMOID, bias=bias_sb[:, b, t:t + 1])
-                if gain_on_scalar:
-                    nc.scalar.activation(scaled[:, t, :], stress[:, t, :], COPY, scale=gain_sb[:, b, t:t + 1])
-            return scaled if gain_on_scalar else stress
+        def load_group(g):
+            for k, tiles in enumerate(unit_tiles(g)):
+                bank = ring(LOAD_RING[g])
+                for t, cols in tiles:
+                    load_passes(bank[:, cols], g, t, True, True)
+                load_sb[g, k] = held([P, N], F32, "load_sb%d%d" % (g, k))
+                nc.scalar.copy(load_sb[g, k][:], bank[:])
 
-        def gain_and_weave(woven, stress, b):
-            gains = gain_sb[:, b, :].unsqueeze(1).unsqueeze(3).to_broadcast([P, N // 2, 4, 2])
-            nc.vector.tensor_tensor(woven.rearrange("p (c i t) -> p c t i", i=2, t=4),
-                                    stress.rearrange("p t (c i) -> p c t i", i=2), gains, MULT)
+        made = {}
 
-        def weave(woven, scaled, copy, pieces):
-            target = woven.rearrange("p (c i t) -> p c t i", i=4, t=4)
-            source = scaled.rearrange("p t (c i) -> p c t i", i=4)
-            step = N // 4 // pieces
-            for c in range(0, N // 4, step):
-                copy(target[:, c:c + step, :, :], source[:, c:c + step, :, :])
+        def stress_of(g):
+            first, width, b = UNITS[g]
+            how = GAIN_WEAVE[g]
+            stress = work.tile([P, 4, width], F32, name="stress", bufs=3)
+            scaled = work.tile([P, 4, width], BF16, name="scaled", bufs=3) if how != "V" else None
+            for k, tiles in enumerate(unit_tiles(g)):
+                bank = ring(STRESS_RING[g])
+                for t, cols in tiles:
+                    if g in TWICE:
+                        load_passes(bank[:, cols], g, t, True, False)
+                    weather_pass(bank[:, cols], g, t, g not in TWICE)
+                summed = bank
+                if g not in TWICE:
+                    summed = work.tile([P, N], F32, name="summed", bufs=8)
+                    nc.vector.tensor_tensor(summed[:], bank[:], load_sb[g, k][:], ADD)
+                for t, cols in tiles:
+                    nc.scalar.activation(stress[:, t, :], summed[:, cols], SIGMOID, bias=bias_sb[:, b, t:t + 1])
+                for t, cols in tiles:
+                    column = gain_sb[:, b, t:t + 1]
+                    if how[0] == "S":
+                        nc.scalar.activation(scaled[:, t, :], stress[:, t, :], COPY, scale=column)
+                    if how[0] == "P":
+                        nc.gpsimd.tensor_scalar(scaled[:, t, :], stress[:, t, :], column, 0.0, MULT, ADD)
+                    if how[0] == "W":
+                        nc.vector.tensor_scalar(scaled[:, t, :], stress[:, t, :], column, None, MULT)
+            made[g] = stress if how == "V" else scaled
 
-        h_codes, h_plane = {}, {}
+        woven, h_codes, h_plane = {}, {}, {}
 
-        def quantise_h(group, fill):
-            woven = work.tile([P, 4 * N], BF16, name="woven", align_bytes=64, bufs=3)
-            fill(woven[:])
-            h_codes[group] = held([P, N], U32, "h_codes%d%d" % group)
-            h_plane[group] = held([P, N], U8, "h_plane%d%d" % group)
-            nc.vector.quantize_mx(h_codes[group][:].bitcast(FP8X4), h_plane[group][:], woven[:])
+        def weave(g):
+            first, width, b = UNITS[g]
+            how = GAIN_WEAVE[g]
+            woven[g] = work.tile([P, 4 * width], BF16, name="woven", align_bytes=64, bufs=3)
+            if how == "V":
+                gains = gain_sb[:, b, :].unsqueeze(1).unsqueeze(3).to_broadcast([P, width // 2, 4, 2])
+                nc.vector.tensor_tensor(woven[g][:].rearrange("p (c i t) -> p c t i", i=2, t=4),
+                                        made[g][:].rearrange("p t (c i) -> p c t i", i=2), gains, MULT)
+                return
+            target = woven[g][:].rearrange("p (c i t) -> p c t i", i=4, t=4)
+            source = made[g][:].rearrange("p t (c i) -> p c t i", i=4)
+            step = width // 4 if how[1] == "V" else 32
+            for c in range(0, width // 4, step):
+                copier[how[1]](target[:, c:c + step, :, :], source[:, c:c + step, :, :])
 
-        scaled_first = stress_of(GROUPS[0], True)
-        w3_planes = held([P, H], U8, "w3_planes")
-        order_plane(w3_planes[:], w3_sc_raw[:])
-        w3_codes = held([P, 2 * H], U32, "w3_codes")
-        order_words(w3_codes[:], w3_raw[:].bitcast(U32), 4)
-        stress_second = stress_of(GROUPS[1], False)
-        quantise_h(GROUPS[0], lambda woven: weave(woven, scaled_first[:], nc.scalar.copy, WEAVE_PIECES))
-        stress_third = stress_of(GROUPS[2], False)
-        quantise_h(GROUPS[1], lambda woven: gain_and_weave(woven, stress_second[:], GROUPS[1][1]))
-        quantise_h(GROUPS[2], lambda woven: gain_and_weave(woven, stress_third[:], GROUPS[2][1]))
-        scaled_last = stress_of(LAST, True)
-        quantise_h(LAST, lambda woven: weave(woven, scaled_last[:], nc.vector.tensor_copy, 1))
+        def quantise_h(g):
+            width = UNITS[g][1]
+            h_codes[g] = held([P, width], U32, "h_codes%d" % g)
+            h_plane[g] = held([P, width], U8, "h_plane%d" % g)
+            nc.vector.quantize_mx(h_codes[g][:].bitcast(FP8X4), h_plane[g][:], woven[g][:])
 
-        out_tiles = out.rearrange("(b p t) j -> b t p j", b=2, t=4)
+        out_rows = out.rearrange("(b p t) j -> b p t j", b=2, t=4)
 
-        def mix_pass(bank, h, b, t, a):
+        def mix_pass(target, g, t, a):
+            b = UNITS[g][2]
             first = b * N + t * P
+            source = g - b + a
             nc.tensor.matmul_mx(
-                bank[:],
-                lhsT=w3_codes[:, a * H + first:a * H + first + P].bitcast(FP8X4),
+                target,
+                lhsT=late["w3_codes"][:, a * H + first:a * H + first + P].bitcast(FP8X4),
                 lhsT_scale=w3_planes[W3_SHIFT + 4 * a:P, first:first + P],
-                rhs=h_codes[h, a][:].bitcast(FP8X4), rhs_scale=h_plane[h, a][:],
-                start=(a == 0 and (h, b) != LAST), stop=(a == 1))
+                rhs=h_codes[source][:].bitcast(FP8X4), rhs_scale=h_plane[source][:],
+                start=(a == 0 and g not in TWICE), stop=(a == 1))
 
-        def open_tile(h, b, t, ring):
-            bank = psum.tile([P, N], F32, name=ring)
-            if (h, b) == LAST:
-                load_passes(bank, h, b, t, False)
-            mix_pass(bank, h, b, t, 0)
-            return bank
+        def open_tile(target, g, t):
+            if g in TWICE:
+                load_passes(target, g, t, True, False)
+            mix_pass(target, g, t, 0)
 
-        def close_tile(bank, h, b, t):
-            mix_pass(bank, h, b, t, 1)
+        opened = {}
+
+        def open_unit(g):
+            for k, tiles in enumerate(unit_tiles(g)):
+                opened[g, k] = ring(MIX_RING[g])
+                t, cols = tiles[0]
+                open_tile(opened[g, k][:, cols], g, t)
+
+        def close_bank(g, k):
+            first, width, b = UNITS[g]
+            tiles = unit_tiles(g)[k]
+            ahead = (g, k) in opened
+            bank = opened[g, k] if ahead else ring(MIX_RING[g])
+            for i, (t, cols) in enumerate(tiles):
+                if i > 0 or not ahead:
+                    open_tile(bank[:, cols], g, t)
+                mix_pass(bank[:, cols], g, t, 1)
             result = work.tile([P, N], F32, name="result", bufs=8)
-            if (h, b) == LAST:
-                nc.scalar.copy(result[:], bank[:])
+            if g in TWICE:
+                copier[OUT_ON[(2 * g + k) % len(OUT_ON)]](result[:], bank[:])
             else:
-                nc.vector.tensor_tensor(result[:], bank[:], load_sb[h, b, t][:], ADD)
-            nc.sync.dma_start(out_tiles[b, t, :, h * N:(h + 1) * N], result[:])
+                nc.vector.tensor_tensor(result[:], bank[:], load_sb[g, k][:], ADD)
+            t0 = tiles[0][0]
+            nc.sync.dma_start(out_rows[b, :, t0:t0 + len(tiles), first:first + width],
+                              result[:].rearrange("p (t j) -> p t j", j=width))
 
-        for b in range(2):
+        def open_last(g):
             for t in range(4):
-                close_tile(open_tile(0, b, t, "second_bank"), 0, b, t)
-        tiles = [(b, t) for t in range(4) for b in range(2)]
-        rings = ["first_bank"] * RING + ["second_bank"] * RING
-        banks = [open_tile(1, b, t, ring) for (b, t), ring in zip(tiles, rings)]
-        for bank, (b, t) in zip(banks, tiles):
-            close_tile(bank, 1, b, t)
+                opened[g, t] = ring(MIX_RING[g])
+                open_tile(opened[g, t][:, 0:UNITS[g][1]], g, t)
+
+        def close_last(unused):
+            for pair in range(2):
+                for g in TWICE:
+                    first, width, b = UNITS[g]
+                    result = work.tile([P, 2, width], F32, name="result", bufs=8)
+                    for i in range(2):
+                        t = 2 * pair + i
+                        mix_pass(opened[g, t][:, 0:width], g, t, 1)
+                        copier[OUT_ON[b]](result[:, i, :], opened[g, t][:, 0:width])
+                    nc.sync.dma_start(out_rows[b, :, 2 * pair:2 * pair + 2, first:first + width], result[:])
+
+        def mix_unit(g):
+            for k in range(len(unit_tiles(g))):
+                close_bank(g, k)
+
+        steps = {"g": lambda i: gather_load(i, 0), "G": lambda i: gather_load(i, 1), "p": gather_weather_plane,
+                 "w": gather_weather, "o": order_w1_words, "O": order_w1_plane, "x": lambda i: order_w3(),
+                 "c": cast_w2, "C": quantise_w2, "L": load_group, "S": stress_of, "W": weave, "Q": quantise_h,
+                 "M": mix_unit, "A": open_last, "E": close_last}
+        for word in STEPS.split():
+            steps[word[0]](int(word[1]))

@@ -23,21 +23,22 @@ N = 512
 TAB2_SHIFT = 0
 W3_SHIFT = 8
 WEAVE_PIECES = 4
-LOADS = "L1s TSs S1a T0s UUs T1s WUa GSs M0a M1s T2s S2s A0s BIs A1s GAs W3s S3s"
-STEPS = "O0 o0 g0 G0 L0 o1 O1 g1 G1 w0 p0 c0 C0 L1 L2 L3 S0 c1 C1 S1 p1 w1 S2 S3 x0 W0 Q0 W1 Q1 M0 W2 Q2 W3 Q3 M1 S4 S5 W4 Q4 W5 Q5 M2 M3 A5 A4 E0"
+LOADS = "L1s TSs S1a T0s UUs T1s WUa GSs M0a M1s A0s S2s T2s BIs A1s GAs W3s S3s"
+STEPS = "O0 o0 g0 G0 L0 o1 O1 g1 G1 c0 C0 p0 w0 L1 L4 L5 S0 c1 C1 S1 p1 w1 S2 S3 p2 w2 W0 Q0 x0 W1 Q1 S4 S5 W2 Q2 W3 Q3 W4 Q4 W5 Q5 M0 M1 B2 B3 M2 M3 B4 B5 M4 M5"
 RING = 4
-PLANES_ON = "VVP"
+PLANES_ON = "VVV"
 W3_ON = "PPPP"
-CAST_ON = "PP"
+CAST_ON = "VP"
 GAIN_WEAVE = ("SV", "SV", "SV", "SV", "SV", "SV")
-LOAD_RING = "1122"
-CAST_PIECES = 1
-STRESS_RING = "121111"
+LOAD_RING = "111111"
+CAST_PIECES = (1, 1)
+STRESS_RING = "212211"
 UNITS = ((0, 512, 0), (0, 512, 1), (512, 256, 0), (512, 256, 1), (768, 256, 0), (768, 256, 1))
-TWICE = (4, 5)
-OUT_ON = "SV"
-MIX_RING = "222212"
+TWICE = (2, 3)
+OUT_ON = "S"
+MIX_RING = "112211"
 STAGE_BUFS = 1
+HOLDS = "g1:picked_first p1:first_sum0 w1:w2_raw1 p2:first_sum1"
 
 
 def tile_list_fleet_ageing_kernel(tc, tab_words, tab_scales, offs, tab2_words, tab2_scales, offs2,
@@ -72,7 +73,7 @@ def tile_list_fleet_ageing_kernel(tc, tab_words, tab_scales, offs, tab2_words, t
         w1_raw = held([P, 2, N], I32, "w1_raw")
         tab_w = [held([P, T], I32, "tab_w%d" % a) for a in range(2)]
         tab2_w = held([P, T], I32, "tab2_w")
-        w2_raw = [held([P, 4, N], F32, "w2_raw%d" % b) for b in range(2)]
+        w2_raw = [work.tile([P, 4, N], F32, name="w2_raw%d" % b, align_bytes=64) for b in range(2)]
         bias_sb = held([P, 2, 4], F32, "bias_sb")
         gain_sb = held([P, 2, 4], F32, "gain_sb")
         w3_raw = held([P, 2, H], I32, "w3_raw")
@@ -173,36 +174,39 @@ def tile_list_fleet_ageing_kernel(tc, tab_words, tab_scales, offs, tab2_words, t
         w2_grouped, w2_codes, w2_plane = {}, {}, {}
 
         def cast_w2(b):
-            w2_grouped[b] = work.tile([P, 4 * N], BF16, name="weight_stage", align_bytes=64, bufs=STAGE_BUFS)
-            target = w2_grouped[b][:].rearrange("p (t m j) -> p m t j", t=4, j=4)
             source = w2_raw[b][:].rearrange("p j (m t) -> p m t j", t=4)
-            step = P // CAST_PIECES
-            for m in range(0, P, step):
-                copier[CAST_ON[b]](target[:, m:m + step, :, :], source[:, m:m + step, :, :])
+            step = 4 // CAST_PIECES[b]
+            for t in range(0, 4, step):
+                w2_grouped[b, t] = work.tile([P, step * N], BF16, name="weight_stage", align_bytes=64, bufs=STAGE_BUFS)
+                copier[CAST_ON[b]](w2_grouped[b, t][:].rearrange("p (t m j) -> p m t j", t=step, j=4), source[:, :, t:t + step, :])
 
         def quantise_w2(b):
-            w2_codes[b] = held([P, N], U32, "w2_codes%d" % b)
-            w2_plane[b] = held([P, N], U8, "w2_plane%d" % b)
-            nc.vector.quantize_mx(w2_codes[b][:].bitcast(FP8X4), w2_plane[b][:], w2_grouped[b][:])
+            step = 4 // CAST_PIECES[b]
+            for t in range(0, 4, step):
+                codes = held([P, step * P], U32, "w2_codes%d%d" % (b, t))
+                plane = held([P, step * P], U8, "w2_plane%d%d" % (b, t))
+                nc.vector.quantize_mx(codes[:].bitcast(FP8X4), plane[:], w2_grouped[b, t][:])
+                for i in range(step):
+                    w2_codes[b, t + i] = codes[:, i * P:(i + 1) * P]
+                    w2_plane[b, t + i] = plane[:, i * P:(i + 1) * P]
 
-        def gather(window, offsets, h, dtype, name):
-            if name + str(h) == "v_codes01":
-                picked = work.tile([P, N], dtype, name="picked_first", align_bytes=64)
-            else:
-                picked = held([P, N], dtype, name + str(h))
-            nc.vector.tensor_copy(picked[:], window.indirect(offsets[:, h * N // 16:(h + 1) * N // 16]))
+        holds = dict(word.split(":") for word in HOLDS.split())
+
+        def gather(window, offsets, first, width, dtype, name):
+            picked = work.tile([P, width], dtype, name=holds.get(name, name), align_bytes=64)
+            nc.vector.tensor_copy(picked[:], window.indirect(offsets[:, first // 16:(first + width) // 16]))
             return picked
 
         v_codes, v2_codes, v2_plane = {}, {}, {}
 
         def gather_load(h, a):
-            v_codes[h, a] = gather(tab_w[a][:].bitcast(U32), list8, h, U32, "v_codes%d" % a)
+            v_codes[h, a] = gather(tab_w[a][:].bitcast(U32), list8, h * N, N, U32, "gG"[a] + str(h))
 
-        def gather_weather_plane(h):
-            v2_plane[h] = gather(late["tab2_sc"][:], list1, h, U8, "v2_plane")
+        def gather_weather_plane(c):
+            v2_plane[c] = gather(late["tab2_sc"][:], list1, UNITS[2 * c][0], UNITS[2 * c][1], U8, "p%d" % c)
 
-        def gather_weather(h):
-            v2_codes[h] = gather(tab2_w[:].bitcast(U32), list1, h, U32, "v2_codes")
+        def gather_weather(c):
+            v2_codes[c] = gather(tab2_w[:].bitcast(U32), list1, UNITS[2 * c][0], UNITS[2 * c][1], U32, "w%d" % c)
 
         def unit_tiles(g):
             width = UNITS[g][1]
@@ -223,12 +227,11 @@ def tile_list_fleet_ageing_kernel(tc, tab_words, tab_scales, offs, tab2_words, t
                     start=(start and (a, c) == pieces[0]), stop=(stop and (a, c) == pieces[-1]))
 
         def weather_pass(target, g, t, start):
-            first, width, b = UNITS[g]
-            h, c = first // N, first % N
+            b = UNITS[g][2]
             nc.tensor.matmul_mx(
                 target,
-                lhsT=w2_codes[b][:, t * P:(t + 1) * P].bitcast(FP8X4), lhsT_scale=w2_plane[b][:, t * P:(t + 1) * P],
-                rhs=v2_codes[h][:, c:c + width].bitcast(FP8X4), rhs_scale=v2_plane[h][:, c:c + width],
+                lhsT=w2_codes[b, t].bitcast(FP8X4), lhsT_scale=w2_plane[b, t],
+                rhs=v2_codes[g // 2][:].bitcast(FP8X4), rhs_scale=v2_plane[g // 2][:],
                 start=start, stop=True)
 
         def ring(which):
@@ -259,7 +262,10 @@ def tile_list_fleet_ageing_kernel(tc, tab_words, tab_scales, offs, tab2_words, t
                     weather_pass(bank[:, cols], g, t, g not in TWICE)
                 summed = bank
                 if g not in TWICE:
-                    summed = work.tile([P, N], F32, name="summed", bufs=8)
+                    if g == 0 and k < 2:
+                        summed = work.tile([P, N], F32, name="first_sum%d" % k, align_bytes=64)
+                    else:
+                        summed = work.tile([P, N], F32, name="summed", bufs=6)
                     nc.vector.tensor_tensor(summed[:], bank[:], load_sb[g, k][:], ADD)
                 for t, cols in tiles:
                     nc.scalar.activation(stress[:, t, :], summed[:, cols], SIGMOID, bias=bias_sb[:, b, t:t + 1])
@@ -333,7 +339,7 @@ def tile_list_fleet_ageing_kernel(tc, tab_words, tab_scales, offs, tab2_words, t
                 mix_pass(bank[:, cols], g, t, 1)
             result = work.tile([P, N], F32, name="result", bufs=8)
             if g in TWICE:
-                copier[OUT_ON[(2 * g + k) % len(OUT_ON)]](result[:], bank[:])
+                copier[OUT_ON[(2 * (g % 2) + k) % len(OUT_ON)]](result[:], bank[:])
             else:
                 nc.vector.tensor_tensor(result[:], bank[:], load_sb[g, k][:], ADD)
             t0 = tiles[0][0]
@@ -363,6 +369,6 @@ def tile_list_fleet_ageing_kernel(tc, tab_words, tab_scales, offs, tab2_words, t
         steps = {"g": lambda i: gather_load(i, 0), "G": lambda i: gather_load(i, 1), "p": gather_weather_plane,
                  "w": gather_weather, "o": order_w1_words, "O": order_w1_plane, "x": lambda i: order_w3(),
                  "c": cast_w2, "C": quantise_w2, "L": load_group, "S": stress_of, "W": weave, "Q": quantise_h,
-                 "M": mix_unit, "A": open_last, "E": close_last}
+                 "M": mix_unit, "A": open_last, "B": open_unit, "E": close_last}
         for word in STEPS.split():
             steps[word[0]](int(word[1]))

@@ -20,32 +20,19 @@ COPY = mybir.ActivationFunctionType.Copy
 
 P = 128
 N = 512
-TAB2_SHIFT = 0
+Q = 256
 W3_SHIFT = 8
-WEAVE_PIECES = 4
-LOADS = "L1s TSs S1a T0s UUs T1s WUa GSs M0a M1s A0s S2s T2s BIs A1s GAs W3s S3s"
-STEPS = "O0 o0 g0 G0 L0 o1 O1 g1 G1 c0 C0 p0 w0 L1 L4 L5 S0 c1 C1 S1 p1 w1 S2 S3 p2 w2 W0 Q0 x0 W1 Q1 S4 S5 W2 Q2 W3 Q3 W4 Q4 W5 Q5 M0 M1 B2 B3 M2 M3 B4 B5 M4 M5"
-RING = 4
-PLANES_ON = "VVV"
-W3_ON = "PPPP"
-CAST_ON = "VP"
-GAIN_WEAVE = ("SV", "SV", "SV", "SV", "SV", "SV")
-LOAD_RING = "111111"
-CAST_PIECES = (1, 1)
-STRESS_RING = "212211"
-UNITS = ((0, 512, 0), (0, 512, 1), (512, 256, 0), (512, 256, 1), (768, 256, 0), (768, 256, 1))
-TWICE = (2, 3)
-OUT_ON = "S"
-MIX_RING = "112211"
-STAGE_BUFS = 1
-HOLDS = "g1:picked_first p1:first_sum0 w1:w2_raw1 p2:first_sum1"
+TAB2_SHIFT = 4
+RINGS = {"first": 4, "second": 4}
+CHUNKS = ((0, 256), (256, 256), (512, 256), (768, 256))
+TWICE = ((2, 0), (3, 0))
+STRESS_BUFS = 6
+RESULT_BUFS = 8
 
 
 def tile_list_fleet_ageing_kernel(tc, tab_words, tab_scales, offs, tab2_words, tab2_scales, offs2,
                                               w1_words, w1_scales, w2, bias, gain, w3_words, w3_scales, out):
     nc = tc.nc
-    queue = {"s": nc.sync, "a": nc.scalar, "g": nc.gpsimd}
-    copier = {"V": nc.vector.tensor_copy, "S": nc.scalar.copy, "P": nc.gpsimd.tensor_copy}
     with ExitStack() as ctx:
         lists = ctx.enter_context(tc.tile_pool(name="lists", bufs=1))
         keep = ctx.enter_context(tc.tile_pool(name="keep", bufs=1))
@@ -55,166 +42,160 @@ def tile_list_fleet_ageing_kernel(tc, tab_words, tab_scales, offs, tab2_words, t
         def held(shape, dtype, name):
             return keep.tile(shape, dtype, name=name, align_bytes=64)
 
-        def first_bank():
-            return psum.tile([P, N], F32, name="first_bank", bufs=RING)
+        def taken(shape, dtype, name):
+            return work.tile(shape, dtype, name=name, align_bytes=64)
 
-        def second_bank():
-            return psum.tile([P, N], F32, name="second_bank", bufs=8 - RING)
+        def bank(ring):
+            return psum.tile([P, N], F32, name=ring, bufs=RINGS[ring])
 
         list8 = lists.tile([P, S // 16], U16, name="list8")
         list1 = lists.tile([P, S // 16], U16, name="list1")
-        tab_sc = work.tile([P, T], U8, name="scale_window", align_bytes=64)
+        tab_sc = held([P, T], U8, "tab_sc")
+        tab2_sc = held([P, T], U8, "tab2_sc")
         w1_sc_raw = held([P, 2 * H], U8, "w1_sc_raw")
         v_planes = [held([P, S], U8, "v_plane%d" % a) for a in range(2)]
         w3_sc_raw = held([P, H], U8, "w3_sc_raw")
         warm = held([P, 8], F32, "warm")
         warmed = held([P, 8], F32, "warmed")
-        picked_sc = work.tile([P, S], U8, name="picked_first", align_bytes=64)
+        picked_sc = taken([P, S], U8, "picked_sc")
         w1_raw = held([P, 2, N], I32, "w1_raw")
         tab_w = [held([P, T], I32, "tab_w%d" % a) for a in range(2)]
         tab2_w = held([P, T], I32, "tab2_w")
-        w2_raw = [work.tile([P, 4, N], F32, name="w2_raw%d" % b, align_bytes=64) for b in range(2)]
+        w2_raw = [taken([P, 4, N], F32, "w2_raw%d" % b) for b in range(2)]
         bias_sb = held([P, 2, 4], F32, "bias_sb")
         gain_sb = held([P, 2, 4], F32, "gain_sb")
         w3_raw = held([P, 2, H], I32, "w3_raw")
 
-        nc.sync.dma_start(list8[:], offs)
-        for plane in (tab_sc, w1_sc_raw, v_planes[1]):
-            nc.vector.memset(plane[:].bitcast(I32), 0)
-        nc.vector.memset(warm[:], 0.0)
-        nc.vector.memset(w3_sc_raw[:].bitcast(I32), 0)
+        def zero(engine, plane):
+            engine.memset(plane[:].bitcast(I32), 0)
 
-        def load_tab_scales(q):
+        def load_tab_scales(queue):
             for e in range(2):
-                q.dma_start(tab_sc[e:P:8, :].bitcast(I32), tab_scales[:, e:16:2, :].bitcast(I32).rearrange("a g c -> g a c"))
+                queue.dma_start(tab_sc[e:P:8, :].bitcast(I32),
+                                tab_scales[:, e:16:2, :].bitcast(I32).rearrange("a g c -> g a c"))
 
-        def load_w1(q):
-            q.dma_start(w1_raw[:], w1_words.bitcast(I32).rearrange("a p c -> p a c"))
+        def load_w1(queue):
+            queue.dma_start(w1_raw[:], w1_words.bitcast(I32).rearrange("a p c -> p a c"))
 
-        def load_w1_scales(q):
-            for d in range(4):
-                q.dma_start(w1_sc_raw[32 * d:32 * d + 4, :].bitcast(I32).rearrange("r (a c) -> r a c", a=2),
-                            w1_scales[:, 4 * d:4 * d + 4, :].bitcast(I32).rearrange("a r c -> r a c"))
-
-        def load_table(q, window, dram_pass):
-            q.dma_start(window[:], dram_pass.rearrange("p c i -> p (c i)").bitcast(I32))
-
-        late = {}
-
-        def load_tab2_scales(q):
-            tab2_sc = work.tile([P, T], U8, name="scale_window", align_bytes=64)
-            late["tab2_sc"] = tab2_sc
+        def load_w1_scales(queue):
             for r in range(4):
-                q.dma_start(tab2_sc[r:P:4, :].bitcast(I32),
-                            tab2_scales[0, r:16:4, :].bitcast(I32).unsqueeze(1).to_broadcast([4, 8, T // 4]))
+                queue.dma_start(w1_sc_raw[r:P:32, :].bitcast(I32).rearrange("d (a c) -> d a c", a=2),
+                                w1_scales[:, r:16:4, :].bitcast(I32).rearrange("a d c -> d a c"))
 
-        def load_w2(q, b):
-            q.dma_start(w2_raw[b][:], w2.rearrange("(p j) c -> p j c", j=4)[:, :, b * N:(b + 1) * N])
+        def load_table(queue, window, dram_pass):
+            queue.dma_start(window[:], dram_pass.rearrange("p c i -> p (c i)").bitcast(I32))
 
-        def load_per_channel(q, columns, vector):
-            q.dma_start(columns[:], vector.rearrange("(b p t) -> p b t", b=2, t=4))
+        def load_tab2_scales(queue):
+            for r in range(4):
+                queue.dma_start(tab2_sc[TAB2_SHIFT + r:P:32, :].bitcast(I32), tab2_scales[0, r:16:4, :].bitcast(I32))
 
-        def load_w3_scales(q):
+        def load_w2(queue, b):
+            queue.dma_start(w2_raw[b][:], w2.rearrange("(p j) c -> p j c", j=4)[:, :, b * N:(b + 1) * N])
+
+        def load_per_channel(queue, columns, vector):
+            queue.dma_start(columns[:], vector.rearrange("(b p t) -> p b t", b=2, t=4))
+
+        def load_w3(queue):
+            queue.dma_start(w3_raw[:], w3_words.rearrange("a p c i -> p a (c i)").bitcast(I32))
+
+        def load_w3_scales(queue):
             for d in range(4):
-                q.dma_start(w3_sc_raw[32 * d + W3_SHIFT:32 * d + W3_SHIFT + 8, :].bitcast(I32),
-                            w3_scales[:, 4 * d:4 * d + 4, :].bitcast(I32))
+                queue.dma_start(w3_sc_raw[32 * d + W3_SHIFT:32 * d + W3_SHIFT + 8, :].bitcast(I32),
+                                w3_scales[:, 4 * d:4 * d + 4, :].bitcast(I32))
 
-        def move_scale_rows(q, a):
+        def gather_tab_scales():
+            nc.vector.tensor_copy(picked_sc[:], tab_sc[:].indirect(list8[:]))
+
+        def move_scale_rows(queues, a):
             if a == 0:
                 nc.vector.tensor_copy(v_planes[0][:].bitcast(U32), picked_sc[:].bitcast(U32))
             for r in range(2 if a == 0 else 0, 4):
-                q.dma_start(v_planes[a][r:P:32, :].bitcast(I32),
-                            picked_sc[16 * (r // 2) + 8 * a + r % 2:P:32, :].bitcast(I32))
+                queues[r].dma_start(v_planes[a][r:P:32, :].bitcast(I32),
+                                picked_sc[16 * (r // 2) + 8 * a + r % 2:P:32, :].bitcast(I32))
 
-        loads = {
-            "TS": load_tab_scales, "S1": load_w1_scales, "S2": load_tab2_scales, "S3": load_w3_scales,
-            "T0": lambda q: load_table(q, tab_w[0], tab_words[0]), "T1": lambda q: load_table(q, tab_w[1], tab_words[1]),
-            "T2": lambda q: load_table(q, tab2_w, tab2_words[0]),
-            "UU": load_w1,
-            "A0": lambda q: load_w2(q, 0), "A1": lambda q: load_w2(q, 1),
-            "L1": lambda q: nc.sync.dma_start(list1[:], offs2),
-            "BI": lambda q: load_per_channel(q, bias_sb, bias), "GA": lambda q: load_per_channel(q, gain_sb, gain),
-            "W3": lambda q: q.dma_start(w3_raw[:], w3_words.rearrange("a p c i -> p a (c i)").bitcast(I32)),
-            "WU": lambda q: nc.scalar.activation(warmed[:], warm[:], SIGMOID),
-            "GS": lambda q: nc.vector.tensor_copy(picked_sc[:], tab_sc[:].indirect(list8[:])),
-            "M0": lambda q: move_scale_rows(q, 0), "M1": lambda q: move_scale_rows(q, 1),
-        }
-        for word in LOADS.split():
-            loads[word[:2]](queue[word[2]])
+        def order_words(engine, target, source, per_line):
+            engine.tensor_copy(target.rearrange("p g (t m i) -> p g m t i", t=4, i=per_line),
+                               source.rearrange("p g (m i t) -> p g m t i", t=4, i=per_line))
 
-        def order_words(copy, target, source, per_line):
-            copy(target.rearrange("p g (t m i) -> p g m t i", t=4, i=per_line),
-                 source.rearrange("p g (m i t) -> p g m t i", t=4, i=per_line))
+        def order_plane(target, source):
+            nc.vector.tensor_copy(target.rearrange("p g (t m) -> p g t m", t=4),
+                                  source.rearrange("p g (m t) -> p g t m", t=4))
 
-        def order_plane(copy, target, source):
-            copy(target.rearrange("p g (t m) -> p g t m", t=4), source.rearrange("p g (m t) -> p g t m", t=4))
+        w1_codes, w1_planes, w3_codes, w3_planes = {}, {}, {}, {}
 
-        w1_codes, w1_planes = {}, {}
+        def order_w1_planes():
+            ordered = held([P, 4, N], U8, "w1_planes")
+            order_plane(ordered[:], w1_sc_raw[:].rearrange("p (g c) -> p g c", g=4))
+            for b in range(2):
+                w1_planes[b] = ordered[:].rearrange("p (a b) c -> p b a c", a=2)[:, b, :, :]
 
-        def order_w1_words(b):
-            w1_codes[b] = held([P, 2, 2 * N], U8, "w1_codes%d" % b)
-            order_words(nc.vector.tensor_copy, w1_codes[b][:].bitcast(U16), w1_raw[:].bitcast(U16)[:, :, b * N:(b + 1) * N], 8)
+        def order_w1_words():
+            ordered = held([P, 4, 2 * N], U8, "w1_codes")
+            order_words(nc.vector, ordered[:].bitcast(U16),
+                        w1_raw[:].bitcast(U16).rearrange("p a (b c) -> p (a b) c", b=2), 8)
+            for b in range(2):
+                w1_codes[b] = ordered[:].rearrange("p (a b) c -> p b a c", a=2)[:, b, :, :]
 
-        def order_w1_plane(b):
-            w1_planes[b] = held([P, 2, N], U8, "w1_planes%d" % b)
-            order_plane(copier[PLANES_ON[b]], w1_planes[b][:],
-                        w1_sc_raw[:].rearrange("p (a c) -> p a c", a=2)[:, :, b * N:(b + 1) * N])
+        def order_w3_block(engine, b, name):
+            ordered = taken([P, 2, N], U32, name)
+            order_words(engine, ordered[:], w3_raw[:, :, b * N:(b + 1) * N].bitcast(U32), 4)
+            for a in range(2):
+                w3_codes[b, a] = ordered[:, a:a + 1, :]
 
-        w3_planes = held([P, H], U8, "w3_planes")
+        def order_w3_words(engine, b, a, name):
+            w3_codes[b, a] = taken([P, 1, N], U32, name)
+            order_words(engine, w3_codes[b, a][:], w3_raw[:, a:a + 1, b * N:(b + 1) * N].bitcast(U32), 4)
 
-        def order_w3():
-            w3_codes = work.tile([P, 2 * H], U32, name="weight_stage", align_bytes=64, bufs=STAGE_BUFS)
-            late["w3_codes"] = w3_codes
-            for g in range(4):
-                order_words(copier[W3_ON[g]], w3_codes[:, g * N:(g + 1) * N].unsqueeze(1),
-                            w3_raw[:, g // 2, (g % 2) * N:(g % 2 + 1) * N].bitcast(U32).unsqueeze(1), 4)
-            order_plane(copier[PLANES_ON[2]], w3_planes[:].rearrange("p (g c) -> p g c", g=2),
-                        w3_sc_raw[:].rearrange("p (g c) -> p g c", g=2))
+        def order_w3_planes(name):
+            w3_planes[0] = taken([P, 2, N], U8, name)
+            order_plane(w3_planes[0][:], w3_sc_raw[:].rearrange("p (g c) -> p g c", g=2))
 
         w2_grouped, w2_codes, w2_plane = {}, {}, {}
 
-        def cast_w2(b):
+        def cast_w2(on, b, name):
+            w2_grouped[b] = taken([P, 4 * N], BF16, name)
+            target = w2_grouped[b][:].rearrange("p (t m j) -> p m t j", t=4, j=4)
             source = w2_raw[b][:].rearrange("p j (m t) -> p m t j", t=4)
-            step = 4 // CAST_PIECES[b]
-            for t in range(0, 4, step):
-                w2_grouped[b, t] = work.tile([P, step * N], BF16, name="weight_stage", align_bytes=64, bufs=STAGE_BUFS)
-                copier[CAST_ON[b]](w2_grouped[b, t][:].rearrange("p (t m j) -> p m t j", t=step, j=4), source[:, :, t:t + step, :])
+            if on == "P":
+                nc.gpsimd.tensor_scalar(target, source, 1.0, 0.0, MULT, ADD)
+            elif on == "C":
+                nc.gpsimd.tensor_copy(target, source)
+            elif on == "S":
+                nc.scalar.copy(target, source)
+            else:
+                nc.vector.tensor_copy(target, source)
 
         def quantise_w2(b):
-            step = 4 // CAST_PIECES[b]
-            for t in range(0, 4, step):
-                codes = held([P, step * P], U32, "w2_codes%d%d" % (b, t))
-                plane = held([P, step * P], U8, "w2_plane%d%d" % (b, t))
-                nc.vector.quantize_mx(codes[:].bitcast(FP8X4), plane[:], w2_grouped[b, t][:])
-                for i in range(step):
-                    w2_codes[b, t + i] = codes[:, i * P:(i + 1) * P]
-                    w2_plane[b, t + i] = plane[:, i * P:(i + 1) * P]
-
-        holds = dict(word.split(":") for word in HOLDS.split())
+            w2_codes[b] = held([P, N], U32, "w2_codes%d" % b)
+            w2_plane[b] = held([P, N], U8, "w2_plane%d" % b)
+            nc.vector.quantize_mx(w2_codes[b][:].bitcast(FP8X4), w2_plane[b][:], w2_grouped[b][:])
 
         def gather(window, offsets, first, width, dtype, name):
-            picked = work.tile([P, width], dtype, name=holds.get(name, name), align_bytes=64)
+            picked = taken([P, width], dtype, name)
             nc.vector.tensor_copy(picked[:], window.indirect(offsets[:, first // 16:(first + width) // 16]))
             return picked
 
         v_codes, v2_codes, v2_plane = {}, {}, {}
 
-        def gather_load(h, a):
-            v_codes[h, a] = gather(tab_w[a][:].bitcast(U32), list8, h * N, N, U32, "gG"[a] + str(h))
+        def gather_load(a, first, width, name):
+            picked = gather(tab_w[a][:].bitcast(U32), list8, first, width, U32, name)
+            for c in range(0, width, N):
+                v_codes[(first + c) // N, a] = picked[:, c:c + N]
 
-        def gather_weather_plane(c):
-            v2_plane[c] = gather(late["tab2_sc"][:], list1, UNITS[2 * c][0], UNITS[2 * c][1], U8, "p%d" % c)
+        def chunks_in(first, width):
+            return [q for q, (start, size) in enumerate(CHUNKS) if first <= start < first + width]
 
-        def gather_weather(c):
-            v2_codes[c] = gather(tab2_w[:].bitcast(U32), list1, UNITS[2 * c][0], UNITS[2 * c][1], U32, "w%d" % c)
+        def gather_weather_plane(first, width, name):
+            picked = gather(tab2_sc[:], list1, first, width, U8, name)
+            for q in chunks_in(first, width):
+                v2_plane[q] = picked[TAB2_SHIFT:P, CHUNKS[q][0] - first:CHUNKS[q][0] - first + CHUNKS[q][1]]
 
-        def unit_tiles(g):
-            width = UNITS[g][1]
-            per_bank = N // width
-            return [[(t0 + i, slice(i * width, (i + 1) * width)) for i in range(per_bank)] for t0 in range(0, 4, per_bank)]
+        def gather_weather(first, width, name):
+            picked = gather(tab2_w[:].bitcast(U32), list1, first, width, U32, name)
+            for q in chunks_in(first, width):
+                v2_codes[q] = picked[:, CHUNKS[q][0] - first:CHUNKS[q][0] - first + CHUNKS[q][1]]
 
-        def load_passes(target, g, t, start, stop):
-            first, width, b = UNITS[g]
+        def load_passes(target, first, width, b, t, start, stop):
             h, step = first // N, (N if width == N else P)
             pieces = [(a, c) for c in range(0, width, step) for a in range(2)]
             for a, c in pieces:
@@ -226,149 +207,204 @@ def tile_list_fleet_ageing_kernel(tc, tab_words, tab_scales, offs, tab2_words, t
                     rhs_scale=v_planes[a][:, first + c:first + c + step],
                     start=(start and (a, c) == pieces[0]), stop=(stop and (a, c) == pieces[-1]))
 
-        def weather_pass(target, g, t, start):
-            b = UNITS[g][2]
-            nc.tensor.matmul_mx(
-                target,
-                lhsT=w2_codes[b, t].bitcast(FP8X4), lhsT_scale=w2_plane[b, t],
-                rhs=v2_codes[g // 2][:].bitcast(FP8X4), rhs_scale=v2_plane[g // 2][:],
-                start=start, stop=True)
-
-        def ring(which):
-            return first_bank() if which == "1" else second_bank()
-
         load_sb = {}
 
-        def load_group(g):
-            for k, tiles in enumerate(unit_tiles(g)):
-                bank = ring(LOAD_RING[g])
-                for t, cols in tiles:
-                    load_passes(bank[:, cols], g, t, True, True)
-                load_sb[g, k] = held([P, N], F32, "load_sb%d%d" % (g, k))
-                nc.scalar.copy(load_sb[g, k][:], bank[:])
+        def side_by_side(tile, width, count):
+            return tile[:, 0:count * width].rearrange("p (i j) -> p i j", j=width)
 
-        made = {}
+        def keep_load(first, width, b, ring):
+            kept = held([P, 4, width], F32, "load%d_%d" % (first, b))
+            per_bank = N // width
+            for t0 in range(0, 4, per_bank):
+                sums = bank(ring)
+                for i in range(per_bank):
+                    load_passes(sums[:, i * width:(i + 1) * width], first, width, b, t0 + i, True, True)
+                nc.scalar.copy(kept[:, t0:t0 + per_bank, :], side_by_side(sums, width, per_bank))
+            for q in chunks_in(first, width):
+                load_sb[q, b] = kept[:, :, CHUNKS[q][0] - first:CHUNKS[q][0] - first + CHUNKS[q][1]]
 
-        def stress_of(g):
-            first, width, b = UNITS[g]
-            how = GAIN_WEAVE[g]
-            stress = work.tile([P, 4, width], F32, name="stress", bufs=3)
-            scaled = work.tile([P, 4, width], BF16, name="scaled", bufs=3) if how != "V" else None
-            for k, tiles in enumerate(unit_tiles(g)):
-                bank = ring(STRESS_RING[g])
-                for t, cols in tiles:
-                    if g in TWICE:
-                        load_passes(bank[:, cols], g, t, True, False)
-                    weather_pass(bank[:, cols], g, t, g not in TWICE)
-                summed = bank
-                if g not in TWICE:
-                    if g == 0 and k < 2:
-                        summed = work.tile([P, N], F32, name="first_sum%d" % k, align_bytes=64)
-                    else:
-                        summed = work.tile([P, N], F32, name="summed", bufs=6)
-                    nc.vector.tensor_tensor(summed[:], bank[:], load_sb[g, k][:], ADD)
-                for t, cols in tiles:
-                    nc.scalar.activation(stress[:, t, :], summed[:, cols], SIGMOID, bias=bias_sb[:, b, t:t + 1])
-                for t, cols in tiles:
+        summed, stress, scaled, woven, h_codes, h_plane = {}, {}, {}, {}, {}, {}
+
+        def sum_unit(q, b, ring, names):
+            first, width = CHUNKS[q]
+            per_bank = N // width
+            for k, t0 in enumerate(range(0, 4, per_bank)):
+                sums = bank(ring)
+                for i in range(per_bank):
+                    t = t0 + i
+                    if (q, b) in TWICE:
+                        load_passes(sums[:, i * width:(i + 1) * width], first, width, b, t, True, False)
+                    nc.tensor.matmul_mx(
+                        sums[:, i * width:(i + 1) * width],
+                        lhsT=w2_codes[b][:, t * P:(t + 1) * P].bitcast(FP8X4), lhsT_scale=w2_plane[b][:, t * P:(t + 1) * P],
+                        rhs=v2_codes[q].bitcast(FP8X4), rhs_scale=v2_plane[q],
+                        start=(q, b) not in TWICE, stop=True)
+                total = sums
+                if (q, b) not in TWICE:
+                    total = taken([P, N], F32, names[k])
+                    nc.vector.tensor_tensor(side_by_side(total, width, per_bank), side_by_side(sums, width, per_bank),
+                                            load_sb[q, b][:, t0:t0 + per_bank, :], ADD)
+                for i in range(per_bank):
+                    summed[q, b, t0 + i] = total[:, i * width:(i + 1) * width]
+
+        def sigmoid(q, b, gain_on):
+            width = CHUNKS[q][1]
+            stress[q, b] = work.tile([P, 4, width], F32, name="stress", bufs=STRESS_BUFS)
+            if gain_on != "F":
+                scaled[q, b] = work.tile([P, 4, width], BF16, name="scaled", bufs=6)
+            for t0 in (0, 2):
+                for t in (t0, t0 + 1):
+                    nc.scalar.activation(stress[q, b][:, t, :], summed[q, b, t], SIGMOID, bias=bias_sb[:, b, t:t + 1])
+                for t in (t0, t0 + 1):
                     column = gain_sb[:, b, t:t + 1]
-                    if how[0] == "S":
-                        nc.scalar.activation(scaled[:, t, :], stress[:, t, :], COPY, scale=column)
-                    if how[0] == "P":
-                        nc.gpsimd.tensor_scalar(scaled[:, t, :], stress[:, t, :], column, 0.0, MULT, ADD)
-                    if how[0] == "W":
-                        nc.vector.tensor_scalar(scaled[:, t, :], stress[:, t, :], column, None, MULT)
-            made[g] = stress if how == "V" else scaled
+                    if gain_on == "S":
+                        nc.scalar.activation(scaled[q, b][:, t, :], stress[q, b][:, t, :], COPY, scale=column)
+                    if gain_on == "P":
+                        nc.gpsimd.tensor_scalar(scaled[q, b][:, t, :], stress[q, b][:, t, :], column, 0.0, MULT, ADD)
+                    if gain_on == "V":
+                        nc.vector.tensor_scalar(scaled[q, b][:, t, :], stress[q, b][:, t, :], column, None, MULT)
 
-        woven, h_codes, h_plane = {}, {}, {}
-
-        def weave(g):
-            first, width, b = UNITS[g]
-            how = GAIN_WEAVE[g]
-            woven[g] = work.tile([P, 4 * width], BF16, name="woven", align_bytes=64, bufs=3)
-            if how == "V":
+        def weave(q, b, on, name):
+            width = CHUNKS[q][1]
+            woven[q, b] = taken([P, 4 * width], BF16, name)
+            if on == "F":
                 gains = gain_sb[:, b, :].unsqueeze(1).unsqueeze(3).to_broadcast([P, width // 2, 4, 2])
-                nc.vector.tensor_tensor(woven[g][:].rearrange("p (c i t) -> p c t i", i=2, t=4),
-                                        made[g][:].rearrange("p t (c i) -> p c t i", i=2), gains, MULT)
-                return
-            target = woven[g][:].rearrange("p (c i t) -> p c t i", i=4, t=4)
-            source = made[g][:].rearrange("p t (c i) -> p c t i", i=4)
-            step = width // 4 if how[1] == "V" else 32
-            for c in range(0, width // 4, step):
-                copier[how[1]](target[:, c:c + step, :, :], source[:, c:c + step, :, :])
+                nc.vector.tensor_tensor(woven[q, b][:].rearrange("p (c i t) -> p c t i", i=2, t=4),
+                                        stress[q, b][:].rearrange("p t (c i) -> p c t i", i=2), gains, MULT)
+            elif on == "P":
+                nc.gpsimd.tensor_scalar(woven[q, b][:].rearrange("p (c t) -> p c t", t=4),
+                                        scaled[q, b][:].rearrange("p t c -> p c t"), 1.0, 0.0, MULT, ADD)
+            else:
+                copy = nc.vector.tensor_copy if on == "V" else nc.scalar.copy
+                copy(woven[q, b][:].rearrange("p (c i t) -> p c t i", i=4, t=4),
+                     scaled[q, b][:].rearrange("p t (c i) -> p c t i", i=4))
 
-        def quantise_h(g):
-            width = UNITS[g][1]
-            h_codes[g] = held([P, width], U32, "h_codes%d" % g)
-            h_plane[g] = held([P, width], U8, "h_plane%d" % g)
-            nc.vector.quantize_mx(h_codes[g][:].bitcast(FP8X4), h_plane[g][:], woven[g][:])
+        def quantise_h(q, b):
+            width = CHUNKS[q][1]
+            h_codes[q, b] = held([P, width], U32, "h_codes%d%d" % (q, b))
+            h_plane[q, b] = held([P, width], U8, "h_plane%d%d" % (q, b))
+            nc.vector.quantize_mx(h_codes[q, b][:].bitcast(FP8X4), h_plane[q, b][:], woven[q, b][:])
 
         out_rows = out.rearrange("(b p t) j -> b p t j", b=2, t=4)
 
-        def mix_pass(target, g, t, a):
-            b = UNITS[g][2]
-            first = b * N + t * P
-            source = g - b + a
+        def mix_pass(target, q, b, t, a):
             nc.tensor.matmul_mx(
                 target,
-                lhsT=late["w3_codes"][:, a * H + first:a * H + first + P].bitcast(FP8X4),
-                lhsT_scale=w3_planes[W3_SHIFT + 4 * a:P, first:first + P],
-                rhs=h_codes[source][:].bitcast(FP8X4), rhs_scale=h_plane[source][:],
-                start=(a == 0 and g not in TWICE), stop=(a == 1))
+                lhsT=w3_codes[b, a][:, 0, t * P:(t + 1) * P].bitcast(FP8X4),
+                lhsT_scale=w3_planes[0][W3_SHIFT + 4 * a:P, b, t * P:(t + 1) * P],
+                rhs=h_codes[q, a][:].bitcast(FP8X4), rhs_scale=h_plane[q, a][:],
+                start=(a == 0 and (q, b) not in TWICE), stop=(a == 1))
 
-        def open_tile(target, g, t):
-            if g in TWICE:
-                load_passes(target, g, t, True, False)
-            mix_pass(target, g, t, 0)
+        def mix_unit(q, b, rings, out_on, per_bank, per_store):
+            first, width = CHUNKS[q]
+            for k, t0 in enumerate(range(0, 4, per_bank)):
+                sums = bank(rings[k % len(rings)])
+                for i in range(per_bank):
+                    target = sums[:, i * width:(i + 1) * width]
+                    if (q, b) in TWICE:
+                        load_passes(target, first, width, b, t0 + i, True, False)
+                    for a in range(2):
+                        mix_pass(target, q, b, t0 + i, a)
+                if t0 % per_store == 0:
+                    result = work.tile([P, N], F32, name="result", bufs=RESULT_BUFS)
+                    stored = side_by_side(result, width, per_store)
+                target = stored[:, t0 % per_store:t0 % per_store + per_bank, :]
+                if (q, b) not in TWICE:
+                    nc.vector.tensor_tensor(target, side_by_side(sums, width, per_bank),
+                                            load_sb[q, b][:, t0:t0 + per_bank, :], ADD)
+                elif out_on == "S":
+                    nc.scalar.copy(target, side_by_side(sums, width, per_bank))
+                else:
+                    nc.vector.tensor_copy(target, side_by_side(sums, width, per_bank))
+                if (t0 + per_bank) % per_store == 0:
+                    t1 = t0 + per_bank - per_store
+                    nc.sync.dma_start(out_rows[b, :, t1:t1 + per_store, first:first + width], stored)
 
-        opened = {}
+        nc.sync.dma_start(list8[:], offs)
+        zero(nc.vector, tab_sc)
+        zero(nc.vector, w1_sc_raw)
+        zero(nc.vector, tab2_sc)
+        zero(nc.vector, v_planes[1])
+        nc.vector.memset(warm[:], 0.0)
+        zero(nc.vector, w3_sc_raw)
+        nc.sync.dma_start(list1[:], offs2)
+        load_tab_scales(nc.sync)
+        load_w1_scales(nc.scalar)
+        load_table(nc.sync, tab_w[0], tab_words[0])
 
-        def open_unit(g):
-            for k, tiles in enumerate(unit_tiles(g)):
-                opened[g, k] = ring(MIX_RING[g])
-                t, cols = tiles[0]
-                open_tile(opened[g, k][:, cols], g, t)
+        load_w1(nc.sync)
+        load_table(nc.sync, tab_w[1], tab_words[1])
+        nc.scalar.activation(warmed[:], warm[:], SIGMOID)
+        gather_tab_scales()
+        move_scale_rows([nc.scalar] * 4, 0)
+        move_scale_rows([nc.scalar, nc.scalar, nc.scalar, nc.sync], 1)
+        load_tab2_scales(nc.scalar)
+        load_w2(nc.sync, 0)
+        load_table(nc.sync, tab2_w, tab2_words[0])
+        load_per_channel(nc.sync, bias_sb, bias)
+        load_w2(nc.sync, 1)
+        load_per_channel(nc.sync, gain_sb, gain)
+        load_w3(nc.sync)
+        load_w3_scales(nc.sync)
 
-        def close_bank(g, k):
-            first, width, b = UNITS[g]
-            tiles = unit_tiles(g)[k]
-            ahead = (g, k) in opened
-            bank = opened[g, k] if ahead else ring(MIX_RING[g])
-            for i, (t, cols) in enumerate(tiles):
-                if i > 0 or not ahead:
-                    open_tile(bank[:, cols], g, t)
-                mix_pass(bank[:, cols], g, t, 1)
-            result = work.tile([P, N], F32, name="result", bufs=8)
-            if g in TWICE:
-                copier[OUT_ON[(2 * (g % 2) + k) % len(OUT_ON)]](result[:], bank[:])
-            else:
-                nc.vector.tensor_tensor(result[:], bank[:], load_sb[g, k][:], ADD)
-            t0 = tiles[0][0]
-            nc.sync.dma_start(out_rows[b, :, t0:t0 + len(tiles), first:first + width],
-                              result[:].rearrange("p (t j) -> p t j", j=width))
-
-        def open_last(g):
-            for t in range(4):
-                opened[g, t] = ring(MIX_RING[g])
-                open_tile(opened[g, t][:, 0:UNITS[g][1]], g, t)
-
-        def close_last(unused):
-            for pair in range(2):
-                for g in TWICE:
-                    first, width, b = UNITS[g]
-                    result = work.tile([P, 2, width], F32, name="result", bufs=8)
-                    for i in range(2):
-                        t = 2 * pair + i
-                        mix_pass(opened[g, t][:, 0:width], g, t, 1)
-                        copier[OUT_ON[b]](result[:, i, :], opened[g, t][:, 0:width])
-                    nc.sync.dma_start(out_rows[b, :, 2 * pair:2 * pair + 2, first:first + width], result[:])
-
-        def mix_unit(g):
-            for k in range(len(unit_tiles(g))):
-                close_bank(g, k)
-
-        steps = {"g": lambda i: gather_load(i, 0), "G": lambda i: gather_load(i, 1), "p": gather_weather_plane,
-                 "w": gather_weather, "o": order_w1_words, "O": order_w1_plane, "x": lambda i: order_w3(),
-                 "c": cast_w2, "C": quantise_w2, "L": load_group, "S": stress_of, "W": weave, "Q": quantise_h,
-                 "M": mix_unit, "A": open_last, "B": open_unit, "E": close_last}
-        for word in STEPS.split():
-            steps[word[0]](int(word[1]))
+        order_w1_planes()
+        gather_load(0, 0, 512, "v00")
+        order_w1_words()
+        gather_load(1, 0, 512, "v10")
+        keep_load(0, 512, 0, "first")
+        gather_weather_plane(0, 512, "p0")
+        cast_w2("V", 0, "stage0")
+        quantise_w2(0)
+        gather_weather(0, 256, "w0")
+        gather_weather(256, 256, "w1")
+        sum_unit(0, 0, "second", ("s0", "s1"))
+        sum_unit(1, 0, "second", ("s2", "s3"))
+        gather_load(0, 512, 512, "picked_sc")
+        gather_load(1, 512, 512, "v11")
+        sigmoid(0, 0, "S")
+        keep_load(0, 512, 1, "first")
+        sigmoid(1, 0, "S")
+        cast_w2("P", 1, "stage1")
+        quantise_w2(1)
+        sum_unit(0, 1, "second", ("s4", "s5"))
+        sum_unit(1, 1, "second", ("s6", "s7"))
+        sigmoid(0, 1, "S")
+        sigmoid(1, 1, "S")
+        keep_load(512, 512, 1, "first")
+        gather_weather_plane(512, 512, "s0")
+        gather_weather(512, 512, "w2_raw1")
+        order_w3_block(nc.gpsimd, 0, "stage1")
+        weave(0, 0, "V", "s4")
+        quantise_h(0, 0)
+        order_w3_planes("s5")
+        weave(1, 0, "V", "s6")
+        quantise_h(1, 0)
+        weave(0, 1, "V", "y01")
+        quantise_h(0, 1)
+        order_w3_block(nc.gpsimd, 1, "y01")
+        sum_unit(2, 0, "second", ())
+        sigmoid(2, 0, "S")
+        sum_unit(2, 1, "second", ("u20", "u21"))
+        sigmoid(2, 1, "S")
+        mix_unit(0, 0, ["first"], "S", 2, 2)
+        weave(1, 1, "V", "u20x")
+        quantise_h(1, 1)
+        mix_unit(0, 1, ["first"], "S", 2, 2)
+        sum_unit(3, 0, "second", ())
+        sum_unit(3, 1, "second", ("u30", "u31"))
+        sigmoid(3, 0, "S")
+        mix_unit(1, 0, ["first"], "S", 2, 2)
+        weave(2, 0, "V", "y20")
+        quantise_h(2, 0)
+        weave(2, 1, "V", "y21")
+        quantise_h(2, 1)
+        mix_unit(1, 1, ["first"], "S", 2, 2)
+        weave(3, 0, "V", "y30")
+        quantise_h(3, 0)
+        mix_unit(2, 0, ["first"], "S", 2, 2)
+        sigmoid(3, 1, "S")
+        weave(3, 1, "V", "y31")
+        quantise_h(3, 1)
+        mix_unit(2, 1, ["first"], "S", 2, 2)
+        mix_unit(3, 0, ["second"], "S", 1, 2)
+        mix_unit(3, 1, ["first"], "S", 2, 2)

@@ -24,9 +24,8 @@ Q = 256
 W3_SHIFT = 8
 TAB2_SHIFT = 4
 RINGS = {"first": 4, "second": 4}
-CHUNKS = ((0, 256), (256, 256), (512, 256), (768, 256))
-TWICE = ((2, 0), (3, 0))
-STRESS_BUFS = 6
+TWICE_FROM = (512, 1024)
+STRESS_BUFS = {256: 6}
 RESULT_BUFS = 8
 
 
@@ -182,18 +181,15 @@ def tile_list_fleet_ageing_kernel(tc, tab_words, tab_scales, offs, tab2_words, t
             for c in range(0, width, N):
                 v_codes[(first + c) // N, a] = picked[:, c:c + N]
 
-        def chunks_in(first, width):
-            return [q for q, (start, size) in enumerate(CHUNKS) if first <= start < first + width]
+        def columns(tiles, first, width):
+            start = max(key for key in tiles if key <= first)
+            return tiles[start], slice(first - start, first - start + width)
 
         def gather_weather_plane(first, width, name):
-            picked = gather(tab2_sc[:], list1, first, width, U8, name)
-            for q in chunks_in(first, width):
-                v2_plane[q] = picked[TAB2_SHIFT:P, CHUNKS[q][0] - first:CHUNKS[q][0] - first + CHUNKS[q][1]]
+            v2_plane[first] = gather(tab2_sc[:], list1, first, width, U8, name)
 
         def gather_weather(first, width, name):
-            picked = gather(tab2_w[:].bitcast(U32), list1, first, width, U32, name)
-            for q in chunks_in(first, width):
-                v2_codes[q] = picked[:, CHUNKS[q][0] - first:CHUNKS[q][0] - first + CHUNKS[q][1]]
+            v2_codes[first] = gather(tab2_w[:].bitcast(U32), list1, first, width, U32, name)
 
         def load_passes(target, first, width, b, t, start, stop):
             h, step = first // N, (N if width == N else P)
@@ -207,111 +203,115 @@ def tile_list_fleet_ageing_kernel(tc, tab_words, tab_scales, offs, tab2_words, t
                     rhs_scale=v_planes[a][:, first + c:first + c + step],
                     start=(start and (a, c) == pieces[0]), stop=(stop and (a, c) == pieces[-1]))
 
-        load_sb = {}
+        load_sb = [{}, {}]
 
         def side_by_side(tile, width, count):
             return tile[:, 0:count * width].rearrange("p (i j) -> p i j", j=width)
 
         def keep_load(first, width, b, ring):
             kept = held([P, 4, width], F32, "load%d_%d" % (first, b))
+            load_sb[b][first] = kept
             per_bank = N // width
             for t0 in range(0, 4, per_bank):
                 sums = bank(ring)
                 for i in range(per_bank):
                     load_passes(sums[:, i * width:(i + 1) * width], first, width, b, t0 + i, True, True)
                 nc.scalar.copy(kept[:, t0:t0 + per_bank, :], side_by_side(sums, width, per_bank))
-            for q in chunks_in(first, width):
-                load_sb[q, b] = kept[:, :, CHUNKS[q][0] - first:CHUNKS[q][0] - first + CHUNKS[q][1]]
 
-        summed, stress, scaled, woven, h_codes, h_plane = {}, {}, {}, {}, {}, {}
+        def twice(first, b):
+            return first >= TWICE_FROM[b]
 
-        def sum_unit(q, b, ring, names):
-            first, width = CHUNKS[q]
+        summed, stress, scaled, woven = {}, {}, {}, {}
+        h_codes, h_plane = [{}, {}], [{}, {}]
+
+        def sum_unit(first, width, b, ring, names):
             per_bank = N // width
             for k, t0 in enumerate(range(0, 4, per_bank)):
                 sums = bank(ring)
                 for i in range(per_bank):
                     t = t0 + i
-                    if (q, b) in TWICE:
+                    if twice(first, b):
                         load_passes(sums[:, i * width:(i + 1) * width], first, width, b, t, True, False)
+                    codes, cols = columns(v2_codes, first, width)
+                    plane, plane_cols = columns(v2_plane, first, width)
                     nc.tensor.matmul_mx(
                         sums[:, i * width:(i + 1) * width],
                         lhsT=w2_codes[b][:, t * P:(t + 1) * P].bitcast(FP8X4), lhsT_scale=w2_plane[b][:, t * P:(t + 1) * P],
-                        rhs=v2_codes[q].bitcast(FP8X4), rhs_scale=v2_plane[q],
-                        start=(q, b) not in TWICE, stop=True)
+                        rhs=codes[:, cols].bitcast(FP8X4), rhs_scale=plane[TAB2_SHIFT:P, plane_cols],
+                        start=not twice(first, b), stop=True)
                 total = sums
-                if (q, b) not in TWICE:
+                if not twice(first, b):
+                    kept, cols = columns(load_sb[b], first, width)
                     total = taken([P, N], F32, names[k])
                     nc.vector.tensor_tensor(side_by_side(total, width, per_bank), side_by_side(sums, width, per_bank),
-                                            load_sb[q, b][:, t0:t0 + per_bank, :], ADD)
+                                            kept[:, t0:t0 + per_bank, cols], ADD)
                 for i in range(per_bank):
-                    summed[q, b, t0 + i] = total[:, i * width:(i + 1) * width]
+                    summed[first, b, t0 + i] = total[:, i * width:(i + 1) * width]
 
-        def sigmoid(q, b, gain_on):
-            width = CHUNKS[q][1]
-            stress[q, b] = work.tile([P, 4, width], F32, name="stress", bufs=STRESS_BUFS)
+        def sigmoid(first, width, b, gain_on):
+            stress[first, b] = work.tile([P, 4, width], F32, name="stress%d" % width, bufs=STRESS_BUFS[width])
             if gain_on != "F":
-                scaled[q, b] = work.tile([P, 4, width], BF16, name="scaled", bufs=6)
+                scaled[first, b] = work.tile([P, 4, width], BF16, name="scaled%d" % width, bufs=STRESS_BUFS[width])
             for t0 in (0, 2):
                 for t in (t0, t0 + 1):
-                    nc.scalar.activation(stress[q, b][:, t, :], summed[q, b, t], SIGMOID, bias=bias_sb[:, b, t:t + 1])
+                    nc.scalar.activation(stress[first, b][:, t, :], summed[first, b, t], SIGMOID, bias=bias_sb[:, b, t:t + 1])
                 for t in (t0, t0 + 1):
                     column = gain_sb[:, b, t:t + 1]
                     if gain_on == "S":
-                        nc.scalar.activation(scaled[q, b][:, t, :], stress[q, b][:, t, :], COPY, scale=column)
+                        nc.scalar.activation(scaled[first, b][:, t, :], stress[first, b][:, t, :], COPY, scale=column)
                     if gain_on == "P":
-                        nc.gpsimd.tensor_scalar(scaled[q, b][:, t, :], stress[q, b][:, t, :], column, 0.0, MULT, ADD)
+                        nc.gpsimd.tensor_scalar(scaled[first, b][:, t, :], stress[first, b][:, t, :], column, 0.0, MULT, ADD)
                     if gain_on == "V":
-                        nc.vector.tensor_scalar(scaled[q, b][:, t, :], stress[q, b][:, t, :], column, None, MULT)
+                        nc.vector.tensor_scalar(scaled[first, b][:, t, :], stress[first, b][:, t, :], column, None, MULT)
 
-        def weave(q, b, on, name):
-            width = CHUNKS[q][1]
-            woven[q, b] = taken([P, 4 * width], BF16, name)
+        def weave(first, width, b, on, name):
+            woven[first, b] = taken([P, 4 * width], BF16, name)
             if on == "F":
                 gains = gain_sb[:, b, :].unsqueeze(1).unsqueeze(3).to_broadcast([P, width // 2, 4, 2])
-                nc.vector.tensor_tensor(woven[q, b][:].rearrange("p (c i t) -> p c t i", i=2, t=4),
-                                        stress[q, b][:].rearrange("p t (c i) -> p c t i", i=2), gains, MULT)
+                nc.vector.tensor_tensor(woven[first, b][:].rearrange("p (c i t) -> p c t i", i=2, t=4),
+                                        stress[first, b][:].rearrange("p t (c i) -> p c t i", i=2), gains, MULT)
             elif on == "P":
-                nc.gpsimd.tensor_scalar(woven[q, b][:].rearrange("p (c t) -> p c t", t=4),
-                                        scaled[q, b][:].rearrange("p t c -> p c t"), 1.0, 0.0, MULT, ADD)
+                nc.gpsimd.tensor_scalar(woven[first, b][:].rearrange("p (c t) -> p c t", t=4),
+                                        scaled[first, b][:].rearrange("p t c -> p c t"), 1.0, 0.0, MULT, ADD)
             else:
                 copy = nc.vector.tensor_copy if on == "V" else nc.scalar.copy
-                copy(woven[q, b][:].rearrange("p (c i t) -> p c t i", i=4, t=4),
-                     scaled[q, b][:].rearrange("p t (c i) -> p c t i", i=4))
+                copy(woven[first, b][:].rearrange("p (c i t) -> p c t i", i=4, t=4),
+                     scaled[first, b][:].rearrange("p t (c i) -> p c t i", i=4))
 
-        def quantise_h(q, b):
-            width = CHUNKS[q][1]
-            h_codes[q, b] = held([P, width], U32, "h_codes%d%d" % (q, b))
-            h_plane[q, b] = held([P, width], U8, "h_plane%d%d" % (q, b))
-            nc.vector.quantize_mx(h_codes[q, b][:].bitcast(FP8X4), h_plane[q, b][:], woven[q, b][:])
+        def quantise_h(first, width, b):
+            codes = held([P, width], U32, "h_codes%d%d" % (first // Q, b))
+            plane = held([P, width], U8, "h_plane%d%d" % (first // Q, b))
+            h_codes[b][first], h_plane[b][first] = codes, plane
+            nc.vector.quantize_mx(codes[:].bitcast(FP8X4), plane[:], woven[first, b][:])
 
         out_rows = out.rearrange("(b p t) j -> b p t j", b=2, t=4)
 
-        def mix_pass(target, q, b, t, a):
+        def mix_pass(target, first, width, b, t, a):
+            codes, cols = columns(h_codes[a], first, width)
+            plane, cols = columns(h_plane[a], first, width)
             nc.tensor.matmul_mx(
                 target,
                 lhsT=w3_codes[b, a][:, 0, t * P:(t + 1) * P].bitcast(FP8X4),
                 lhsT_scale=w3_planes[0][W3_SHIFT + 4 * a:P, b, t * P:(t + 1) * P],
-                rhs=h_codes[q, a][:].bitcast(FP8X4), rhs_scale=h_plane[q, a][:],
-                start=(a == 0 and (q, b) not in TWICE), stop=(a == 1))
+                rhs=codes[:, cols].bitcast(FP8X4), rhs_scale=plane[:, cols],
+                start=(a == 0 and not twice(first, b)), stop=(a == 1))
 
-        def mix_unit(q, b, rings, out_on, per_bank, per_store):
-            first, width = CHUNKS[q]
-            for k, t0 in enumerate(range(0, 4, per_bank)):
-                sums = bank(rings[k % len(rings)])
+        def mix_unit(first, width, b, ring, out_on, per_bank, per_store):
+            for t0 in range(0, 4, per_bank):
+                sums = bank(ring)
                 for i in range(per_bank):
                     target = sums[:, i * width:(i + 1) * width]
-                    if (q, b) in TWICE:
+                    if twice(first, b):
                         load_passes(target, first, width, b, t0 + i, True, False)
                     for a in range(2):
-                        mix_pass(target, q, b, t0 + i, a)
+                        mix_pass(target, first, width, b, t0 + i, a)
                 if t0 % per_store == 0:
                     result = work.tile([P, N], F32, name="result", bufs=RESULT_BUFS)
                     stored = side_by_side(result, width, per_store)
                 target = stored[:, t0 % per_store:t0 % per_store + per_bank, :]
-                if (q, b) not in TWICE:
-                    nc.vector.tensor_tensor(target, side_by_side(sums, width, per_bank),
-                                            load_sb[q, b][:, t0:t0 + per_bank, :], ADD)
+                if not twice(first, b):
+                    kept, cols = columns(load_sb[b], first, width)
+                    nc.vector.tensor_tensor(target, side_by_side(sums, width, per_bank), kept[:, t0:t0 + per_bank, cols], ADD)
                 elif out_on == "S":
                     nc.scalar.copy(target, side_by_side(sums, width, per_bank))
                 else:
@@ -322,8 +322,8 @@ def tile_list_fleet_ageing_kernel(tc, tab_words, tab_scales, offs, tab2_words, t
 
         nc.sync.dma_start(list8[:], offs)
         zero(nc.vector, tab_sc)
-        zero(nc.vector, w1_sc_raw)
         zero(nc.vector, tab2_sc)
+        zero(nc.vector, w1_sc_raw)
         zero(nc.vector, v_planes[1])
         nc.vector.memset(warm[:], 0.0)
         zero(nc.vector, w3_sc_raw)
@@ -338,7 +338,7 @@ def tile_list_fleet_ageing_kernel(tc, tab_words, tab_scales, offs, tab2_words, t
         gather_tab_scales()
         move_scale_rows([nc.scalar] * 4, 0)
         move_scale_rows([nc.scalar, nc.scalar, nc.scalar, nc.sync], 1)
-        load_tab2_scales(nc.scalar)
+        load_tab2_scales(nc.gpsimd)
         load_w2(nc.sync, 0)
         load_table(nc.sync, tab2_w, tab2_words[0])
         load_per_channel(nc.sync, bias_sb, bias)
@@ -348,63 +348,63 @@ def tile_list_fleet_ageing_kernel(tc, tab_words, tab_scales, offs, tab2_words, t
         load_w3_scales(nc.sync)
 
         order_w1_planes()
-        gather_load(0, 0, 512, "v00")
+        gather_load(0, 0, 512, "va0")
         order_w1_words()
-        gather_load(1, 0, 512, "v10")
+        gather_load(1, 0, 512, "va1")
         keep_load(0, 512, 0, "first")
-        gather_weather_plane(0, 512, "p0")
         cast_w2("V", 0, "stage0")
+        gather_weather_plane(0, 512, "w2_raw0")
         quantise_w2(0)
         gather_weather(0, 256, "w0")
         gather_weather(256, 256, "w1")
-        sum_unit(0, 0, "second", ("s0", "s1"))
-        sum_unit(1, 0, "second", ("s2", "s3"))
+        sum_unit(0, 256, 0, "second", ("s000", "s001",))
+        sum_unit(256, 256, 0, "second", ("s100", "s101",))
         gather_load(0, 512, 512, "picked_sc")
-        gather_load(1, 512, 512, "v11")
-        sigmoid(0, 0, "S")
+        gather_load(1, 512, 512, "vb1")
+        sigmoid(0, 256, 0, "S")
         keep_load(0, 512, 1, "first")
-        sigmoid(1, 0, "S")
+        sigmoid(256, 256, 0, "S")
         cast_w2("P", 1, "stage1")
         quantise_w2(1)
-        sum_unit(0, 1, "second", ("s4", "s5"))
-        sum_unit(1, 1, "second", ("s6", "s7"))
-        sigmoid(0, 1, "S")
-        sigmoid(1, 1, "S")
+        sum_unit(0, 256, 1, "second", ("s010", "s011",))
+        sum_unit(256, 256, 1, "second", ("s110", "s111",))
+        sigmoid(0, 256, 1, "S")
+        sigmoid(256, 256, 1, "S")
         keep_load(512, 512, 1, "first")
-        gather_weather_plane(512, 512, "s0")
+        gather_weather_plane(512, 512, "s000")
         gather_weather(512, 512, "w2_raw1")
         order_w3_block(nc.gpsimd, 0, "stage1")
-        weave(0, 0, "V", "s4")
-        quantise_h(0, 0)
-        order_w3_planes("s5")
-        weave(1, 0, "V", "s6")
-        quantise_h(1, 0)
-        weave(0, 1, "V", "y01")
-        quantise_h(0, 1)
+        weave(0, 256, 0, "V", "s010")
+        quantise_h(0, 256, 0)
+        order_w3_planes("w3_planes")
+        weave(256, 256, 0, "V", "s110")
+        quantise_h(256, 256, 0)
+        weave(0, 256, 1, "V", "y01")
+        quantise_h(0, 256, 1)
         order_w3_block(nc.gpsimd, 1, "y01")
-        sum_unit(2, 0, "second", ())
-        sigmoid(2, 0, "S")
-        sum_unit(2, 1, "second", ("u20", "u21"))
-        sigmoid(2, 1, "S")
-        mix_unit(0, 0, ["first"], "S", 2, 2)
-        weave(1, 1, "V", "u20x")
-        quantise_h(1, 1)
-        mix_unit(0, 1, ["first"], "S", 2, 2)
-        sum_unit(3, 0, "second", ())
-        sum_unit(3, 1, "second", ("u30", "u31"))
-        sigmoid(3, 0, "S")
-        mix_unit(1, 0, ["first"], "S", 2, 2)
-        weave(2, 0, "V", "y20")
-        quantise_h(2, 0)
-        weave(2, 1, "V", "y21")
-        quantise_h(2, 1)
-        mix_unit(1, 1, ["first"], "S", 2, 2)
-        weave(3, 0, "V", "y30")
-        quantise_h(3, 0)
-        mix_unit(2, 0, ["first"], "S", 2, 2)
-        sigmoid(3, 1, "S")
-        weave(3, 1, "V", "y31")
-        quantise_h(3, 1)
-        mix_unit(2, 1, ["first"], "S", 2, 2)
-        mix_unit(3, 0, ["second"], "S", 1, 2)
-        mix_unit(3, 1, ["first"], "S", 2, 2)
+        sum_unit(512, 256, 0, "second", ("s200", "s201",))
+        sigmoid(512, 256, 0, "S")
+        sum_unit(512, 256, 1, "second", ("s210", "s211",))
+        sigmoid(512, 256, 1, "S")
+        mix_unit(0, 256, 0, "first", "S", 2, 2)
+        weave(256, 256, 1, "V", "y11")
+        quantise_h(256, 256, 1)
+        mix_unit(0, 256, 1, "first", "S", 2, 2)
+        sum_unit(768, 256, 0, "second", ("s300", "s301",))
+        sum_unit(768, 256, 1, "second", ("s310", "s311",))
+        sigmoid(768, 256, 0, "S")
+        mix_unit(256, 256, 0, "first", "S", 2, 2)
+        weave(512, 256, 0, "V", "y20")
+        quantise_h(512, 256, 0)
+        weave(512, 256, 1, "V", "y21")
+        quantise_h(512, 256, 1)
+        mix_unit(256, 256, 1, "first", "S", 2, 2)
+        weave(768, 256, 0, "V", "y30")
+        quantise_h(768, 256, 0)
+        sigmoid(768, 256, 1, "S")
+        mix_unit(512, 256, 0, "first", "S", 2, 2)
+        weave(768, 256, 1, "V", "y31")
+        quantise_h(768, 256, 1)
+        mix_unit(512, 256, 1, "first", "S", 2, 2)
+        mix_unit(768, 256, 0, "second", "S", 1, 2)
+        mix_unit(768, 256, 1, "first", "S", 2, 2)

@@ -27,6 +27,7 @@ RINGS = {"first": 4, "second": 4}
 TWICE_FROM = (512, 1024)
 STRESS_BUFS = {256: 6}
 RESULT_BUFS = 8
+GROUPS = (((0, 0),), ((256, 0),), ((0, 1),), ((256, 1),), ((512, 0),), ((512, 1),), ((768, 0),), ((768, 1),))
 
 
 def tile_list_fleet_ageing_kernel(tc, tab_words, tab_scales, offs, tab2_words, tab2_scales, offs2,
@@ -221,7 +222,7 @@ def tile_list_fleet_ageing_kernel(tc, tab_words, tab_scales, offs, tab2_words, t
         def twice(first, b):
             return first >= TWICE_FROM[b]
 
-        summed, stress, scaled, woven = {}, {}, {}, {}
+        summed, stress, scaled, woven, grouped = {}, {}, {}, {}, {}
         h_codes, h_plane = [{}, {}], [{}, {}]
 
         def sum_unit(first, width, b, ring, names):
@@ -250,8 +251,11 @@ def tile_list_fleet_ageing_kernel(tc, tab_words, tab_scales, offs, tab2_words, t
 
         def sigmoid(first, width, b, gain_on):
             stress[first, b] = work.tile([P, 4, width], F32, name="stress%d" % width, bufs=STRESS_BUFS[width])
+            group = [g for g in GROUPS if (first, b) in g][0]
+            if gain_on != "F" and group not in grouped:
+                grouped[group] = held([P, len(group), 4, width], BF16, "scaled%d%d" % (first // P, b))
             if gain_on != "F":
-                scaled[first, b] = work.tile([P, 4, width], BF16, name="scaled%d" % width, bufs=STRESS_BUFS[width])
+                scaled[first, b] = grouped[group][:, group.index((first, b)), :, :]
             for t0 in (0, 2):
                 for t in (t0, t0 + 1):
                     nc.scalar.activation(stress[first, b][:, t, :], summed[first, b, t], SIGMOID, bias=bias_sb[:, b, t:t + 1])
@@ -265,24 +269,28 @@ def tile_list_fleet_ageing_kernel(tc, tab_words, tab_scales, offs, tab2_words, t
                         nc.vector.tensor_scalar(scaled[first, b][:, t, :], stress[first, b][:, t, :], column, None, MULT)
 
         def weave(first, width, b, on, name):
-            woven[first, b] = taken([P, 4 * width], BF16, name)
+            group = [g for g in GROUPS if (first, b) in g][0]
+            woven[group] = taken([P, len(group), 4 * width], BF16, name)
             if on == "F":
                 gains = gain_sb[:, b, :].unsqueeze(1).unsqueeze(3).to_broadcast([P, width // 2, 4, 2])
-                nc.vector.tensor_tensor(woven[first, b][:].rearrange("p (c i t) -> p c t i", i=2, t=4),
+                nc.vector.tensor_tensor(woven[group][:, 0, :].rearrange("p (c i t) -> p c t i", i=2, t=4),
                                         stress[first, b][:].rearrange("p t (c i) -> p c t i", i=2), gains, MULT)
             elif on == "P":
-                nc.gpsimd.tensor_scalar(woven[first, b][:].rearrange("p (c t) -> p c t", t=4),
-                                        scaled[first, b][:].rearrange("p t c -> p c t"), 1.0, 0.0, MULT, ADD)
+                nc.gpsimd.tensor_scalar(woven[group][:].rearrange("p g (c t) -> p g c t", t=4),
+                                        grouped[group][:].rearrange("p g t c -> p g c t"), 1.0, 0.0, MULT, ADD)
             else:
                 copy = nc.vector.tensor_copy if on == "V" else nc.scalar.copy
-                copy(woven[first, b][:].rearrange("p (c i t) -> p c t i", i=4, t=4),
-                     scaled[first, b][:].rearrange("p t (c i) -> p c t i", i=4))
+                copy(woven[group][:].rearrange("p g (c i t) -> p g c t i", i=4, t=4),
+                     grouped[group][:].rearrange("p g t (c i) -> p g c t i", i=4))
 
         def quantise_h(first, width, b):
-            codes = held([P, width], U32, "h_codes%d%d" % (first // Q, b))
-            plane = held([P, width], U8, "h_plane%d%d" % (first // Q, b))
-            h_codes[b][first], h_plane[b][first] = codes, plane
-            nc.vector.quantize_mx(codes[:].bitcast(FP8X4), plane[:], woven[first, b][:])
+            group = [g for g in GROUPS if (first, b) in g][0]
+            codes = held([P, len(group) * width], U32, "h_codes%d%d" % (first // P, b))
+            plane = held([P, len(group) * width], U8, "h_plane%d%d" % (first // P, b))
+            for i, (start, block) in enumerate(group):
+                h_codes[block][start] = codes[:, i * width:(i + 1) * width]
+                h_plane[block][start] = plane[:, i * width:(i + 1) * width]
+            nc.vector.quantize_mx(codes[:].bitcast(FP8X4), plane[:], woven[group][:].rearrange("p g c -> p (g c)"))
 
         out_rows = out.rearrange("(b p t) j -> b p t j", b=2, t=4)
 
@@ -322,8 +330,8 @@ def tile_list_fleet_ageing_kernel(tc, tab_words, tab_scales, offs, tab2_words, t
 
         nc.sync.dma_start(list8[:], offs)
         zero(nc.vector, tab_sc)
-        zero(nc.vector, tab2_sc)
         zero(nc.vector, w1_sc_raw)
+        zero(nc.vector, tab2_sc)
         zero(nc.vector, v_planes[1])
         nc.vector.memset(warm[:], 0.0)
         zero(nc.vector, w3_sc_raw)
@@ -338,9 +346,9 @@ def tile_list_fleet_ageing_kernel(tc, tab_words, tab_scales, offs, tab2_words, t
         gather_tab_scales()
         move_scale_rows([nc.scalar] * 4, 0)
         move_scale_rows([nc.scalar, nc.scalar, nc.scalar, nc.sync], 1)
-        load_tab2_scales(nc.gpsimd)
         load_w2(nc.sync, 0)
         load_table(nc.sync, tab2_w, tab2_words[0])
+        load_tab2_scales(nc.sync)
         load_per_channel(nc.sync, bias_sb, bias)
         load_w2(nc.sync, 1)
         load_per_channel(nc.sync, gain_sb, gain)
@@ -353,10 +361,11 @@ def tile_list_fleet_ageing_kernel(tc, tab_words, tab_scales, offs, tab2_words, t
         gather_load(1, 0, 512, "va1")
         keep_load(0, 512, 0, "first")
         cast_w2("V", 0, "stage0")
-        gather_weather_plane(0, 512, "w2_raw0")
         quantise_w2(0)
         gather_weather(0, 256, "w0")
         gather_weather(256, 256, "w1")
+        gather_weather_plane(0, 256, "p0")
+        gather_weather_plane(256, 256, "p1")
         sum_unit(0, 256, 0, "second", ("s000", "s001",))
         sum_unit(256, 256, 0, "second", ("s100", "s101",))
         gather_load(0, 512, 512, "picked_sc")
@@ -376,7 +385,7 @@ def tile_list_fleet_ageing_kernel(tc, tab_words, tab_scales, offs, tab2_words, t
         order_w3_block(nc.gpsimd, 0, "stage1")
         weave(0, 256, 0, "V", "s010")
         quantise_h(0, 256, 0)
-        order_w3_planes("w3_planes")
+        order_w3_planes("s011")
         weave(256, 256, 0, "V", "s110")
         quantise_h(256, 256, 0)
         weave(0, 256, 1, "V", "y01")

@@ -21,13 +21,13 @@ COPY = mybir.ActivationFunctionType.Copy
 P = 128
 N = 512
 Q = 256
-W3_SHIFT = 8
 TAB2_SHIFT = 4
-RINGS = {"first": 4, "second": 4}
-TWICE_FROM = (512, 1024)
-STRESS_BUFS = {256: 6}
+W3_SHIFT = 8
+RING = 4
+TWICE = ((2, 0), (3, 0))
+FUSED = ((1, 1), (3, 1))
+SIGMOID_BUFS = 5
 RESULT_BUFS = 8
-GROUPS = (((0, 0),), ((256, 0),), ((0, 1),), ((256, 1),), ((512, 0),), ((512, 1),), ((768, 0),), ((768, 1),))
 
 
 def tile_list_fleet_ageing_kernel(tc, tab_words, tab_scales, offs, tab2_words, tab2_scales, offs2,
@@ -42,11 +42,14 @@ def tile_list_fleet_ageing_kernel(tc, tab_words, tab_scales, offs, tab2_words, t
         def held(shape, dtype, name):
             return keep.tile(shape, dtype, name=name, align_bytes=64)
 
-        def taken(shape, dtype, name):
+        def shared(shape, dtype, name):
             return work.tile(shape, dtype, name=name, align_bytes=64)
 
         def bank(ring):
-            return psum.tile([P, N], F32, name=ring, bufs=RINGS[ring])
+            return psum.tile([P, N], F32, name=ring, bufs=RING)
+
+        def side_by_side(tile, count, width):
+            return tile[:, 0:count * width].rearrange("p (i j) -> p i j", j=width)
 
         list8 = lists.tile([P, S // 16], U16, name="list8")
         list1 = lists.tile([P, S // 16], U16, name="list1")
@@ -57,61 +60,62 @@ def tile_list_fleet_ageing_kernel(tc, tab_words, tab_scales, offs, tab2_words, t
         w3_sc_raw = held([P, H], U8, "w3_sc_raw")
         warm = held([P, 8], F32, "warm")
         warmed = held([P, 8], F32, "warmed")
-        picked_sc = taken([P, S], U8, "picked_sc")
+        picked_sc = shared([P, S], U8, "picked_sc")
         w1_raw = held([P, 2, N], I32, "w1_raw")
         tab_w = [held([P, T], I32, "tab_w%d" % a) for a in range(2)]
         tab2_w = held([P, T], I32, "tab2_w")
-        w2_raw = [taken([P, 4, N], F32, "w2_raw%d" % b) for b in range(2)]
+        w2_raw = [shared([P, 4, N], F32, "w2_raw%d" % b) for b in range(2)]
         bias_sb = held([P, 2, 4], F32, "bias_sb")
         gain_sb = held([P, 2, 4], F32, "gain_sb")
-        w3_raw = held([P, 2, H], I32, "w3_raw")
+        w3_raw = [shared([P, 2, N], I32, "w3_raw%d" % b) for b in range(2)]
 
-        def zero(engine, plane):
-            engine.memset(plane[:].bitcast(I32), 0)
+        def load_table(window, dram_pass):
+            nc.sync.dma_start(window[:], dram_pass.rearrange("p c i -> p (c i)").bitcast(I32))
 
-        def load_tab_scales(queue):
-            for e in range(2):
-                queue.dma_start(tab_sc[e:P:8, :].bitcast(I32),
-                                tab_scales[:, e:16:2, :].bitcast(I32).rearrange("a g c -> g a c"))
+        def load_w2(b):
+            nc.sync.dma_start(w2_raw[b][:], w2.rearrange("(p j) c -> p j c", j=4)[:, :, b * N:(b + 1) * N])
 
-        def load_w1(queue):
-            queue.dma_start(w1_raw[:], w1_words.bitcast(I32).rearrange("a p c -> p a c"))
+        def load_per_channel(columns, vector):
+            nc.sync.dma_start(columns[:], vector.rearrange("(b p t) -> p b t", b=2, t=4))
 
-        def load_w1_scales(queue):
-            for r in range(4):
-                queue.dma_start(w1_sc_raw[r:P:32, :].bitcast(I32).rearrange("d (a c) -> d a c", a=2),
+        nc.sync.dma_start(list8[:], offs)
+        for scale_tile in (tab_sc, w1_sc_raw, tab2_sc, v_planes[1]):
+            nc.vector.memset(scale_tile[:].bitcast(I32), 0)
+        nc.vector.memset(warm[:], 0.0)
+        nc.vector.memset(w3_sc_raw[:].bitcast(I32), 0)
+        nc.sync.dma_start(list1[:], offs2)
+        for e in range(2):
+            nc.sync.dma_start(tab_sc[e:P:8, :].bitcast(I32),
+                              tab_scales[:, e:16:2, :].bitcast(I32).rearrange("a g c -> g a c"))
+        for r in range(4):
+            nc.scalar.dma_start(w1_sc_raw[r:P:32, :].bitcast(I32).rearrange("d (a c) -> d a c", a=2),
                                 w1_scales[:, r:16:4, :].bitcast(I32).rearrange("a d c -> d a c"))
+        load_table(tab_w[0], tab_words[0])
+        nc.sync.dma_start(w1_raw[:], w1_words.bitcast(I32).rearrange("a p c -> p a c"))
+        load_table(tab_w[1], tab_words[1])
+        nc.scalar.activation(warmed[:], warm[:], SIGMOID)
 
-        def load_table(queue, window, dram_pass):
-            queue.dma_start(window[:], dram_pass.rearrange("p c i -> p (c i)").bitcast(I32))
+        nc.vector.tensor_copy(picked_sc[:], tab_sc[:].indirect(list8[:]))
+        nc.vector.tensor_copy(v_planes[0][:].bitcast(U32), picked_sc[:].bitcast(U32))
+        moves = [(0, 2), (0, 3)] + [(1, r) for r in range(4)]
+        for a, r in moves:
+            queue = nc.sync if (a, r) == moves[-1] else nc.scalar
+            queue.dma_start(v_planes[a][r:P:32, :].bitcast(I32),
+                            picked_sc[16 * (r // 2) + 8 * a + r % 2:P:32, :].bitcast(I32))
 
-        def load_tab2_scales(queue):
-            for r in range(4):
-                queue.dma_start(tab2_sc[TAB2_SHIFT + r:P:32, :].bitcast(I32), tab2_scales[0, r:16:4, :].bitcast(I32))
-
-        def load_w2(queue, b):
-            queue.dma_start(w2_raw[b][:], w2.rearrange("(p j) c -> p j c", j=4)[:, :, b * N:(b + 1) * N])
-
-        def load_per_channel(queue, columns, vector):
-            queue.dma_start(columns[:], vector.rearrange("(b p t) -> p b t", b=2, t=4))
-
-        def load_w3(queue):
-            queue.dma_start(w3_raw[:], w3_words.rearrange("a p c i -> p a (c i)").bitcast(I32))
-
-        def load_w3_scales(queue):
-            for d in range(4):
-                queue.dma_start(w3_sc_raw[32 * d + W3_SHIFT:32 * d + W3_SHIFT + 8, :].bitcast(I32),
-                                w3_scales[:, 4 * d:4 * d + 4, :].bitcast(I32))
-
-        def gather_tab_scales():
-            nc.vector.tensor_copy(picked_sc[:], tab_sc[:].indirect(list8[:]))
-
-        def move_scale_rows(queues, a):
-            if a == 0:
-                nc.vector.tensor_copy(v_planes[0][:].bitcast(U32), picked_sc[:].bitcast(U32))
-            for r in range(2 if a == 0 else 0, 4):
-                queues[r].dma_start(v_planes[a][r:P:32, :].bitcast(I32),
-                                picked_sc[16 * (r // 2) + 8 * a + r % 2:P:32, :].bitcast(I32))
+        load_w2(0)
+        load_table(tab2_w, tab2_words[0])
+        for r in range(4):
+            nc.sync.dma_start(tab2_sc[TAB2_SHIFT + r:P:32, :].bitcast(I32), tab2_scales[0, r:16:4, :].bitcast(I32))
+        load_per_channel(bias_sb, bias)
+        load_w2(1)
+        load_per_channel(gain_sb, gain)
+        for b in range(2):
+            nc.sync.dma_start(w3_raw[b][:],
+                              w3_words.rearrange("a p c i -> p a (c i)").bitcast(I32)[:, :, b * N:(b + 1) * N])
+        for d in range(4):
+            nc.sync.dma_start(w3_sc_raw[32 * d + W3_SHIFT:32 * d + W3_SHIFT + 8, :].bitcast(I32),
+                              w3_scales[:, 4 * d:4 * d + 4, :].bitcast(I32))
 
         def order_words(engine, target, source, per_line):
             engine.tensor_copy(target.rearrange("p g (t m i) -> p g m t i", t=4, i=per_line),
@@ -121,299 +125,212 @@ def tile_list_fleet_ageing_kernel(tc, tab_words, tab_scales, offs, tab2_words, t
             nc.vector.tensor_copy(target.rearrange("p g (t m) -> p g t m", t=4),
                                   source.rearrange("p g (m t) -> p g t m", t=4))
 
-        w1_codes, w1_planes, w3_codes, w3_planes = {}, {}, {}, {}
-
-        def order_w1_planes():
-            ordered = held([P, 4, N], U8, "w1_planes")
-            order_plane(ordered[:], w1_sc_raw[:].rearrange("p (g c) -> p g c", g=4))
-            for b in range(2):
-                w1_planes[b] = ordered[:].rearrange("p (a b) c -> p b a c", a=2)[:, b, :, :]
-
-        def order_w1_words():
-            ordered = held([P, 4, 2 * N], U8, "w1_codes")
-            order_words(nc.vector, ordered[:].bitcast(U16),
-                        w1_raw[:].bitcast(U16).rearrange("p a (b c) -> p (a b) c", b=2), 8)
-            for b in range(2):
-                w1_codes[b] = ordered[:].rearrange("p (a b) c -> p b a c", a=2)[:, b, :, :]
-
-        def order_w3_block(engine, b, name):
-            ordered = taken([P, 2, N], U32, name)
-            order_words(engine, ordered[:], w3_raw[:, :, b * N:(b + 1) * N].bitcast(U32), 4)
-            for a in range(2):
-                w3_codes[b, a] = ordered[:, a:a + 1, :]
-
-        def order_w3_words(engine, b, a, name):
-            w3_codes[b, a] = taken([P, 1, N], U32, name)
-            order_words(engine, w3_codes[b, a][:], w3_raw[:, a:a + 1, b * N:(b + 1) * N].bitcast(U32), 4)
-
-        def order_w3_planes(name):
-            w3_planes[0] = taken([P, 2, N], U8, name)
-            order_plane(w3_planes[0][:], w3_sc_raw[:].rearrange("p (g c) -> p g c", g=2))
-
-        w2_grouped, w2_codes, w2_plane = {}, {}, {}
-
-        def cast_w2(on, b, name):
-            w2_grouped[b] = taken([P, 4 * N], BF16, name)
-            target = w2_grouped[b][:].rearrange("p (t m j) -> p m t j", t=4, j=4)
-            source = w2_raw[b][:].rearrange("p j (m t) -> p m t j", t=4)
-            if on == "P":
-                nc.gpsimd.tensor_scalar(target, source, 1.0, 0.0, MULT, ADD)
-            elif on == "C":
-                nc.gpsimd.tensor_copy(target, source)
-            elif on == "S":
-                nc.scalar.copy(target, source)
-            else:
-                nc.vector.tensor_copy(target, source)
-
-        def quantise_w2(b):
-            w2_codes[b] = held([P, N], U32, "w2_codes%d" % b)
-            w2_plane[b] = held([P, N], U8, "w2_plane%d" % b)
-            nc.vector.quantize_mx(w2_codes[b][:].bitcast(FP8X4), w2_plane[b][:], w2_grouped[b][:])
-
         def gather(window, offsets, first, width, dtype, name):
-            picked = taken([P, width], dtype, name)
+            picked = shared([P, width], dtype, name)
             nc.vector.tensor_copy(picked[:], window.indirect(offsets[:, first // 16:(first + width) // 16]))
             return picked
 
-        v_codes, v2_codes, v2_plane = {}, {}, {}
+        v_codes, v2_codes, v2_plane, w2_codes, w2_plane, w3_codes = {}, {}, {}, {}, {}, {}
+        load_sb, summed, stress, scaled, woven, h_codes, h_plane = {}, {}, {}, {}, {}, {}, {}
+        w1_planes = held([P, 4, N], U8, "w1_planes")
+        w1_codes = held([P, 4, 2 * N], U8, "w1_codes")
 
-        def gather_load(a, first, width, name):
-            picked = gather(tab_w[a][:].bitcast(U32), list8, first, width, U32, name)
-            for c in range(0, width, N):
-                v_codes[(first + c) // N, a] = picked[:, c:c + N]
+        def gather_load(half, a, name):
+            v_codes[half, a] = gather(tab_w[a][:].bitcast(U32), list8, half * N, N, U32, name)
 
-        def columns(tiles, first, width):
-            start = max(key for key in tiles if key <= first)
-            return tiles[start], slice(first - start, first - start + width)
+        def gather_weather_codes(half, name):
+            v2_codes[half] = gather(tab2_w[:].bitcast(U32), list1, half * N, N, U32, name)
 
-        def gather_weather_plane(first, width, name):
-            v2_plane[first] = gather(tab2_sc[:], list1, first, width, U8, name)
+        def gather_weather_plane(half, name):
+            v2_plane[half] = gather(tab2_sc[:], list1, half * N, N, U8, name)
 
-        def gather_weather(first, width, name):
-            v2_codes[first] = gather(tab2_w[:].bitcast(U32), list1, first, width, U32, name)
+        def columns(q, width):
+            return slice(q % 2 * Q, q % 2 * Q + width)
 
-        def load_passes(target, first, width, b, t, start, stop):
-            h, step = first // N, (N if width == N else P)
+        def weave_w2(b):
+            grouped = shared([P, 4 * N], BF16, "w2_grouped%d" % b)
+            return (grouped, grouped[:].rearrange("p (t m j) -> p m t j", t=4, j=4),
+                    w2_raw[b][:].rearrange("p j (m t) -> p m t j", t=4))
+
+        def quantise_w2(b, grouped):
+            w2_codes[b] = held([P, N], U32, "w2_codes%d" % b)
+            w2_plane[b] = held([P, N], U8, "w2_plane%d" % b)
+            nc.vector.quantize_mx(w2_codes[b][:].bitcast(FP8X4), w2_plane[b][:], grouped[:])
+
+        def order_w3(b, name):
+            w3_codes[b] = shared([P, 2, N], U32, name)
+            order_words(nc.gpsimd, w3_codes[b][:], w3_raw[b][:].bitcast(U32), 4)
+
+        def load_passes(target, first, width, b, t, stop):
+            step = N if width == N else P
             pieces = [(a, c) for c in range(0, width, step) for a in range(2)]
             for a, c in pieces:
                 nc.tensor.matmul_mx(
                     target[:, c:c + step],
-                    lhsT=w1_codes[b][:, a, 2 * t * P:2 * (t + 1) * P].bitcast(FP4X4),
-                    lhsT_scale=w1_planes[b][:, a, t * P:(t + 1) * P],
-                    rhs=v_codes[h, a][:, first % N + c:first % N + c + step].bitcast(FP8X4),
+                    lhsT=w1_codes[:, 2 * a + b, 2 * t * P:2 * (t + 1) * P].bitcast(FP4X4),
+                    lhsT_scale=w1_planes[:, 2 * a + b, t * P:(t + 1) * P],
+                    rhs=v_codes[first // N, a][:, first % N + c:first % N + c + step].bitcast(FP8X4),
                     rhs_scale=v_planes[a][:, first + c:first + c + step],
-                    start=(start and (a, c) == pieces[0]), stop=(stop and (a, c) == pieces[-1]))
+                    start=(a, c) == pieces[0], stop=(stop and (a, c) == pieces[-1]))
 
-        load_sb = [{}, {}]
+        def keep_load(half, b):
+            load_sb[half, b] = held([P, 4, N], F32, "load%d%d" % (half, b))
+            for t in range(4):
+                sums = bank("first")
+                load_passes(sums[:], half * N, N, b, t, True)
+                nc.scalar.copy(load_sb[half, b][:, t, :], sums[:])
 
-        def side_by_side(tile, width, count):
-            return tile[:, 0:count * width].rearrange("p (i j) -> p i j", j=width)
-
-        def keep_load(first, width, b, ring):
-            kept = held([P, 4, width], F32, "load%d_%d" % (first, b))
-            load_sb[b][first] = kept
-            per_bank = N // width
-            for t0 in range(0, 4, per_bank):
-                sums = bank(ring)
-                for i in range(per_bank):
-                    load_passes(sums[:, i * width:(i + 1) * width], first, width, b, t0 + i, True, True)
-                nc.scalar.copy(kept[:, t0:t0 + per_bank, :], side_by_side(sums, width, per_bank))
-
-        def twice(first, b):
-            return first >= TWICE_FROM[b]
-
-        summed, stress, scaled, woven, grouped = {}, {}, {}, {}, {}
-        h_codes, h_plane = [{}, {}], [{}, {}]
-
-        def sum_unit(first, width, b, ring, names):
+        def sum_unit(q, b, width, ring):
             per_bank = N // width
             for k, t0 in enumerate(range(0, 4, per_bank)):
                 sums = bank(ring)
                 for i in range(per_bank):
                     t = t0 + i
-                    if twice(first, b):
-                        load_passes(sums[:, i * width:(i + 1) * width], first, width, b, t, True, False)
-                    codes, cols = columns(v2_codes, first, width)
-                    plane, plane_cols = columns(v2_plane, first, width)
+                    if (q, b) in TWICE:
+                        load_passes(sums[:, i * width:(i + 1) * width], q * Q, width, b, t, False)
                     nc.tensor.matmul_mx(
                         sums[:, i * width:(i + 1) * width],
-                        lhsT=w2_codes[b][:, t * P:(t + 1) * P].bitcast(FP8X4), lhsT_scale=w2_plane[b][:, t * P:(t + 1) * P],
-                        rhs=codes[:, cols].bitcast(FP8X4), rhs_scale=plane[TAB2_SHIFT:P, plane_cols],
-                        start=not twice(first, b), stop=True)
+                        lhsT=w2_codes[b][:, t * P:(t + 1) * P].bitcast(FP8X4),
+                        lhsT_scale=w2_plane[b][:, t * P:(t + 1) * P],
+                        rhs=v2_codes[q // 2][:, columns(q, width)].bitcast(FP8X4),
+                        rhs_scale=v2_plane[q // 2][TAB2_SHIFT:P, columns(q, width)],
+                        start=(q, b) not in TWICE, stop=True)
                 total = sums
-                if not twice(first, b):
-                    kept, cols = columns(load_sb[b], first, width)
-                    total = taken([P, N], F32, names[k])
-                    nc.vector.tensor_tensor(side_by_side(total, width, per_bank), side_by_side(sums, width, per_bank),
-                                            kept[:, t0:t0 + per_bank, cols], ADD)
+                if (q, b) not in TWICE:
+                    total = shared([P, N], F32, "sum%d%d%d" % (q, b, k))
+                    nc.vector.tensor_tensor(side_by_side(total, per_bank, width), side_by_side(sums, per_bank, width),
+                                            load_sb[q // 2, b][:, t0:t0 + per_bank, columns(q, width)], ADD)
                 for i in range(per_bank):
-                    summed[first, b, t0 + i] = total[:, i * width:(i + 1) * width]
+                    summed[q, b, t0 + i] = total[:, i * width:(i + 1) * width]
 
-        def sigmoid(first, width, b, gain_on):
-            stress[first, b] = work.tile([P, 4, width], F32, name="stress%d" % width, bufs=STRESS_BUFS[width])
-            group = [g for g in GROUPS if (first, b) in g][0]
-            if gain_on != "F" and group not in grouped:
-                grouped[group] = held([P, len(group), 4, width], BF16, "scaled%d%d" % (first // P, b))
-            if gain_on != "F":
-                scaled[first, b] = grouped[group][:, group.index((first, b)), :, :]
+        def sigmoid(q, b, width):
+            stress[q, b] = work.tile([P, 4, width], F32, name="stress%d" % width,
+                                     bufs=(SIGMOID_BUFS if width == Q else 1))
+            if (q, b) not in FUSED:
+                scaled[q, b] = held([P, 4, width], BF16, "scaled%d%d" % (q, b))
             for t0 in (0, 2):
                 for t in (t0, t0 + 1):
-                    nc.scalar.activation(stress[first, b][:, t, :], summed[first, b, t], SIGMOID, bias=bias_sb[:, b, t:t + 1])
-                for t in (t0, t0 + 1):
-                    column = gain_sb[:, b, t:t + 1]
-                    if gain_on == "S":
-                        nc.scalar.activation(scaled[first, b][:, t, :], stress[first, b][:, t, :], COPY, scale=column)
-                    if gain_on == "P":
-                        nc.gpsimd.tensor_scalar(scaled[first, b][:, t, :], stress[first, b][:, t, :], column, 0.0, MULT, ADD)
-                    if gain_on == "V":
-                        nc.vector.tensor_scalar(scaled[first, b][:, t, :], stress[first, b][:, t, :], column, None, MULT)
+                    nc.scalar.activation(stress[q, b][:, t, :], summed[q, b, t], SIGMOID, bias=bias_sb[:, b, t:t + 1])
+                if (q, b) not in FUSED:
+                    for t in (t0, t0 + 1):
+                        nc.scalar.activation(scaled[q, b][:, t, :], stress[q, b][:, t, :], COPY,
+                                             scale=gain_sb[:, b, t:t + 1])
 
-        def weave(first, width, b, on, name):
-            group = [g for g in GROUPS if (first, b) in g][0]
-            woven[group] = taken([P, len(group), 4 * width], BF16, name)
-            if on == "F":
-                gains = gain_sb[:, b, :].unsqueeze(1).unsqueeze(3).to_broadcast([P, width // 2, 4, 2])
-                nc.vector.tensor_tensor(woven[group][:, 0, :].rearrange("p (c i t) -> p c t i", i=2, t=4),
-                                        stress[first, b][:].rearrange("p t (c i) -> p c t i", i=2), gains, MULT)
-            elif on == "P":
-                nc.gpsimd.tensor_scalar(woven[group][:].rearrange("p g (c t) -> p g c t", t=4),
-                                        grouped[group][:].rearrange("p g t c -> p g c t"), 1.0, 0.0, MULT, ADD)
-            else:
-                copy = nc.vector.tensor_copy if on == "V" else nc.scalar.copy
-                copy(woven[group][:].rearrange("p g (c i t) -> p g c t i", i=4, t=4),
-                     grouped[group][:].rearrange("p g t (c i) -> p g c t i", i=4))
+        def weave(copy, q, b, width, name):
+            woven[q, b] = shared([P, 4 * width], BF16, name)
+            copy(woven[q, b][:].rearrange("p (c i t) -> p c t i", i=4, t=4),
+                 scaled[q, b][:].rearrange("p t (c i) -> p c t i", i=4))
 
-        def quantise_h(first, width, b):
-            group = [g for g in GROUPS if (first, b) in g][0]
-            codes = held([P, len(group) * width], U32, "h_codes%d%d" % (first // P, b))
-            plane = held([P, len(group) * width], U8, "h_plane%d%d" % (first // P, b))
-            for i, (start, block) in enumerate(group):
-                h_codes[block][start] = codes[:, i * width:(i + 1) * width]
-                h_plane[block][start] = plane[:, i * width:(i + 1) * width]
-            nc.vector.quantize_mx(codes[:].bitcast(FP8X4), plane[:], woven[group][:].rearrange("p g c -> p (g c)"))
+        def weave_with_gain(q, b, name):
+            woven[q, b] = shared([P, 4 * Q], BF16, name)
+            gains = gain_sb[:, b, :].unsqueeze(1).unsqueeze(3).to_broadcast([P, Q // 2, 4, 2])
+            nc.vector.tensor_tensor(woven[q, b][:].rearrange("p (c i t) -> p c t i", i=2, t=4),
+                                    stress[q, b][:].rearrange("p t (c i) -> p c t i", i=2), gains, MULT)
+
+        def weave_on_gpsimd(q, b, name):
+            woven[q, b] = shared([P, 4 * Q], BF16, name)
+            nc.gpsimd.tensor_scalar(woven[q, b][:].rearrange("p (c t) -> p c t", t=4),
+                                    scaled[q, b][:].rearrange("p t c -> p c t"), 1.0, 0.0, MULT, ADD)
+
+        def quantise_h(q, b, width):
+            codes = held([P, width], U32, "h_codes%d%d" % (q, b))
+            plane = held([P, width], U8, "h_plane%d%d" % (q, b))
+            nc.vector.quantize_mx(codes[:].bitcast(FP8X4), plane[:], woven[q, b][:])
+            for i in range(width // Q):
+                h_codes[q + i, b] = codes[:, i * Q:(i + 1) * Q]
+                h_plane[q + i, b] = plane[:, i * Q:(i + 1) * Q]
 
         out_rows = out.rearrange("(b p t) j -> b p t j", b=2, t=4)
 
-        def mix_pass(target, first, width, b, t, a):
-            codes, cols = columns(h_codes[a], first, width)
-            plane, cols = columns(h_plane[a], first, width)
-            nc.tensor.matmul_mx(
-                target,
-                lhsT=w3_codes[b, a][:, 0, t * P:(t + 1) * P].bitcast(FP8X4),
-                lhsT_scale=w3_planes[0][W3_SHIFT + 4 * a:P, b, t * P:(t + 1) * P],
-                rhs=codes[:, cols].bitcast(FP8X4), rhs_scale=plane[:, cols],
-                start=(a == 0 and not twice(first, b)), stop=(a == 1))
-
-        def mix_unit(first, width, b, ring, out_on, per_bank, per_store):
+        def mix_unit(q, b, ring, per_bank, copies):
             for t0 in range(0, 4, per_bank):
                 sums = bank(ring)
                 for i in range(per_bank):
-                    target = sums[:, i * width:(i + 1) * width]
-                    if twice(first, b):
-                        load_passes(target, first, width, b, t0 + i, True, False)
+                    t = t0 + i
+                    if (q, b) in TWICE:
+                        load_passes(sums[:, i * Q:(i + 1) * Q], q * Q, Q, b, t, False)
                     for a in range(2):
-                        mix_pass(target, first, width, b, t0 + i, a)
-                if t0 % per_store == 0:
-                    result = work.tile([P, N], F32, name="result", bufs=RESULT_BUFS)
-                    stored = side_by_side(result, width, per_store)
-                target = stored[:, t0 % per_store:t0 % per_store + per_bank, :]
-                if not twice(first, b):
-                    kept, cols = columns(load_sb[b], first, width)
-                    nc.vector.tensor_tensor(target, side_by_side(sums, width, per_bank), kept[:, t0:t0 + per_bank, cols], ADD)
-                elif out_on == "S":
-                    nc.scalar.copy(target, side_by_side(sums, width, per_bank))
+                        nc.tensor.matmul_mx(
+                            sums[:, i * Q:(i + 1) * Q],
+                            lhsT=w3_codes[b][:, a, t * P:(t + 1) * P].bitcast(FP8X4),
+                            lhsT_scale=w3_planes[W3_SHIFT + 4 * a:P, b, t * P:(t + 1) * P],
+                            rhs=h_codes[q, a].bitcast(FP8X4), rhs_scale=h_plane[q, a],
+                            start=(a == 0 and (q, b) not in TWICE), stop=(a == 1))
+                if t0 % 2 == 0:
+                    result = side_by_side(work.tile([P, N], F32, name="result", bufs=RESULT_BUFS), 2, Q)
+                target = result[:, t0 % 2:t0 % 2 + per_bank, :]
+                if (q, b) in TWICE:
+                    copies[t0 % len(copies)](target, side_by_side(sums, per_bank, Q))
                 else:
-                    nc.vector.tensor_copy(target, side_by_side(sums, width, per_bank))
-                if (t0 + per_bank) % per_store == 0:
-                    t1 = t0 + per_bank - per_store
-                    nc.sync.dma_start(out_rows[b, :, t1:t1 + per_store, first:first + width], stored)
+                    nc.vector.tensor_tensor(target, side_by_side(sums, per_bank, Q),
+                                            load_sb[q // 2, b][:, t0:t0 + per_bank, columns(q, Q)], ADD)
+                if (t0 + per_bank) % 2 == 0:
+                    t1 = t0 + per_bank - 2
+                    nc.sync.dma_start(out_rows[b, :, t1:t1 + 2, q * Q:(q + 1) * Q], result)
 
-        nc.sync.dma_start(list8[:], offs)
-        zero(nc.vector, tab_sc)
-        zero(nc.vector, w1_sc_raw)
-        zero(nc.vector, tab2_sc)
-        zero(nc.vector, v_planes[1])
-        nc.vector.memset(warm[:], 0.0)
-        zero(nc.vector, w3_sc_raw)
-        nc.sync.dma_start(list1[:], offs2)
-        load_tab_scales(nc.sync)
-        load_w1_scales(nc.scalar)
-        load_table(nc.sync, tab_w[0], tab_words[0])
+        order_plane(w1_planes[:], w1_sc_raw[:].rearrange("p (g c) -> p g c", g=4))
+        gather_load(0, 0, "v_codes00")
+        order_words(nc.vector, w1_codes[:].bitcast(U16),
+                    w1_raw[:].bitcast(U16).rearrange("p a (b c) -> p (a b) c", b=2), 8)
+        gather_load(0, 1, "v_codes01")
+        keep_load(0, 0)
 
-        load_w1(nc.sync)
-        load_table(nc.sync, tab_w[1], tab_words[1])
-        nc.scalar.activation(warmed[:], warm[:], SIGMOID)
-        gather_tab_scales()
-        move_scale_rows([nc.scalar] * 4, 0)
-        move_scale_rows([nc.scalar, nc.scalar, nc.scalar, nc.sync], 1)
-        load_w2(nc.sync, 0)
-        load_table(nc.sync, tab2_w, tab2_words[0])
-        load_tab2_scales(nc.sync)
-        load_per_channel(nc.sync, bias_sb, bias)
-        load_w2(nc.sync, 1)
-        load_per_channel(nc.sync, gain_sb, gain)
-        load_w3(nc.sync)
-        load_w3_scales(nc.sync)
+        grouped, target, source = weave_w2(0)
+        nc.vector.tensor_copy(target, source)
+        quantise_w2(0, grouped)
+        gather_weather_codes(0, "v2_codes0")
+        gather_weather_plane(0, "v2_plane0")
+        sum_unit(0, 0, N, "second")
+        gather_load(1, 0, "picked_sc")
+        gather_load(1, 1, "v_codes11")
+        sigmoid(0, 0, N)
+        keep_load(0, 1)
 
-        order_w1_planes()
-        gather_load(0, 0, 512, "va0")
-        order_w1_words()
-        gather_load(1, 0, 512, "va1")
-        keep_load(0, 512, 0, "first")
-        cast_w2("V", 0, "stage0")
-        quantise_w2(0)
-        gather_weather(0, 256, "w0")
-        gather_weather(256, 256, "w1")
-        gather_weather_plane(0, 256, "p0")
-        gather_weather_plane(256, 256, "p1")
-        sum_unit(0, 256, 0, "second", ("s000", "s001",))
-        sum_unit(256, 256, 0, "second", ("s100", "s101",))
-        gather_load(0, 512, 512, "picked_sc")
-        gather_load(1, 512, 512, "vb1")
-        sigmoid(0, 256, 0, "S")
-        keep_load(0, 512, 1, "first")
-        sigmoid(256, 256, 0, "S")
-        cast_w2("P", 1, "stage1")
-        quantise_w2(1)
-        sum_unit(0, 256, 1, "second", ("s010", "s011",))
-        sum_unit(256, 256, 1, "second", ("s110", "s111",))
-        sigmoid(0, 256, 1, "S")
-        sigmoid(256, 256, 1, "S")
-        keep_load(512, 512, 1, "first")
-        gather_weather_plane(512, 512, "s000")
-        gather_weather(512, 512, "w2_raw1")
-        order_w3_block(nc.gpsimd, 0, "stage1")
-        weave(0, 256, 0, "V", "s010")
-        quantise_h(0, 256, 0)
-        order_w3_planes("s011")
-        weave(256, 256, 0, "V", "s110")
-        quantise_h(256, 256, 0)
-        weave(0, 256, 1, "V", "y01")
-        quantise_h(0, 256, 1)
-        order_w3_block(nc.gpsimd, 1, "y01")
-        sum_unit(512, 256, 0, "second", ("s200", "s201",))
-        sigmoid(512, 256, 0, "S")
-        sum_unit(512, 256, 1, "second", ("s210", "s211",))
-        sigmoid(512, 256, 1, "S")
-        mix_unit(0, 256, 0, "first", "S", 2, 2)
-        weave(256, 256, 1, "V", "y11")
-        quantise_h(256, 256, 1)
-        mix_unit(0, 256, 1, "first", "S", 2, 2)
-        sum_unit(768, 256, 0, "second", ("s300", "s301",))
-        sum_unit(768, 256, 1, "second", ("s310", "s311",))
-        sigmoid(768, 256, 0, "S")
-        mix_unit(256, 256, 0, "first", "S", 2, 2)
-        weave(512, 256, 0, "V", "y20")
-        quantise_h(512, 256, 0)
-        weave(512, 256, 1, "V", "y21")
-        quantise_h(512, 256, 1)
-        mix_unit(256, 256, 1, "first", "S", 2, 2)
-        weave(768, 256, 0, "V", "y30")
-        quantise_h(768, 256, 0)
-        sigmoid(768, 256, 1, "S")
-        mix_unit(512, 256, 0, "first", "S", 2, 2)
-        weave(768, 256, 1, "V", "y31")
-        quantise_h(768, 256, 1)
-        mix_unit(512, 256, 1, "first", "S", 2, 2)
-        mix_unit(768, 256, 0, "second", "S", 1, 2)
-        mix_unit(768, 256, 1, "first", "S", 2, 2)
+        grouped, target, source = weave_w2(1)
+        nc.gpsimd.tensor_scalar(target, source, 1.0, 0.0, MULT, ADD)
+        quantise_w2(1, grouped)
+        sum_unit(0, 1, Q, "second")
+        sum_unit(1, 1, Q, "second")
+        sigmoid(0, 1, Q)
+        sigmoid(1, 1, Q)
+        keep_load(1, 1)
+        gather_weather_plane(1, "v2_plane1")
+        gather_weather_codes(1, "w2_raw1")
+
+        order_w3(0, "w2_grouped1")
+        weave(nc.vector.tensor_copy, 0, 0, N, "sum010")
+        w3_planes = shared([P, 2, N], U8, "sum011")
+        order_plane(w3_planes[:], w3_sc_raw[:].rearrange("p (g c) -> p g c", g=2))
+        quantise_h(0, 0, N)
+        weave(nc.vector.tensor_copy, 0, 1, Q, "woven01")
+        weave_with_gain(1, 1, "woven11")
+        quantise_h(0, 1, Q)
+        quantise_h(1, 1, Q)
+
+        order_w3(1, "woven11")
+        sum_unit(2, 0, Q, "second")
+        sigmoid(2, 0, Q)
+        sum_unit(2, 1, Q, "first")
+        sigmoid(2, 1, Q)
+        mix_unit(0, 0, "first", 2, None)
+        mix_unit(1, 0, "first", 2, None)
+
+        sum_unit(3, 0, Q, "second")
+        sum_unit(3, 1, Q, "second")
+        sigmoid(3, 0, Q)
+        weave_on_gpsimd(2, 0, "w3_raw1")
+        weave_on_gpsimd(2, 1, "woven21")
+        mix_unit(0, 1, "first", 2, None)
+        quantise_h(2, 0, Q)
+        quantise_h(2, 1, Q)
+        mix_unit(1, 1, "first", 2, None)
+
+        sigmoid(3, 1, Q)
+        weave(nc.scalar.copy, 3, 0, Q, "woven30")
+        mix_unit(2, 0, "first", 2, [nc.scalar.copy])
+        weave_with_gain(3, 1, "woven31")
+        quantise_h(3, 0, Q)
+        quantise_h(3, 1, Q)
+        mix_unit(2, 1, "first", 2, None)
+        mix_unit(3, 1, "first", 2, None)
+        mix_unit(3, 0, "second", 1, [nc.scalar.copy, nc.vector.tensor_copy])

@@ -79,31 +79,38 @@ def tile_list_fleet_ageing_kernel(tc, tab_words, tab_scales, offs, tab2_words, t
             nc.sync.dma_start(columns[:], vector.rearrange("(b p t) -> p b t", b=2, t=4))
 
         nc.sync.dma_start(list8[:], offs)
-        for scale_tile in (tab_sc, w1_sc_raw, tab2_sc, v_planes[1]):
+        nc.vector.memset(tab_sc[:, 0:T // 2].bitcast(I32), 0)
+        nc.gpsimd.memset(tab_sc[:, T // 2:T].bitcast(I32), 0)
+        for scale_tile in (w1_sc_raw, tab2_sc, v_planes[1]):
             nc.vector.memset(scale_tile[:].bitcast(I32), 0)
         nc.vector.memset(warm[:], 0.0)
         nc.vector.memset(w3_sc_raw[:].bitcast(I32), 0)
-        nc.sync.dma_start(list1[:], offs2)
         for e in range(2):
             nc.sync.dma_start(tab_sc[e:P:8, :].bitcast(I32),
                               tab_scales[:, e:16:2, :].bitcast(I32).rearrange("a g c -> g a c"))
         for r in range(4):
             nc.scalar.dma_start(w1_sc_raw[r:P:32, :].bitcast(I32).rearrange("d (a c) -> d a c", a=2),
                                 w1_scales[:, r:16:4, :].bitcast(I32).rearrange("a d c -> d a c"))
-        load_table(tab_w[0], tab_words[0])
         nc.sync.dma_start(w1_raw[:], w1_words.bitcast(I32).rearrange("a p c -> p a c"))
-        load_table(tab_w[1], tab_words[1])
+        load_table(tab_w[0], tab_words[0])
+        second_pass = tab_words[1].rearrange("p c i -> p (c i)").bitcast(I32)
+        nc.sync.dma_start(tab_w[1][:, 0:T // 2], second_pass[:, 0:T // 2])
         nc.scalar.activation(warmed[:], warm[:], SIGMOID)
 
         nc.vector.tensor_copy(picked_sc[:], tab_sc[:].indirect(list8[:]))
         nc.vector.tensor_copy(v_planes[0][:].bitcast(U32), picked_sc[:].bitcast(U32))
-        moves = [(0, 2), (0, 3)] + [(1, r) for r in range(4)]
-        for a, r in moves:
-            queue = nc.sync if (a, r) == moves[-1] else nc.scalar
+        def move_rows(queue, a, r):
             queue.dma_start(v_planes[a][r:P:32, :].bitcast(I32),
                             picked_sc[16 * (r // 2) + 8 * a + r % 2:P:32, :].bitcast(I32))
 
+        for r in (2, 3):
+            move_rows(nc.sync, 0, r)
+        nc.sync.dma_start(tab_w[1][:, T // 2:T], second_pass[:, T // 2:T])
+        for r in range(4):
+            move_rows(nc.scalar if r < 3 else nc.sync, 1, r)
+
         load_w2(0)
+        nc.sync.dma_start(list1[:], offs2)
         load_table(tab2_w, tab2_words[0])
         for r in range(4):
             nc.sync.dma_start(tab2_sc[TAB2_SHIFT + r:P:32, :].bitcast(I32), tab2_scales[0, r:16:4, :].bitcast(I32))
@@ -117,9 +124,9 @@ def tile_list_fleet_ageing_kernel(tc, tab_words, tab_scales, offs, tab2_words, t
             nc.sync.dma_start(w3_sc_raw[32 * d + W3_SHIFT:32 * d + W3_SHIFT + 8, :].bitcast(I32),
                               w3_scales[:, 4 * d:4 * d + 4, :].bitcast(I32))
 
-        def order_words(engine, target, source, per_line):
-            engine.tensor_copy(target.rearrange("p g (t m i) -> p g m t i", t=4, i=per_line),
-                               source.rearrange("p g (m i t) -> p g m t i", t=4, i=per_line))
+        def order_words(copy, target, source, per_line):
+            copy(target.rearrange("p g (t m i) -> p g m t i", t=4, i=per_line),
+                 source.rearrange("p g (m i t) -> p g m t i", t=4, i=per_line))
 
         def order_plane(target, source):
             nc.vector.tensor_copy(target.rearrange("p g (t m) -> p g t m", t=4),
@@ -133,7 +140,7 @@ def tile_list_fleet_ageing_kernel(tc, tab_words, tab_scales, offs, tab2_words, t
         v_codes, v2_codes, v2_plane, w2_codes, w2_plane, w3_codes = {}, {}, {}, {}, {}, {}
         load_sb, summed, stress, scaled, woven, h_codes, h_plane = {}, {}, {}, {}, {}, {}, {}
         w1_planes = held([P, 4, N], U8, "w1_planes")
-        w1_codes = held([P, 4, 2 * N], U8, "w1_codes")
+        w1_codes = [held([P, 2, 2 * N], U8, "w1_codes%d" % b) for b in range(2)]
 
         def gather_load(half, a, name):
             v_codes[half, a] = gather(tab_w[a][:].bitcast(U32), list8, half * N, N, U32, name)
@@ -159,15 +166,15 @@ def tile_list_fleet_ageing_kernel(tc, tab_words, tab_scales, offs, tab2_words, t
 
         def order_w3(b, name):
             w3_codes[b] = shared([P, 2, N], U32, name)
-            order_words(nc.gpsimd, w3_codes[b][:], w3_raw[b][:].bitcast(U32), 4)
+            order_words(nc.gpsimd.tensor_copy, w3_codes[b][:], w3_raw[b][:].bitcast(U32), 4)
 
         def load_passes(target, first, width, b, t, stop):
-            step = N if width == N else P
+            step = width
             pieces = [(a, c) for c in range(0, width, step) for a in range(2)]
             for a, c in pieces:
                 nc.tensor.matmul_mx(
                     target[:, c:c + step],
-                    lhsT=w1_codes[:, 2 * a + b, 2 * t * P:2 * (t + 1) * P].bitcast(FP4X4),
+                    lhsT=w1_codes[b][:, a, 2 * t * P:2 * (t + 1) * P].bitcast(FP4X4),
                     lhsT_scale=w1_planes[:, 2 * a + b, t * P:(t + 1) * P],
                     rhs=v_codes[first // N, a][:, first % N + c:first % N + c + step].bitcast(FP8X4),
                     rhs_scale=v_planes[a][:, first + c:first + c + step],
@@ -270,8 +277,8 @@ def tile_list_fleet_ageing_kernel(tc, tab_words, tab_scales, offs, tab2_words, t
 
         order_plane(w1_planes[:], w1_sc_raw[:].rearrange("p (g c) -> p g c", g=4))
         gather_load(0, 0, "v_codes00")
-        order_words(nc.vector, w1_codes[:].bitcast(U16),
-                    w1_raw[:].bitcast(U16).rearrange("p a (b c) -> p (a b) c", b=2), 8)
+        for b in range(2):
+            order_words(nc.scalar.copy, w1_codes[b][:].bitcast(U16), w1_raw[:].bitcast(U16)[:, :, b * N:(b + 1) * N], 8)
         gather_load(0, 1, "v_codes01")
         keep_load(0, 0)
 
@@ -281,7 +288,7 @@ def tile_list_fleet_ageing_kernel(tc, tab_words, tab_scales, offs, tab2_words, t
         gather_weather_codes(0, "v2_codes0")
         gather_weather_plane(0, "v2_plane0")
         sum_unit(0, 0, N, "second")
-        gather_load(1, 0, "picked_sc")
+        gather_load(1, 0, "v_codes10")
         gather_load(1, 1, "v_codes11")
         sigmoid(0, 0, N)
         keep_load(0, 1)

@@ -79,12 +79,11 @@ def tile_list_fleet_ageing_kernel(tc, tab_words, tab_scales, offs, tab2_words, t
             nc.sync.dma_start(columns[:], vector.rearrange("(b p t) -> p b t", b=2, t=4))
 
         nc.sync.dma_start(list8[:], offs)
-        nc.vector.memset(tab_sc[:, 0:T // 2].bitcast(I32), 0)
-        nc.gpsimd.memset(tab_sc[:, T // 2:T].bitcast(I32), 0)
-        for scale_tile in (w1_sc_raw, tab2_sc, v_planes[1]):
+        for scale_tile in (tab_sc, w1_sc_raw, tab2_sc, v_planes[1]):
             nc.vector.memset(scale_tile[:].bitcast(I32), 0)
         nc.vector.memset(warm[:], 0.0)
         nc.vector.memset(w3_sc_raw[:].bitcast(I32), 0)
+        nc.sync.dma_start(list1[:], offs2)
         for e in range(2):
             nc.sync.dma_start(tab_sc[e:P:8, :].bitcast(I32),
                               tab_scales[:, e:16:2, :].bitcast(I32).rearrange("a g c -> g a c"))
@@ -110,7 +109,6 @@ def tile_list_fleet_ageing_kernel(tc, tab_words, tab_scales, offs, tab2_words, t
             move_rows(nc.scalar if r < 3 else nc.sync, 1, r)
 
         load_w2(0)
-        nc.sync.dma_start(list1[:], offs2)
         load_table(tab2_w, tab2_words[0])
         for r in range(4):
             nc.sync.dma_start(tab2_sc[TAB2_SHIFT + r:P:32, :].bitcast(I32), tab2_scales[0, r:16:4, :].bitcast(I32))

from contextlib import ExitStack

import concourse.mybir as mybir

K, K2, H, T, S = 1024, 512, 1024, 2048, 1024
FLOPS = 2 * S * H * (K + K2 + H)

F32 = mybir.dt.float32
BF16 = mybir.dt.bfloat16
I32 = mybir.dt.int32
U32 = mybir.dt.uint32
U16 = mybir.dt.uint16
U8 = mybir.dt.uint8
FP8X4 = mybir.dt.float8_e4m3fn_x4
FP4X4 = mybir.dt.float4_e2m1fn_x4
MULT = mybir.AluOpType.mult
ADD = mybir.AluOpType.add
SIGMOID = mybir.ActivationFunctionType.Sigmoid
COPY = mybir.ActivationFunctionType.Copy

P = 128
N = 512
Q = 256
TAB2_SHIFT = 4
W3_SHIFT = 8
RING = 4
TWICE = ((2, 0), (3, 0))
FUSED = ((1, 1), (3, 1))
SIGMOID_BUFS = 5
RESULT_BUFS = 8


def tile_list_fleet_ageing_kernel(tc, tab_words, tab_scales, offs, tab2_words, tab2_scales, offs2,
                                              w1_words, w1_scales, w2, bias, gain, w3_words, w3_scales, out):
    nc = tc.nc
    with ExitStack() as ctx:
        lists = ctx.enter_context(tc.tile_pool(name="lists", bufs=1))
        keep = ctx.enter_context(tc.tile_pool(name="keep", bufs=1))
        work = ctx.enter_context(tc.tile_pool(name="work", bufs=1))
        psum = ctx.enter_context(tc.psum_pool(name="psum", bufs=1))

        def held(shape, dtype, name):
            return keep.tile(shape, dtype, name=name, align_bytes=64)

        def shared(shape, dtype, name):
            return work.tile(shape, dtype, name=name, align_bytes=64)

        def bank(ring):
            return psum.tile([P, N], F32, name=ring, bufs=RING)

        def side_by_side(tile, count, width):
            return tile[:, 0:count * width].rearrange("p (i j) -> p i j", j=width)

        list8 = lists.tile([P, S // 16], U16, name="list8")
        list1 = lists.tile([P, S // 16], U16, name="list1")
        tab_sc = held([P, T], U8, "tab_sc")
        tab2_sc = held([P, T], U8, "tab2_sc")
        w1_sc_raw = held([P, 2 * H], U8, "w1_sc_raw")
        v_planes = [held([P, S], U8, "v_plane%d" % a) for a in range(2)]
        w3_sc_raw = held([P, H], U8, "w3_sc_raw")
        warm = held([P, 8], F32, "warm")
        warmed = held([P, 8], F32, "warmed")
        picked_sc = shared([P, S], U8, "picked_sc")
        w1_raw = held([P, 2, N], I32, "w1_raw")
        tab_w = [held([P, T], I32, "tab_w%d" % a) for a in range(2)]
        tab2_w = held([P, T], I32, "tab2_w")
        w2_raw = [shared([P, 4, N], F32, "w2_raw%d" % b) for b in range(2)]
        bias_sb = held([P, 2, 4], F32, "bias_sb")
        gain_sb = held([P, 2, 4], F32, "gain_sb")
        w3_raw = [shared([P, 2, N], I32, "w3_raw%d" % b) for b in range(2)]

        def load_table(window, dram_pass):
            nc.sync.dma_start(window[:], dram_pass.rearrange("p c i -> p (c i)").bitcast(I32))

        def load_w2(b):
            nc.sync.dma_start(w2_raw[b][:], w2.rearrange("(p j) c -> p j c", j=4)[:, :, b * N:(b + 1) * N])

        def load_per_channel(columns, vector):
            nc.sync.dma_start(columns[:], vector.rearrange("(b p t) -> p b t", b=2, t=4))

        nc.sync.dma_start(list8[:], offs)
        for scale_tile in (tab_sc, w1_sc_raw, tab2_sc, v_planes[1]):
            nc.vector.memset(scale_tile[:].bitcast(I32), 0)
        nc.vector.memset(warm[:], 0.0)
        nc.vector.memset(w3_sc_raw[:].bitcast(I32), 0)
        nc.sync.dma_start(list1[:], offs2)
        for e in range(2):
            nc.sync.dma_start(tab_sc[e:P:8, :].bitcast(I32),
                              tab_scales[:, e:16:2, :].bitcast(I32).rearrange("a g c -> g a c"))
        for r in range(4):
            nc.scalar.dma_start(w1_sc_raw[r:P:32, :].bitcast(I32).rearrange("d (a c) -> d a c", a=2),
                                w1_scales[:, r:16:4, :].bitcast(I32).rearrange("a d c -> d a c"))
        nc.sync.dma_start(w1_raw[:], w1_words.bitcast(I32).rearrange("a p c -> p a c"))
        load_table(tab_w[0], tab_words[0])
        second_pass = tab_words[1].rearrange("p c i -> p (c i)").bitcast(I32)
        nc.sync.dma_start(tab_w[1][:, 0:T // 2], second_pass[:, 0:T // 2])
        nc.scalar.activation(warmed[:], warm[:], SIGMOID)

        nc.vector.tensor_copy(picked_sc[:], tab_sc[:].indirect(list8[:]))
        nc.vector.tensor_copy(v_planes[0][:].bitcast(U32), picked_sc[:].bitcast(U32))
        def move_rows(queue, a, r):
            queue.dma_start(v_planes[a][r:P:32, :].bitcast(I32),
                            picked_sc[16 * (r // 2) + 8 * a + r % 2:P:32, :].bitcast(I32))

        for r in (2, 3):
            move_rows(nc.sync, 0, r)
        nc.sync.dma_start(tab_w[1][:, T // 2:T], second_pass[:, T // 2:T])
        for r in range(4):
            move_rows(nc.scalar if r < 3 else nc.sync, 1, r)

        load_w2(0)
        load_table(tab2_w, tab2_words[0])
        for r in range(4):
            nc.sync.dma_start(tab2_sc[TAB2_SHIFT + r:P:32, :].bitcast(I32), tab2_scales[0, r:16:4, :].bitcast(I32))
        load_per_channel(bias_sb, bias)
        load_w2(1)
        load_per_channel(gain_sb, gain)
        for b in range(2):
            nc.sync.dma_start(w3_raw[b][:],
                              w3_words.rearrange("a p c i -> p a (c i)").bitcast(I32)[:, :, b * N:(b + 1) * N])
        for d in range(4):
            nc.sync.dma_start(w3_sc_raw[32 * d + W3_SHIFT:32 * d + W3_SHIFT + 8, :].bitcast(I32),
                              w3_scales[:, 4 * d:4 * d + 4, :].bitcast(I32))

        def order_words(copy, target, source, per_line):
            copy(target.rearrange("p g (t m i) -> p g m t i", t=4, i=per_line),
                 source.rearrange("p g (m i t) -> p g m t i", t=4, i=per_line))

        def order_plane(target, source):
            nc.vector.tensor_copy(target.rearrange("p g (t m) -> p g t m", t=4),
                                  source.rearrange("p g (m t) -> p g t m", t=4))

        def gather(window, offsets, first, width, dtype, name):
            picked = shared([P, width], dtype, name)
            nc.vector.tensor_copy(picked[:], window.indirect(offsets[:, first // 16:(first + width) // 16]))
            return picked

        v_codes, v2_codes, v2_plane, w2_codes, w2_plane, w3_codes = {}, {}, {}, {}, {}, {}
        load_sb, summed, stress, scaled, woven, h_codes, h_plane = {}, {}, {}, {}, {}, {}, {}
        w1_planes = held([P, 4, N], U8, "w1_planes")
        w1_codes = [held([P, 2, 2 * N], U8, "w1_codes%d" % b) for b in range(2)]

        def gather_load(half, a, name):
            v_codes[half, a] = gather(tab_w[a][:].bitcast(U32), list8, half * N, N, U32, name)

        def gather_weather_codes(half, name):
            v2_codes[half] = gather(tab2_w[:].bitcast(U32), list1, half * N, N, U32, name)

        def gather_weather_plane(half, name):
            v2_plane[half] = gather(tab2_sc[:], list1, half * N, N, U8, name)

        def columns(q, width):
            return slice(q % 2 * Q, q % 2 * Q + width)

        def weave_w2(b):
            grouped = shared([P, 4 * N], BF16, "w2_grouped%d" % b)
            return (grouped, grouped[:].rearrange("p (t m j) -> p m t j", t=4, j=4),
                    w2_raw[b][:].rearrange("p j (m t) -> p m t j", t=4))

        def quantise_w2(b, grouped):
            w2_codes[b] = held([P, N], U32, "w2_codes%d" % b)
            w2_plane[b] = held([P, N], U8, "w2_plane%d" % b)
            nc.vector.quantize_mx(w2_codes[b][:].bitcast(FP8X4), w2_plane[b][:], grouped[:])

        def order_w3(b, name):
            w3_codes[b] = shared([P, 2, N], U32, name)
            order_words(nc.gpsimd.tensor_copy, w3_codes[b][:], w3_raw[b][:].bitcast(U32), 4)

        def load_passes(target, first, width, b, t, stop):
            step = width
            pieces = [(a, c) for c in range(0, width, step) for a in range(2)]
            for a, c in pieces:
                nc.tensor.matmul_mx(
                    target[:, c:c + step],
                    lhsT=w1_codes[b][:, a, 2 * t * P:2 * (t + 1) * P].bitcast(FP4X4),
                    lhsT_scale=w1_planes[:, 2 * a + b, t * P:(t + 1) * P],
                    rhs=v_codes[first // N, a][:, first % N + c:first % N + c + step].bitcast(FP8X4),
                    rhs_scale=v_planes[a][:, first + c:first + c + step],
                    start=(a, c) == pieces[0], stop=(stop and (a, c) == pieces[-1]))

        def keep_load(half, b):
            load_sb[half, b] = held([P, 4, N], F32, "load%d%d" % (half, b))
            for t in range(4):
                sums = bank("first")
                load_passes(sums[:], half * N, N, b, t, True)
                nc.scalar.copy(load_sb[half, b][:, t, :], sums[:])

        def sum_unit(q, b, width, ring):
            per_bank = N // width
            for k, t0 in enumerate(range(0, 4, per_bank)):
                sums = bank(ring)
                for i in range(per_bank):
                    t = t0 + i
                    if (q, b) in TWICE:
                        load_passes(sums[:, i * width:(i + 1) * width], q * Q, width, b, t, False)
                    nc.tensor.matmul_mx(
                        sums[:, i * width:(i + 1) * width],
                        lhsT=w2_codes[b][:, t * P:(t + 1) * P].bitcast(FP8X4),
                        lhsT_scale=w2_plane[b][:, t * P:(t + 1) * P],
                        rhs=v2_codes[q // 2][:, columns(q, width)].bitcast(FP8X4),
                        rhs_scale=v2_plane[q // 2][TAB2_SHIFT:P, columns(q, width)],
                        start=(q, b) not in TWICE, stop=True)
                total = sums
                if (q, b) not in TWICE:
                    total = shared([P, N], F32, "sum%d%d%d" % (q, b, k))
                    nc.vector.tensor_tensor(side_by_side(total, per_bank, width), side_by_side(sums, per_bank, width),
                                            load_sb[q // 2, b][:, t0:t0 + per_bank, columns(q, width)], ADD)
                for i in range(per_bank):
                    summed[q, b, t0 + i] = total[:, i * width:(i + 1) * width]

        def sigmoid(q, b, width):
            stress[q, b] = work.tile([P, 4, width], F32, name="stress%d" % width,
                                     bufs=(SIGMOID_BUFS if width == Q else 1))
            if (q, b) not in FUSED:
                scaled[q, b] = held([P, 4, width], BF16, "scaled%d%d" % (q, b))
            for t0 in (0, 2):
                for t in (t0, t0 + 1):
                    nc.scalar.activation(stress[q, b][:, t, :], summed[q, b, t], SIGMOID, bias=bias_sb[:, b, t:t + 1])
                if (q, b) not in FUSED:
                    for t in (t0, t0 + 1):
                        nc.scalar.activation(scaled[q, b][:, t, :], stress[q, b][:, t, :], COPY,
                                             scale=gain_sb[:, b, t:t + 1])

        def weave(copy, q, b, width, name):
            woven[q, b] = shared([P, 4 * width], BF16, name)
            copy(woven[q, b][:].rearrange("p (c i t) -> p c t i", i=4, t=4),
                 scaled[q, b][:].rearrange("p t (c i) -> p c t i", i=4))

        def weave_with_gain(q, b, name):
            woven[q, b] = shared([P, 4 * Q], BF16, name)
            gains = gain_sb[:, b, :].unsqueeze(1).unsqueeze(3).to_broadcast([P, Q // 2, 4, 2])
            nc.vector.tensor_tensor(woven[q, b][:].rearrange("p (c i t) -> p c t i", i=2, t=4),
                                    stress[q, b][:].rearrange("p t (c i) -> p c t i", i=2), gains, MULT)

        def weave_on_gpsimd(q, b, name):
            woven[q, b] = shared([P, 4 * Q], BF16, name)
            nc.gpsimd.tensor_scalar(woven[q, b][:].rearrange("p (c t) -> p c t", t=4),
                                    scaled[q, b][:].rearrange("p t c -> p c t"), 1.0, 0.0, MULT, ADD)

        def quantise_h(q, b, width):
            codes = held([P, width], U32, "h_codes%d%d" % (q, b))
            plane = held([P, width], U8, "h_plane%d%d" % (q, b))
            nc.vector.quantize_mx(codes[:].bitcast(FP8X4), plane[:], woven[q, b][:])
            for i in range(width // Q):
                h_codes[q + i, b] = codes[:, i * Q:(i + 1) * Q]
                h_plane[q + i, b] = plane[:, i * Q:(i + 1) * Q]

        out_rows = out.rearrange("(b p t) j -> b p t j", b=2, t=4)

        def mix_unit(q, b, ring, per_bank, copies):
            for t0 in range(0, 4, per_bank):
                sums = bank(ring)
                for i in range(per_bank):
                    t = t0 + i
                    if (q, b) in TWICE:
                        load_passes(sums[:, i * Q:(i + 1) * Q], q * Q, Q, b, t, False)
                    for a in range(2):
                        nc.tensor.matmul_mx(
                            sums[:, i * Q:(i + 1) * Q],
                            lhsT=w3_codes[b][:, a, t * P:(t + 1) * P].bitcast(FP8X4),
                            lhsT_scale=w3_planes[W3_SHIFT + 4 * a:P, b, t * P:(t + 1) * P],
                            rhs=h_codes[q, a].bitcast(FP8X4), rhs_scale=h_plane[q, a],
                            start=(a == 0 and (q, b) not in TWICE), stop=(a == 1))
                if t0 % 2 == 0:
                    result = side_by_side(work.tile([P, N], F32, name="result", bufs=RESULT_BUFS), 2, Q)
                target = result[:, t0 % 2:t0 % 2 + per_bank, :]
                if (q, b) in TWICE:
                    copies[t0 % len(copies)](target, side_by_side(sums, per_bank, Q))
                else:
                    nc.vector.tensor_tensor(target, side_by_side(sums, per_bank, Q),
                                            load_sb[q // 2, b][:, t0:t0 + per_bank, columns(q, Q)], ADD)
                if (t0 + per_bank) % 2 == 0:
                    t1 = t0 + per_bank - 2
                    nc.sync.dma_start(out_rows[b, :, t1:t1 + 2, q * Q:(q + 1) * Q], result)

        order_plane(w1_planes[:], w1_sc_raw[:].rearrange("p (g c) -> p g c", g=4))
        gather_load(0, 0, "v_codes00")
        for b in range(2):
            order_words(nc.scalar.copy, w1_codes[b][:].bitcast(U16), w1_raw[:].bitcast(U16)[:, :, b * N:(b + 1) * N], 8)
        gather_load(0, 1, "v_codes01")
        keep_load(0, 0)

        grouped, target, source = weave_w2(0)
        nc.vector.tensor_copy(target, source)
        quantise_w2(0, grouped)
        gather_weather_codes(0, "v2_codes0")
        gather_weather_plane(0, "v2_plane0")
        sum_unit(0, 0, N, "second")
        gather_load(1, 0, "v_codes10")
        gather_load(1, 1, "v_codes11")
        sigmoid(0, 0, N)
        keep_load(0, 1)

        grouped, target, source = weave_w2(1)
        nc.gpsimd.tensor_scalar(target, source, 1.0, 0.0, MULT, ADD)
        quantise_w2(1, grouped)
        sum_unit(0, 1, Q, "second")
        sum_unit(1, 1, Q, "second")
        sigmoid(0, 1, Q)
        sigmoid(1, 1, Q)
        keep_load(1, 1)
        gather_weather_plane(1, "v2_plane1")
        gather_weather_codes(1, "w2_raw1")

        order_w3(0, "w2_grouped1")
        weave(nc.vector.tensor_copy, 0, 0, N, "sum010")
        w3_planes = shared([P, 2, N], U8, "sum011")
        order_plane(w3_planes[:], w3_sc_raw[:].rearrange("p (g c) -> p g c", g=2))
        quantise_h(0, 0, N)
        weave(nc.vector.tensor_copy, 0, 1, Q, "woven01")
        weave_with_gain(1, 1, "woven11")
        quantise_h(0, 1, Q)
        quantise_h(1, 1, Q)

        order_w3(1, "woven11")
        sum_unit(2, 0, Q, "second")
        sigmoid(2, 0, Q)
        sum_unit(2, 1, Q, "first")
        sigmoid(2, 1, Q)
        mix_unit(0, 0, "first", 2, None)
        mix_unit(1, 0, "first", 2, None)

        sum_unit(3, 0, Q, "second")
        sum_unit(3, 1, Q, "second")
        sigmoid(3, 0, Q)
        weave_on_gpsimd(2, 0, "w3_raw1")
        weave_on_gpsimd(2, 1, "woven21")
        mix_unit(0, 1, "first", 2, None)
        quantise_h(2, 0, Q)
        quantise_h(2, 1, Q)
        mix_unit(1, 1, "first", 2, None)

        sigmoid(3, 1, Q)
        weave(nc.scalar.copy, 3, 0, Q, "woven30")
        mix_unit(2, 0, "first", 2, [nc.scalar.copy])
        weave_with_gain(3, 1, "woven31")
        quantise_h(3, 0, Q)
        quantise_h(3, 1, Q)
        mix_unit(2, 1, "first", 2, None)
        mix_unit(3, 1, "first", 2, None)
        mix_unit(3, 0, "second", 1, [nc.scalar.copy, nc.vector.tensor_copy])
